import numpy as np
import ml_dtypes


def mxq(x, axis, fmt="e4m3"):
    dtype, down = {"e4m3": (ml_dtypes.float8_e4m3fn, 7), "e5m2": (ml_dtypes.float8_e5m2, 14)}[fmt]
    v = np.moveaxis(np.asarray(x, np.float32).astype(ml_dtypes.bfloat16).astype(np.float64), axis, -1)
    blocks = v.reshape(v.shape[:-1] + (-1, 32))
    amax = np.abs(blocks).max(-1, keepdims=True)
    byte = np.maximum(np.where(amax > 0, np.frexp(amax)[1] - 1 + 127, 0) - down, 1)
    scale = np.exp2(byte - 127.0)
    codes = (blocks / scale).astype(np.float32).astype(dtype).astype(np.float64)
    return np.moveaxis((codes * scale).reshape(v.shape), -1, axis)


WIDE = False


def mx_kscale(k):
    if not WIDE:
        return np.ones(k)
    levels = np.array([10, -10, 5, -5, 0])
    if k % 512:
        return np.exp2(np.random.permutation(np.resize(levels, k // 32))).repeat(32)
    a = np.empty((k // 512, 16))
    for p in range(k // 512):
        a[p, :8] = np.random.permutation(np.resize(levels, 8))
        for g in range(8):
            far = levels[np.abs(levels - a[p, g]) >= 10]
            a[p, g + 8] = far[np.random.randint(len(far))]
    return np.exp2(a.ravel()).repeat(32)


def f64(x):
    return np.asarray(x).astype(np.float64)


def striped(idx):
    return np.tile(idx.reshape(-1, 16).T, (8, 1)).astype(np.uint16)


def unstriped(offs):
    return offs[:16].T.reshape(-1).astype(np.int64)


E2M1 = np.array([0.0, 0.5, 1.0, 1.5, 2.0, 3.0, 4.0, 6.0, -0.0, -0.5, -1.0, -1.5, -2.0, -3.0, -4.0, -6.0])


def pack_weight(w, fmt):
    k, n = w.shape
    w = f64(np.asarray(w, np.float32).astype(ml_dtypes.bfloat16)).reshape(k // 32, 32, n)
    amax = np.abs(w).max(1)
    if fmt == "e4m3":
        byte = np.frexp(amax)[1] - 1 + 127 - 7
    else:
        mant, ex = np.frexp(amax / 6.0)
        byte = np.where(mant > 0.5, ex, ex - 1) + 127
    byte = np.clip(np.where(amax > 0, byte, 1), 1, 254)
    scaled = (w * np.exp2(127.0 - byte)[:, None, :]).reshape(k, n).astype(np.float32)
    by_word = np.ascontiguousarray(scaled.reshape(k // 512, 128, 4, n).transpose(0, 1, 3, 2))
    if fmt == "e4m3":
        words = by_word.astype(ml_dtypes.float8_e4m3fn).view(np.uint8)
    else:
        c = by_word.astype(ml_dtypes.float4_e2m1fn).view(np.uint8) & 0xF
        words = (c[..., 0::2] | (c[..., 1::2] << 4)).reshape(k // 512, 128, 2 * n)
    return np.ascontiguousarray(words), np.ascontiguousarray(byte.astype(np.uint8).reshape(k // 512, 16, n))


def unpack_weight(words, scales, fmt):
    g, _, n = scales.shape
    words = np.ascontiguousarray(words).reshape(g, 128, n, -1)
    if fmt == "e4m3":
        vals = words.view(ml_dtypes.float8_e4m3fn).astype(np.float64)
    else:
        nib = np.empty((g, 128, n, 4), np.uint8)
        nib[..., 0::2] = words & 0xF
        nib[..., 1::2] = words >> 4
        vals = E2M1[nib]
    vals = vals * np.repeat(np.exp2(scales.astype(np.float64) - 127.0), 8, axis=1)[..., None]
    return vals.transpose(0, 1, 3, 2).reshape(g * 512, n)


def gelu(v):
    return 0.5 * v * (1.0 + np.tanh(np.sqrt(2.0 / np.pi) * (v + 0.044715 * v**3)))


K, H, T, S, P = 1536, 1024, 2048, 1024, 512

def setup_inputs():
    n = np.random.standard_normal
    s = mx_kscale(K)[:, None]
    u = mx_kscale(H)[:, None]
    tab_words, tab_scales = pack_weight(n((K, T)) * s, "e4m3")
    w1_words, w1_scales = pack_weight(0.5 * n((K, H)) / np.sqrt(K) / s, "e2m1")
    w2 = n((H, H)) / np.sqrt(H) / u
    return {
        "tab_words": tab_words, "tab_scales": tab_scales,
        "offs": striped(np.random.permutation(T)[:S]),
        "w1_words": w1_words, "w1_scales": w1_scales,
        "pos1": striped(np.random.permutation(S)[:P]),
        "pos2": striped(np.random.permutation(S)[:P]),
        "gain": (np.random.uniform(0.5, 1.5, H) * u[:, 0]).astype(np.float32),
        "w2": w2.astype(np.float32),
        "nw": (-np.random.uniform(0.2, 0.6, H)).astype(np.float32),
    }

def reference(tab_words, tab_scales, offs, w1_words, w1_scales, pos1, pos2, gain, w2, nw):
    v = unpack_weight(tab_words, tab_scales, "e4m3")[:, unstriped(offs)]
    w1 = unpack_weight(w1_words, w1_scales, "e2m1")
    h = w1.T @ v
    x = f64(gain)[:, None] * np.cos(h[:, unstriped(pos1)])
    y = mxq(f64(w2), 0, "e4m3").T @ mxq(x, 0, "e4m3")
    d = y - h[:, unstriped(pos2)]
    return np.exp(f64(nw)[:, None] * np.square(d))

@@ -1,0 +1,268 @@
+import math
+from contextlib import ExitStack
+
+import concourse.mybir as mybir
+
+K, H, T, S, M = 1536, 1024, 2048, 1024, 512
+FLOPS = 2 * K * H * S + 2 * H * H * M
+
+F32 = mybir.dt.float32
+BF16 = mybir.dt.bfloat16
+I32 = mybir.dt.int32
+U32 = mybir.dt.uint32
+U16 = mybir.dt.uint16
+U8 = mybir.dt.uint8
+FP8X4 = mybir.dt.float8_e4m3fn_x4
+FP4X4 = mybir.dt.float4_e2m1fn_x4
+ALU = mybir.AluOpType
+ACT = mybir.ActivationFunctionType
+
+P = 128
+PACK = 4
+K_PASS = P * PACK
+PASSES1 = K // K_PASS
+PASSES2 = H // K_PASS
+N = 512
+HALVES = S // N
+LIST_ROWS = 16
+QUAD = 32
+FIRST_ROW = QUAD - PACK * PASSES1
+MOVED_ROWS = P - QUAD + PACK
+TWO_PI = 2.0 * math.pi
+X_PARTS = 2
+X_COLS = M // X_PARTS
+W2_PARTS = 2
+W2_COLS = P // W2_PARTS
+TILES = PASSES2 * PACK
+
+
+def tile_list_escapement_wear_match_kernel(
+    tc, tab_words, tab_scales, offs, w1_words, w1_scales, pos1, pos2, gain, w2, nw, out
+):
+    nc = tc.nc
+    with ExitStack() as ctx:
+        lists = ctx.enter_context(tc.tile_pool(name="lists", bufs=1))
+        keep = ctx.enter_context(tc.tile_pool(name="keep", bufs=1))
+        ring = ctx.enter_context(tc.tile_pool(name="ring", bufs=2))
+        psum = ctx.enter_context(tc.psum_pool(name="psum", bufs=1))
+
+        offs_sb = lists.tile([P, S // LIST_ROWS], U16, name="offs_sb")
+        pos1_sb = lists.tile([P, M // LIST_ROWS], U16, name="pos1_sb")
+        pos2_sb = lists.tile([P, M // LIST_ROWS], U16, name="pos2_sb")
+
+        tab_scale_window = keep.tile([P, T], U8, name="tab_scale_window", tag="slot_b", align_bytes=64)
+        w1_scale_raw = keep.tile([P, PASSES1, H], U8, name="w1_scale_raw", tag="slot_c", align_bytes=64)
+        v_planes = [keep.tile([P, S], U8, name="v_plane%d" % a, align_bytes=64) for a in range(PASSES1)]
+        nc.gpsimd.memset(w1_scale_raw[:].bitcast(I32), 0)
+        for q in range(4):
+            nc.vector.memset(tab_scale_window[QUAD * q : QUAD * q + FIRST_ROW, :].bitcast(I32), 0)
+        for a in range(PASSES1):
+            nc.gpsimd.memset(v_planes[a][P - QUAD : P, :].bitcast(I32), 0)
+
+        nc.sync.dma_start(offs_sb[:], offs)
+        for q in range(4):
+            queue = nc.sync if q < 2 else nc.scalar
+            queue.dma_start(
+                out=tab_scale_window[QUAD * q + FIRST_ROW : QUAD * (q + 1), :].bitcast(I32),
+                in_=tab_scales[:, 4 * q : 4 * q + 4, :].bitcast(I32),
+            )
+        w1_raw = keep.tile([P, PASSES1, H // 2], I32, name="w1_raw", tag="slot_d", align_bytes=64)
+        nc.sync.dma_start(out=w1_raw[:], in_=w1_words.bitcast(I32).rearrange("a p w -> p a w"))
+        for r in range(4):
+            nc.scalar.dma_start(
+                out=w1_scale_raw[r:P:QUAD].bitcast(I32),
+                in_=w1_scales.bitcast(I32).rearrange("a (q r) w -> r q a w", r=4)[r],
+            )
+        tab_windows = {}
+
+        def load_table(a):
+            window = keep.tile([P, T], I32, name="tab_window%d" % a, tag="slot_" + "abd"[a], align_bytes=64)
+            nc.sync.dma_start(out=window[:], in_=tab_words[a].rearrange("p t i -> p (t i)").bitcast(I32))
+            tab_windows[a] = window
+
+        load_table(0)
+        nc.sync.dma_start(pos1_sb[:], pos1)
+        nc.sync.dma_start(pos2_sb[:], pos2)
+        gain_sb = keep.tile([P, PASSES2, PACK], F32, name="gain_sb")
+        nw_sb = keep.tile([P, PASSES2, PACK], F32, name="nw_sb")
+        nc.gpsimd.dma_start(out=gain_sb[:], in_=gain.rearrange("(b p t) -> p b t", p=P, t=PACK))
+        nc.gpsimd.dma_start(out=nw_sb[:], in_=nw.rearrange("(b p t) -> p b t", p=P, t=PACK))
+
+        v_packed = keep.tile([P, S], U8, name="v_packed", align_bytes=64)
+        nc.vector.tensor_copy(out=v_packed[:], in_=tab_scale_window[:].indirect(offs_sb[:]))
+        load_table(1)
+        for a in range(PASSES1):
+            first = FIRST_ROW + PACK * a
+            nc.scalar.dma_start(
+                out=v_planes[a][0:MOVED_ROWS, :].bitcast(I32),
+                in_=v_packed[first : first + MOVED_ROWS, :].bitcast(I32),
+            )
+
+        w1_codes = keep.tile([P, PASSES1, 2 * H], U8, name="w1_codes", align_bytes=64)
+        nc.vector.tensor_copy(
+            out=w1_codes[:].bitcast(U16).rearrange("p a (b t c) -> p (a b) t c", t=PACK, c=P),
+            in_=w1_raw[:].bitcast(U16).rearrange("p a (b c t) -> p (a b) t c", t=PACK, c=P),
+        )
+        load_table(2)
+        w1_planes = {}
+
+        def order_w1_scales(b, tag):
+            w1_planes[b] = keep.tile([P, PASSES1, K_PASS], U8, name="w1_planes%d" % b, tag=tag, align_bytes=64)
+            nc.vector.tensor_copy(
+                out=w1_planes[b][:].rearrange("p a (t c) -> p t a c", t=PACK),
+                in_=w1_scale_raw[:, :, K_PASS * b : K_PASS * (b + 1)].rearrange("p a (c t) -> p t a c", t=PACK),
+            )
+
+        order_w1_scales(0, "slot_e")
+        v_codes = {}
+        for a in range(PASSES1):
+            for j in range(HALVES):
+                v_codes[a, j] = keep.tile([P, N], U32, name="v_codes%d%d" % (a, j), align_bytes=64)
+                cols = slice(j * N // LIST_ROWS, (j + 1) * N // LIST_ROWS)
+                nc.vector.tensor_copy(
+                    out=v_codes[a, j][:], in_=tab_windows[a][:].bitcast(U32).indirect(offs_sb[:, cols])
+                )
+        order_w1_scales(1, "slot_d")
+
+        w2_raw = {}
+
+        def load_w2(b, c, tag):
+            w2_raw[b, c] = keep.tile([P, PACK, K_PASS], F32, name="w2_raw%d%d" % (b, c), tag=tag, align_bytes=64)
+            rows = w2[K_PASS * b : K_PASS * (b + 1), K_PASS * c : K_PASS * (c + 1)]
+            nc.sync.dma_start(out=w2_raw[b, c][:], in_=rows.rearrange("(p t) n -> p t n", t=PACK))
+
+        load_w2(0, 0, "slot_a")
+        load_w2(0, 1, "slot_b")
+        load_w2(1, 0, "slot_c")
+
+        gain2 = keep.tile([P, PASSES2, PACK], F32, name="gain2")
+        nc.scalar.mul(gain2[:], gain_sb[:], -2.0)
+        h_tiles = {}
+        x_codes = {}
+        x_planes = {}
+        w2_codes = {}
+        w2_planes = {}
+
+        def quantise_w2(b, c):
+            woven = ring.tile([P, PACK, P, PACK], BF16, name="w2_woven", align_bytes=64)
+            for part in range(W2_PARTS):
+                cols = slice(part * W2_COLS, (part + 1) * W2_COLS)
+                nc.scalar.copy(
+                    out=woven[:, :, cols, :].rearrange("p u c t -> p c t u"),
+                    in_=w2_raw[b, c][:].rearrange("p t (c u) -> p c t u", u=PACK)[:, cols],
+                )
+            w2_codes[b, c] = keep.tile([P, K_PASS], U32, name="w2_codes%d%d" % (b, c), align_bytes=64)
+            w2_planes[b, c] = keep.tile([P, K_PASS], U8, name="w2_plane%d%d" % (b, c), align_bytes=64)
+            nc.vector.quantize_mx(
+                out=w2_codes[b, c][:].bitcast(FP8X4),
+                scales=w2_planes[b, c][:],
+                in_=woven[:].rearrange("p u c t -> p (u c t)"),
+            )
+
+        def first_product(bank, b, t, j, a):
+            col = K_PASS * b + P * t
+            nc.tensor.matmul_mx(
+                out=bank[:],
+                lhsT=w1_codes[:, a, 2 * col : 2 * (col + P)].bitcast(FP4X4),
+                lhsT_scale=w1_planes[b][:, a, P * t : P * (t + 1)],
+                rhs=v_codes[a, j][:].bitcast(FP8X4),
+                rhs_scale=v_planes[a][:, j * N : (j + 1) * N],
+                start=(a == 0),
+                stop=(a == PASSES1 - 1),
+            )
+
+        picked = [keep.tile([P, 2 * M], F32, name="picked%d" % s) for s in range(2)]
+        reduced = [keep.tile([P, 2 * M], F32, name="reduced%d" % s) for s in range(2)]
+        banks = {}
+        for a in range(PASSES1):
+            for j in range(HALVES):
+                for t in range(PACK):
+                    if a == 0:
+                        banks[t, j] = psum.tile([P, N], F32, name="bank%d" % (2 * t + j))
+                    first_product(banks[t, j], 0, t, j, a)
+        for b in range(PASSES2):
+            sines = ring.tile([P, PACK, M], F32, name="sines")
+            for t in range(PACK):
+                h_tiles[b, t] = keep.tile([P, S], F32, name="h%d%d" % (b, t))
+                for j in range(HALVES):
+                    if b > 0:
+                        banks[t, j] = psum.tile([P, N], F32, name="bank%d" % (2 * t + j))
+                        for a in range(PASSES1):
+                            first_product(banks[t, j], b, t, j, a)
+                    nc.scalar.copy(out=h_tiles[b, t][:, j * N : (j + 1) * N], in_=banks[t, j][:])
+                healthy = picked[t // 2]
+                nc.vector.tensor_copy(
+                    out=healthy[:, M * (t % 2) : M * (t % 2 + 1)], in_=h_tiles[b, t][:].indirect(pos1_sb[:])
+                )
+                if t % 2 == 1:
+                    turns = ring.tile([P, 2 * M], I32, name="turns")
+                    nc.vector.tensor_scalar(turns[:], healthy[:], 1.0 / TWO_PI, None, ALU.mult)
+                    nc.vector.scalar_tensor_tensor(
+                        reduced[t // 2][:], turns[:], -TWO_PI, healthy[:], ALU.mult, ALU.add
+                    )
+                    nc.scalar.activation(
+                        sines[:, t - 1 : t + 1, :].rearrange("p t m -> p (t m)"), reduced[t // 2][:], ACT.Sin, scale=0.5
+                    )
+            x_codes[b] = keep.tile([P, M], U32, name="x_codes%d" % b, align_bytes=64)
+            x_planes[b] = keep.tile([P, M], U8, name="x_plane%d" % b, align_bytes=64)
+            for j in range(X_PARTS):
+                cols = slice(j * X_COLS, (j + 1) * X_COLS)
+                squares = ring.tile([P, X_COLS, PACK], F32, name="squares")
+                nc.scalar.activation(
+                    squares[:].rearrange("p (c i) t -> p c t i", i=PACK),
+                    sines[:, :, cols].rearrange("p t (c i) -> p c t i", i=PACK),
+                    ACT.Square,
+                )
+                x_woven = ring.tile([P, X_COLS, PACK], BF16, name="x_woven", align_bytes=64)
+                nc.vector.scalar_tensor_tensor(
+                    x_woven[:],
+                    squares[:],
+                    -0.5,
+                    gain2[:, b, :].unsqueeze(1).to_broadcast([P, X_COLS, PACK]),
+                    ALU.add,
+                    ALU.mult,
+                )
+                nc.vector.quantize_mx(
+                    out=x_codes[b][:, cols].bitcast(FP8X4),
+                    scales=x_planes[b][:, cols],
+                    in_=x_woven[:].rearrange("p m t -> p (m t)"),
+                )
+            for c in range(PASSES2):
+                quantise_w2(b, c)
+                if (b, c) == (0, 0):
+                    load_w2(1, 1, "slot_a")
+
+        y_banks = {}
+        for b in range(PASSES2):
+            for c in range(PASSES2):
+                for u in range(PACK):
+                    if b == 0:
+                        y_banks[c, u] = psum.tile([P, M], F32, name="bank%d" % (PACK * c + u))
+                    nc.tensor.matmul_mx(
+                        out=y_banks[c, u][:],
+                        lhsT=w2_codes[b, c][:, P * u : P * (u + 1)].bitcast(FP8X4),
+                        lhsT_scale=w2_planes[b, c][:, P * u : P * (u + 1)],
+                        rhs=x_codes[b][:].bitcast(FP8X4),
+                        rhs_scale=x_planes[b][:],
+                        start=(b == 0),
+                        stop=(b == PASSES2 - 1),
+                    )
+        out_rows = out.rearrange("(c p u) m -> c u p m", p=P, u=PACK)
+        spots = [picked[1][:, 0:M], picked[1][:, M : 2 * M], reduced[1][:, 0:M], reduced[1][:, M : 2 * M]]
+
+        def pick_suspects(i):
+            nc.vector.tensor_copy(out=spots[i % len(spots)], in_=h_tiles[divmod(i, PACK)][:].indirect(pos2_sb[:]))
+
+        for i in range(len(spots)):
+            pick_suspects(i)
+        for i in range(TILES):
+            c, u = divmod(i, PACK)
+            diff = ring.tile([P, M], F32, name="diff", bufs=3)
+            nc.vector.tensor_tensor(diff[:], y_banks[c, u][:], spots[i % len(spots)], ALU.subtract)
+            square = ring.tile([P, M], F32, name="square", bufs=3)
+            nc.scalar.activation(square[:], diff[:], ACT.Square)
+            score = ring.tile([P, M], F32, name="score", bufs=4)
+            nc.scalar.activation(score[:], square[:], ACT.Exp, scale=nw_sb[:, c, u : u + 1])
+            nc.sync.dma_start(out=out_rows[c, u], in_=score[:])
+            if i + len(spots) < TILES:
+                pick_suspects(i + len(spots))

@@ -26,7 +26,8 @@ N = 512
 HALVES = S // N
 LIST_ROWS = 16
 QUAD = 32
-FIRST_ROW = QUAD - PACK * PASSES1
+PAIR_ROW = QUAD - 2 * PACK
+LAST_ROW = PAIR_ROW - 4 * PACK
 MOVED_ROWS = P - QUAD + PACK
 TWO_PI = 2.0 * math.pi
 X_PARTS = 2
@@ -34,6 +35,7 @@ X_COLS = M // X_PARTS
 W2_PARTS = 2
 W2_COLS = P // W2_PARTS
 TILES = PASSES2 * PACK
+OPEN_TILES = 2
 
 
 def tile_list_escapement_wear_match_kernel(
@@ -50,29 +52,31 @@ def tile_list_escapement_wear_match_kernel(
         pos1_sb = lists.tile([P, M // LIST_ROWS], U16, name="pos1_sb")
         pos2_sb = lists.tile([P, M // LIST_ROWS], U16, name="pos2_sb")
 
-        tab_scale_window = keep.tile([P, T], U8, name="tab_scale_window", tag="slot_b", align_bytes=64)
+        tab_scale_window = keep.tile([P, T], U8, name="tab_scale_window", align_bytes=64)
         w1_scale_raw = keep.tile([P, PASSES1, H], U8, name="w1_scale_raw", tag="slot_c", align_bytes=64)
         v_planes = [keep.tile([P, S], U8, name="v_plane%d" % a, align_bytes=64) for a in range(PASSES1)]
-        nc.gpsimd.memset(w1_scale_raw[:].bitcast(I32), 0)
+        nc.gpsimd.memset(w1_scale_raw[:, 0:2, :].bitcast(I32), 0)
+        nc.vector.memset(w1_scale_raw[:, 2, :].bitcast(I32), 0)
         for q in range(4):
-            nc.vector.memset(tab_scale_window[QUAD * q : QUAD * q + FIRST_ROW, :].bitcast(I32), 0)
-        for a in range(PASSES1):
+            free_rows = LAST_ROW if q == 0 else PAIR_ROW
+            nc.vector.memset(tab_scale_window[QUAD * q : QUAD * q + free_rows, :].bitcast(I32), 0)
+        for a in range(2):
             nc.gpsimd.memset(v_planes[a][P - QUAD : P, :].bitcast(I32), 0)
+        nc.gpsimd.memset(v_planes[2][:].bitcast(I32), 0)
+
+        warm = keep.tile([P, 2], F32, name="warm")
+        nc.gpsimd.memset(warm[:, 0:1], 0.0)
+        nc.scalar.activation(warm[:, 1:2], warm[:, 0:1], ACT.Sin)
 
         nc.sync.dma_start(offs_sb[:], offs)
         for q in range(4):
-            queue = nc.sync if q < 2 else nc.scalar
-            queue.dma_start(
-                out=tab_scale_window[QUAD * q + FIRST_ROW : QUAD * (q + 1), :].bitcast(I32),
-                in_=tab_scales[:, 4 * q : 4 * q + 4, :].bitcast(I32),
+            nc.sync.dma_start(
+                out=tab_scale_window[QUAD * q + PAIR_ROW : QUAD * (q + 1), :].bitcast(I32),
+                in_=tab_scales[0:2, 4 * q : 4 * q + 4, :].bitcast(I32),
             )
+        nc.sync.dma_start(out=tab_scale_window[LAST_ROW:PAIR_ROW, :].bitcast(I32), in_=tab_scales[2].bitcast(I32))
         w1_raw = keep.tile([P, PASSES1, H // 2], I32, name="w1_raw", tag="slot_d", align_bytes=64)
         nc.sync.dma_start(out=w1_raw[:], in_=w1_words.bitcast(I32).rearrange("a p w -> p a w"))
-        for r in range(4):
-            nc.scalar.dma_start(
-                out=w1_scale_raw[r:P:QUAD].bitcast(I32),
-                in_=w1_scales.bitcast(I32).rearrange("a (q r) w -> r q a w", r=4)[r],
-            )
         tab_windows = {}
 
         def load_table(a):
@@ -81,21 +85,36 @@ def tile_list_escapement_wear_match_kernel(
             tab_windows[a] = window
 
         load_table(0)
+        load_table(1)
         nc.sync.dma_start(pos1_sb[:], pos1)
         nc.sync.dma_start(pos2_sb[:], pos2)
+        for r in range(4):
+            nc.scalar.dma_start(
+                out=w1_scale_raw[r:P:QUAD].bitcast(I32),
+                in_=w1_scales.bitcast(I32).rearrange("a (q r) w -> r q a w", r=4)[r],
+            )
         gain_sb = keep.tile([P, PASSES2, PACK], F32, name="gain_sb")
-        nw_sb = keep.tile([P, PASSES2, PACK], F32, name="nw_sb")
         nc.gpsimd.dma_start(out=gain_sb[:], in_=gain.rearrange("(b p t) -> p b t", p=P, t=PACK))
-        nc.gpsimd.dma_start(out=nw_sb[:], in_=nw.rearrange("(b p t) -> p b t", p=P, t=PACK))
+        w2_raw = {}
 
-        v_packed = keep.tile([P, S], U8, name="v_packed", align_bytes=64)
+        def load_w2(b, c, tag):
+            w2_raw[b, c] = keep.tile([P, PACK, K_PASS], F32, name="w2_raw%d%d" % (b, c), tag=tag, align_bytes=64)
+            rows = w2[K_PASS * b : K_PASS * (b + 1), K_PASS * c : K_PASS * (c + 1)]
+            nc.sync.dma_start(out=w2_raw[b, c][:], in_=rows.rearrange("(p t) n -> p t n", t=PACK))
+
+
+        v_packed = keep.tile([P, S], U8, name="v_packed", tag="slot_g", align_bytes=64)
         nc.vector.tensor_copy(out=v_packed[:], in_=tab_scale_window[:].indirect(offs_sb[:]))
-        load_table(1)
-        for a in range(PASSES1):
-            first = FIRST_ROW + PACK * a
+        for a in range(2):
+            first = PAIR_ROW + PACK * a
             nc.scalar.dma_start(
                 out=v_planes[a][0:MOVED_ROWS, :].bitcast(I32),
                 in_=v_packed[first : first + MOVED_ROWS, :].bitcast(I32),
+            )
+        for q in range(4):
+            nc.scalar.dma_start(
+                out=v_planes[2][QUAD * q : QUAD * q + 4, :].bitcast(I32),
+                in_=v_packed[LAST_ROW + 4 * q : LAST_ROW + 4 * q + 4, :].bitcast(I32),
             )
 
         w1_codes = keep.tile([P, PASSES1, 2 * H], U8, name="w1_codes", align_bytes=64)
@@ -113,25 +132,19 @@ def tile_list_escapement_wear_match_kernel(
                 in_=w1_scale_raw[:, :, K_PASS * b : K_PASS * (b + 1)].rearrange("p a (c t) -> p t a c", t=PACK),
             )
 
-        order_w1_scales(0, "slot_e")
         v_codes = {}
         for a in range(PASSES1):
             for j in range(HALVES):
-                v_codes[a, j] = keep.tile([P, N], U32, name="v_codes%d%d" % (a, j), align_bytes=64)
+                v_codes[a, j] = keep.tile([P, N], U32, name="v_codes%d%d" % (a, j), tag="v_codes%d%d" % (a, j), align_bytes=64)
                 cols = slice(j * N // LIST_ROWS, (j + 1) * N // LIST_ROWS)
                 nc.vector.tensor_copy(
                     out=v_codes[a, j][:], in_=tab_windows[a][:].bitcast(U32).indirect(offs_sb[:, cols])
                 )
+            if a == 0:
+                order_w1_scales(0, "slot_a")
         order_w1_scales(1, "slot_d")
 
-        w2_raw = {}
-
-        def load_w2(b, c, tag):
-            w2_raw[b, c] = keep.tile([P, PACK, K_PASS], F32, name="w2_raw%d%d" % (b, c), tag=tag, align_bytes=64)
-            rows = w2[K_PASS * b : K_PASS * (b + 1), K_PASS * c : K_PASS * (c + 1)]
-            nc.sync.dma_start(out=w2_raw[b, c][:], in_=rows.rearrange("(p t) n -> p t n", t=PACK))
-
-        load_w2(0, 0, "slot_a")
+        load_w2(0, 0, "slot_g")
         load_w2(0, 1, "slot_b")
         load_w2(1, 0, "slot_c")
 
@@ -143,21 +156,26 @@ def tile_list_escapement_wear_match_kernel(
         w2_codes = {}
         w2_planes = {}
 
-        def quantise_w2(b, c):
-            woven = ring.tile([P, PACK, P, PACK], BF16, name="w2_woven", align_bytes=64)
-            for part in range(W2_PARTS):
-                cols = slice(part * W2_COLS, (part + 1) * W2_COLS)
-                nc.scalar.copy(
-                    out=woven[:, :, cols, :].rearrange("p u c t -> p c t u"),
-                    in_=w2_raw[b, c][:].rearrange("p t (c u) -> p c t u", u=PACK)[:, cols],
-                )
-            w2_codes[b, c] = keep.tile([P, K_PASS], U32, name="w2_codes%d%d" % (b, c), align_bytes=64)
-            w2_planes[b, c] = keep.tile([P, K_PASS], U8, name="w2_plane%d%d" % (b, c), align_bytes=64)
-            nc.vector.quantize_mx(
-                out=w2_codes[b, c][:].bitcast(FP8X4),
-                scales=w2_planes[b, c][:],
-                in_=woven[:].rearrange("p u c t -> p (u c t)"),
+        w2_woven = {}
+
+        def weave_w2(step):
+            chunk, part = divmod(step, W2_PARTS)
+            b, c = divmod(chunk, PASSES2)
+            if part == 0:
+                w2_woven[b, c] = ring.tile([P, PACK, P, PACK], BF16, name="w2_woven", bufs=4, align_bytes=64)
+            cols = slice(part * W2_COLS, (part + 1) * W2_COLS)
+            nc.scalar.copy(
+                out=w2_woven[b, c][:, :, cols, :].rearrange("p u c t -> p c t u"),
+                in_=w2_raw[b, c][:].rearrange("p t (c u) -> p c t u", u=PACK)[:, cols],
             )
+            if part == W2_PARTS - 1:
+                w2_codes[b, c] = keep.tile([P, K_PASS], U32, name="w2_codes%d%d" % (b, c), align_bytes=64)
+                w2_planes[b, c] = keep.tile([P, K_PASS], U8, name="w2_plane%d%d" % (b, c), align_bytes=64)
+                nc.vector.quantize_mx(
+                    out=w2_codes[b, c][:].bitcast(FP8X4),
+                    scales=w2_planes[b, c][:],
+                    in_=w2_woven[b, c][:].rearrange("p u c t -> p (u c t)"),
+                )
 
         def first_product(bank, b, t, j, a):
             col = K_PASS * b + P * t
@@ -176,20 +194,25 @@ def tile_list_escapement_wear_match_kernel(
         banks = {}
         for a in range(PASSES1):
             for j in range(HALVES):
-                for t in range(PACK):
+                for t in range(OPEN_TILES):
                     if a == 0:
                         banks[t, j] = psum.tile([P, N], F32, name="bank%d" % (2 * t + j))
                     first_product(banks[t, j], 0, t, j, a)
+        for i in range(TILES):
+            b, t = divmod(i, PACK)
+            h_tiles[b, t] = keep.tile([P, S], F32, name="h%d%d" % (b, t))
+            for j in range(HALVES):
+                if i >= OPEN_TILES:
+                    banks[t, j] = psum.tile([P, N], F32, name="bank%d" % (2 * (i % OPEN_TILES) + j))
+                    for a in range(PASSES1):
+                        first_product(banks[t, j], b, t, j, a)
+                nc.scalar.copy(out=h_tiles[b, t][:, j * N : (j + 1) * N], in_=banks[t, j][:])
+        for step in range(W2_PARTS):
+            weave_w2(step)
+        load_w2(1, 1, "slot_g")
         for b in range(PASSES2):
             sines = ring.tile([P, PACK, M], F32, name="sines")
             for t in range(PACK):
-                h_tiles[b, t] = keep.tile([P, S], F32, name="h%d%d" % (b, t))
-                for j in range(HALVES):
-                    if b > 0:
-                        banks[t, j] = psum.tile([P, N], F32, name="bank%d" % (2 * t + j))
-                        for a in range(PASSES1):
-                            first_product(banks[t, j], b, t, j, a)
-                    nc.scalar.copy(out=h_tiles[b, t][:, j * N : (j + 1) * N], in_=banks[t, j][:])
                 healthy = picked[t // 2]
                 nc.vector.tensor_copy(
                     out=healthy[:, M * (t % 2) : M * (t % 2 + 1)], in_=h_tiles[b, t][:].indirect(pos1_sb[:])
@@ -203,11 +226,16 @@ def tile_list_escapement_wear_match_kernel(
                     nc.scalar.activation(
                         sines[:, t - 1 : t + 1, :].rearrange("p t m -> p (t m)"), reduced[t // 2][:], ACT.Sin, scale=0.5
                     )
+                    chunk = (PACK * b + t + 1) // 2
+                    if chunk < PASSES2 * PASSES2:
+                        for part in range(W2_PARTS):
+                            weave_w2(W2_PARTS * chunk + part)
             x_codes[b] = keep.tile([P, M], U32, name="x_codes%d" % b, align_bytes=64)
             x_planes[b] = keep.tile([P, M], U8, name="x_plane%d" % b, align_bytes=64)
             for j in range(X_PARTS):
                 cols = slice(j * X_COLS, (j + 1) * X_COLS)
                 squares = ring.tile([P, X_COLS, PACK], F32, name="squares")
+                last_squares = squares
                 nc.scalar.activation(
                     squares[:].rearrange("p (c i) t -> p c t i", i=PACK),
                     sines[:, :, cols].rearrange("p t (c i) -> p c t i", i=PACK),
@@ -227,11 +255,10 @@ def tile_list_escapement_wear_match_kernel(
                     scales=x_planes[b][:, cols],
                     in_=x_woven[:].rearrange("p m t -> p (m t)"),
                 )
-            for c in range(PASSES2):
-                quantise_w2(b, c)
-                if (b, c) == (0, 0):
-                    load_w2(1, 1, "slot_a")
 
+        nc.scalar.activation(warm[:, 1:2], last_squares[:, 0, 0:1], ACT.Exp)
+        nw_sb = keep.tile([P, PASSES2, PACK], F32, name="nw_sb", tag="v_codes00", align_bytes=64)
+        nc.sync.dma_start(out=nw_sb[:], in_=nw.rearrange("(b p t) -> p b t", p=P, t=PACK))
         y_banks = {}
         for b in range(PASSES2):
             for c in range(PASSES2):
@@ -248,21 +275,29 @@ def tile_list_escapement_wear_match_kernel(
                         stop=(b == PASSES2 - 1),
                     )
         out_rows = out.rearrange("(c p u) m -> c u p m", p=P, u=PACK)
-        spots = [picked[1][:, 0:M], picked[1][:, M : 2 * M], reduced[1][:, 0:M], reduced[1][:, M : 2 * M]]
+        spots = [
+            picked[1][:, 0:M],
+            picked[1][:, M : 2 * M],
+            reduced[1][:, 0:M],
+            last_squares[:].rearrange("p m t -> p (m t)")[:, M : 2 * M],
+        ]
+
+        def spot(i):
+            return spots[i] if i < len(spots) else spots[1 + (i - 1) % 3]
 
         def pick_suspects(i):
-            nc.vector.tensor_copy(out=spots[i % len(spots)], in_=h_tiles[divmod(i, PACK)][:].indirect(pos2_sb[:]))
+            nc.vector.tensor_copy(out=spot(i), in_=h_tiles[divmod(i, PACK)][:].indirect(pos2_sb[:]))
 
         for i in range(len(spots)):
             pick_suspects(i)
         for i in range(TILES):
             c, u = divmod(i, PACK)
-            diff = ring.tile([P, M], F32, name="diff", bufs=3)
-            nc.vector.tensor_tensor(diff[:], y_banks[c, u][:], spots[i % len(spots)], ALU.subtract)
+            diff = ring.tile([P, M], F32, name="diff", bufs=4)
+            nc.vector.tensor_tensor(diff[:], y_banks[c, u][:], spot(i), ALU.subtract)
             square = ring.tile([P, M], F32, name="square", bufs=3)
             nc.scalar.activation(square[:], diff[:], ACT.Square)
             score = ring.tile([P, M], F32, name="score", bufs=4)
             nc.scalar.activation(score[:], square[:], ACT.Exp, scale=nw_sb[:, c, u : u + 1])
             nc.sync.dma_start(out=out_rows[c, u], in_=score[:])
-            if i + len(spots) < TILES:
-                pick_suspects(i + len(spots))
+            if len(spots) <= i + 2 < TILES:
+                pick_suspects(i + 2)

@@ -93,8 +93,6 @@ def tile_list_escapement_wear_match_kernel(
                 out=w1_scale_raw[r:P:QUAD].bitcast(I32),
                 in_=w1_scales.bitcast(I32).rearrange("a (q r) w -> r q a w", r=4)[r],
             )
-        gain_sb = keep.tile([P, PASSES2, PACK], F32, name="gain_sb")
-        nc.gpsimd.dma_start(out=gain_sb[:], in_=gain.rearrange("(b p t) -> p b t", p=P, t=PACK))
         w2_raw = {}
 
         def load_w2(b, c, tag):
@@ -148,8 +146,6 @@ def tile_list_escapement_wear_match_kernel(
         load_w2(0, 1, "slot_b")
         load_w2(1, 0, "slot_c")
 
-        gain2 = keep.tile([P, PASSES2, PACK], F32, name="gain2")
-        nc.scalar.mul(gain2[:], gain_sb[:], -2.0)
         h_tiles = {}
         x_codes = {}
         x_planes = {}
@@ -198,6 +194,9 @@ def tile_list_escapement_wear_match_kernel(
                     if a == 0:
                         banks[t, j] = psum.tile([P, N], F32, name="bank%d" % (2 * t + j))
                     first_product(banks[t, j], 0, t, j, a)
+        for step in range(W2_PARTS):
+            weave_w2(step)
+        load_w2(1, 1, "slot_g")
         for i in range(TILES):
             b, t = divmod(i, PACK)
             h_tiles[b, t] = keep.tile([P, S], F32, name="h%d%d" % (b, t))
@@ -207,9 +206,10 @@ def tile_list_escapement_wear_match_kernel(
                     for a in range(PASSES1):
                         first_product(banks[t, j], b, t, j, a)
                 nc.scalar.copy(out=h_tiles[b, t][:, j * N : (j + 1) * N], in_=banks[t, j][:])
-        for step in range(W2_PARTS):
-            weave_w2(step)
-        load_w2(1, 1, "slot_g")
+        gain_sb = keep.tile([P, PASSES2, PACK], F32, name="gain_sb", tag="v_codes01", align_bytes=64)
+        nc.sync.dma_start(out=gain_sb[:], in_=gain.rearrange("(b p t) -> p b t", p=P, t=PACK))
+        gain2 = keep.tile([P, PASSES2, PACK], F32, name="gain2")
+        nc.scalar.mul(gain2[:], gain_sb[:], -2.0)
         for b in range(PASSES2):
             sines = ring.tile([P, PACK, M], F32, name="sines")
             for t in range(PACK):
@@ -292,12 +292,15 @@ def tile_list_escapement_wear_match_kernel(
             pick_suspects(i)
         for i in range(TILES):
             c, u = divmod(i, PACK)
-            diff = ring.tile([P, M], F32, name="diff", bufs=4)
-            nc.vector.tensor_tensor(diff[:], y_banks[c, u][:], spot(i), ALU.subtract)
-            square = ring.tile([P, M], F32, name="square", bufs=3)
-            nc.scalar.activation(square[:], diff[:], ACT.Square)
-            score = ring.tile([P, M], F32, name="score", bufs=4)
-            nc.scalar.activation(score[:], square[:], ACT.Exp, scale=nw_sb[:, c, u : u + 1])
-            nc.sync.dma_start(out=out_rows[c, u], in_=score[:])
+            width = M // 2 if i == TILES - 1 else M
+            for first in range(0, M, width):
+                cols = slice(first, first + width)
+                diff = ring.tile([P, width], F32, name="diff", bufs=4)
+                nc.vector.tensor_tensor(diff[:], y_banks[c, u][:, cols], spot(i)[:, cols], ALU.subtract)
+                square = ring.tile([P, width], F32, name="square", bufs=3)
+                nc.scalar.activation(square[:], diff[:], ACT.Square)
+                score = ring.tile([P, width], F32, name="score", bufs=4)
+                nc.scalar.activation(score[:], square[:], ACT.Exp, scale=nw_sb[:, c, u : u + 1])
+                nc.sync.dma_start(out=out_rows[c, u][:, cols], in_=score[:])
             if len(spots) <= i + 2 < TILES:
                 pick_suspects(i + 2)

@@ -19,6 +19,7 @@ ACT = mybir.ActivationFunctionType
 
 P = 128
 PACK = 4
+RUN = 8
 K_PASS = P * PACK
 PASSES1 = K // K_PASS
 PASSES2 = H // K_PASS
@@ -26,16 +27,14 @@ N = 512
 HALVES = S // N
 LIST_ROWS = 16
 QUAD = 32
-PAIR_ROW = QUAD - 2 * PACK
-LAST_ROW = PAIR_ROW - 4 * PACK
-MOVED_ROWS = P - QUAD + PACK
+SCALE_ROWS = 16
+FIRST_ROW = P - PASSES1 * SCALE_ROWS
 TWO_PI = 2.0 * math.pi
 X_PARTS = 2
 X_COLS = M // X_PARTS
-W2_PARTS = 2
-W2_COLS = P // W2_PARTS
 TILES = PASSES2 * PACK
 OPEN_TILES = 2
+EARLY_PICKS = 2
 
 
 def tile_list_escapement_wear_match_kernel(
@@ -43,6 +42,7 @@ def tile_list_escapement_wear_match_kernel(
 ):
     nc = tc.nc
     with ExitStack() as ctx:
+        ctx.enter_context(nc.allow_non_contiguous_dma(reason="gain and nw land one value a row tile on each partition"))
         lists = ctx.enter_context(tc.tile_pool(name="lists", bufs=1))
         keep = ctx.enter_context(tc.tile_pool(name="keep", bufs=1))
         ring = ctx.enter_context(tc.tile_pool(name="ring", bufs=2))
@@ -52,82 +52,60 @@ def tile_list_escapement_wear_match_kernel(
         pos1_sb = lists.tile([P, M // LIST_ROWS], U16, name="pos1_sb")
         pos2_sb = lists.tile([P, M // LIST_ROWS], U16, name="pos2_sb")
 
-        tab_scale_window = keep.tile([P, T], U8, name="tab_scale_window", align_bytes=64)
-        w1_scale_raw = keep.tile([P, PASSES1, H], U8, name="w1_scale_raw", tag="slot_c", align_bytes=64)
-        v_planes = [keep.tile([P, S], U8, name="v_plane%d" % a, align_bytes=64) for a in range(PASSES1)]
-        nc.gpsimd.memset(w1_scale_raw[:, 0:2, :].bitcast(I32), 0)
-        nc.vector.memset(w1_scale_raw[:, 2, :].bitcast(I32), 0)
-        for q in range(4):
-            free_rows = LAST_ROW if q == 0 else PAIR_ROW
-            nc.vector.memset(tab_scale_window[QUAD * q : QUAD * q + free_rows, :].bitcast(I32), 0)
-        for a in range(2):
-            nc.gpsimd.memset(v_planes[a][P - QUAD : P, :].bitcast(I32), 0)
-        nc.gpsimd.memset(v_planes[2][:].bitcast(I32), 0)
-
-        warm = keep.tile([P, 2], F32, name="warm")
-        nc.gpsimd.memset(warm[:, 0:1], 0.0)
-        nc.scalar.activation(warm[:, 1:2], warm[:, 0:1], ACT.Sin)
+        tab_scale_window = keep.tile([P, T], U8, name="tab_scale_window", tag="slot_s", align_bytes=64)
+        w1_scale_raw = keep.tile([P, H], U8, name="w1_scale_raw", align_bytes=64)
+        planes = [keep.tile([P, S + H], U8, name="planes%d" % a, align_bytes=64) for a in range(PASSES1)]
+        nc.vector.memset(tab_scale_window[0:FIRST_ROW, :].bitcast(I32), 0)
+        nc.gpsimd.memset(w1_scale_raw[P // 2 : FIRST_ROW, :].bitcast(I32), 0)
+        nc.vector.memset(planes[0][:].bitcast(I32), 0)
+        for a in range(1, PASSES1):
+            nc.gpsimd.memset(planes[a][:].bitcast(I32), 0)
 
         nc.sync.dma_start(offs_sb[:], offs)
-        for q in range(4):
-            nc.sync.dma_start(
-                out=tab_scale_window[QUAD * q + PAIR_ROW : QUAD * (q + 1), :].bitcast(I32),
-                in_=tab_scales[0:2, 4 * q : 4 * q + 4, :].bitcast(I32),
-            )
-        nc.sync.dma_start(out=tab_scale_window[LAST_ROW:PAIR_ROW, :].bitcast(I32), in_=tab_scales[2].bitcast(I32))
-        w1_raw = keep.tile([P, PASSES1, H // 2], I32, name="w1_raw", tag="slot_d", align_bytes=64)
-        nc.sync.dma_start(out=w1_raw[:], in_=w1_words.bitcast(I32).rearrange("a p w -> p a w"))
+        for tile, scales in ((tab_scale_window, tab_scales), (w1_scale_raw, w1_scales)):
+            scale_rows = scales.rearrange("a q t -> (a q) t").bitcast(I32)
+            for rows in (slice(0, 2 * SCALE_ROWS), slice(2 * SCALE_ROWS, 3 * SCALE_ROWS)):
+                nc.sync.dma_start(
+                    out=tile[FIRST_ROW + rows.start : FIRST_ROW + rows.stop, :].bitcast(I32), in_=scale_rows[rows]
+                )
         tab_windows = {}
 
-        def load_table(a):
-            window = keep.tile([P, T], I32, name="tab_window%d" % a, tag="slot_" + "abd"[a], align_bytes=64)
+        def load_table(a, tag):
+            window = keep.tile([P, T], I32, name="tab_window%d" % a, tag=tag, align_bytes=64)
             nc.sync.dma_start(out=window[:], in_=tab_words[a].rearrange("p t i -> p (t i)").bitcast(I32))
             tab_windows[a] = window
 
-        load_table(0)
-        load_table(1)
+        load_table(0, "slot_a")
+        w1_raw = keep.tile([P, PASSES1, H // 2], I32, name="w1_raw", align_bytes=64)
+        nc.sync.dma_start(out=w1_raw[:], in_=w1_words.bitcast(I32).rearrange("a p w -> p a w"))
         nc.sync.dma_start(pos1_sb[:], pos1)
         nc.sync.dma_start(pos2_sb[:], pos2)
-        for r in range(4):
-            nc.scalar.dma_start(
-                out=w1_scale_raw[r:P:QUAD].bitcast(I32),
-                in_=w1_scales.bitcast(I32).rearrange("a (q r) w -> r q a w", r=4)[r],
-            )
-        w2_raw = {}
-
-        def load_w2(b, c, tag):
-            w2_raw[b, c] = keep.tile([P, PACK, K_PASS], F32, name="w2_raw%d%d" % (b, c), tag=tag, align_bytes=64)
-            rows = w2[K_PASS * b : K_PASS * (b + 1), K_PASS * c : K_PASS * (c + 1)]
-            nc.sync.dma_start(out=w2_raw[b, c][:], in_=rows.rearrange("(p t) n -> p t n", t=PACK))
-
+        load_table(1, "slot_b")
 
         v_packed = keep.tile([P, S], U8, name="v_packed", tag="slot_g", align_bytes=64)
         nc.vector.tensor_copy(out=v_packed[:], in_=tab_scale_window[:].indirect(offs_sb[:]))
-        for a in range(2):
-            first = PAIR_ROW + PACK * a
-            nc.scalar.dma_start(
-                out=v_planes[a][0:MOVED_ROWS, :].bitcast(I32),
-                in_=v_packed[first : first + MOVED_ROWS, :].bitcast(I32),
-            )
-        for q in range(4):
-            nc.scalar.dma_start(
-                out=v_planes[2][QUAD * q : QUAD * q + 4, :].bitcast(I32),
-                in_=v_packed[LAST_ROW + 4 * q : LAST_ROW + 4 * q + 4, :].bitcast(I32),
-            )
-
-        w1_codes = keep.tile([P, PASSES1, 2 * H], U8, name="w1_codes", align_bytes=64)
+        scale_rows = keep.tile([P, (S + H) // 4], I32, name="scale_rows", align_bytes=64)
+        upper = slice(P // 2, P)
         nc.vector.tensor_copy(
-            out=w1_codes[:].bitcast(U16).rearrange("p a (b t c) -> p (a b) t c", t=PACK, c=P),
-            in_=w1_raw[:].bitcast(U16).rearrange("p a (b c t) -> p (a b) t c", t=PACK, c=P),
+            out=scale_rows[upper, S // 4 :].rearrange("p (b t j w) -> p b t j w", b=PASSES2, t=PACK, w=RUN // 4),
+            in_=w1_scale_raw[upper].bitcast(I32).rearrange("p (b j t w) -> p b t j w", b=PASSES2, t=PACK, w=RUN // 4),
         )
-        load_table(2)
-        w1_planes = {}
+        nc.vector.tensor_copy(out=scale_rows[upper, 0 : S // 4], in_=v_packed[upper].bitcast(I32))
+        for a in range(PASSES1):
+            for q in range(4):
+                first = FIRST_ROW + SCALE_ROWS * a + 4 * q
+                nc.sync.dma_start(out=planes[a][QUAD * q : QUAD * q + 4, :].bitcast(I32), in_=scale_rows[first : first + 4, :])
+                if (a, q) == (1, 0):
+                    load_table(2, "slot_g")
 
-        def order_w1_scales(b, tag):
-            w1_planes[b] = keep.tile([P, PASSES1, K_PASS], U8, name="w1_planes%d" % b, tag=tag, align_bytes=64)
+        w1_codes = {}
+
+        def order_w1(b):
+            words = slice(b * K_PASS // 2, (b + 1) * K_PASS // 2)
+            w1_codes[b] = keep.tile([P, PASSES1, K_PASS // 2], I32, name="w1_codes%d" % b, align_bytes=64)
             nc.vector.tensor_copy(
-                out=w1_planes[b][:].rearrange("p a (t c) -> p t a c", t=PACK),
-                in_=w1_scale_raw[:, :, K_PASS * b : K_PASS * (b + 1)].rearrange("p a (c t) -> p t a c", t=PACK),
+                out=w1_codes[b][:].rearrange("p a (t j w) -> p t a j w", t=PACK, w=RUN // 2),
+                in_=w1_raw[:, :, words].rearrange("p a (j t w) -> p t a j w", t=PACK, w=RUN // 2),
             )
 
         v_codes = {}
@@ -139,115 +117,100 @@ def tile_list_escapement_wear_match_kernel(
                     out=v_codes[a, j][:], in_=tab_windows[a][:].bitcast(U32).indirect(offs_sb[:, cols])
                 )
             if a == 0:
-                order_w1_scales(0, "slot_a")
-        order_w1_scales(1, "slot_d")
+                order_w1(0)
+        order_w1(1)
 
-        load_w2(0, 0, "slot_g")
-        load_w2(0, 1, "slot_b")
-        load_w2(1, 0, "slot_c")
+        w2_raw = {}
+        w2_rows = w2.rearrange("(b j t i) n -> b t j i n", t=PACK, i=RUN, b=PASSES2)
+        for b in range(PASSES2):
+            w2_raw[b] = keep.tile([P, PACK, H], F32, name="w2_raw%d" % b, tag="slot_" + "ab"[b], align_bytes=64)
+            for t in range(PACK):
+                nc.sync.dma_start(out=w2_raw[b][:, t, :], in_=w2_rows[b, t])
 
-        h_tiles = {}
-        x_codes = {}
-        x_planes = {}
-        w2_codes = {}
-        w2_planes = {}
+        def load_by_row(vec, name, tag):
+            tile = keep.tile([P, PASSES2, PACK, RUN], F32, name=name, tag=tag, align_bytes=64)
+            rows = vec.rearrange("(b j t i o) -> b t j i o", t=PACK, i=RUN, b=PASSES2, o=1)
+            for b in range(PASSES2):
+                for t in range(PACK):
+                    nc.sync.dma_start(out=tile[:, b, t, 0:1], in_=rows[b, t])
+            return tile
 
-        w2_woven = {}
-
-        def weave_w2(step):
-            chunk, part = divmod(step, W2_PARTS)
-            b, c = divmod(chunk, PASSES2)
-            if part == 0:
-                w2_woven[b, c] = ring.tile([P, PACK, P, PACK], BF16, name="w2_woven", bufs=4, align_bytes=64)
-            cols = slice(part * W2_COLS, (part + 1) * W2_COLS)
-            nc.scalar.copy(
-                out=w2_woven[b, c][:, :, cols, :].rearrange("p u c t -> p c t u"),
-                in_=w2_raw[b, c][:].rearrange("p t (c u) -> p c t u", u=PACK)[:, cols],
-            )
-            if part == W2_PARTS - 1:
-                w2_codes[b, c] = keep.tile([P, K_PASS], U32, name="w2_codes%d%d" % (b, c), align_bytes=64)
-                w2_planes[b, c] = keep.tile([P, K_PASS], U8, name="w2_plane%d%d" % (b, c), align_bytes=64)
-                nc.vector.quantize_mx(
-                    out=w2_codes[b, c][:].bitcast(FP8X4),
-                    scales=w2_planes[b, c][:],
-                    in_=w2_woven[b, c][:].rearrange("p u c t -> p (u c t)"),
-                )
+        gain_sb = load_by_row(gain, "gain_sb", "slot_g")
 
         def first_product(bank, b, t, j, a):
-            col = K_PASS * b + P * t
             nc.tensor.matmul_mx(
                 out=bank[:],
-                lhsT=w1_codes[:, a, 2 * col : 2 * (col + P)].bitcast(FP4X4),
-                lhsT_scale=w1_planes[b][:, a, P * t : P * (t + 1)],
+                lhsT=w1_codes[b][:, a, t * P // 2 : (t + 1) * P // 2].bitcast(U8).bitcast(FP4X4),
+                lhsT_scale=planes[a][:, S + K_PASS * b + P * t : S + K_PASS * b + P * (t + 1)],
                 rhs=v_codes[a, j][:].bitcast(FP8X4),
-                rhs_scale=v_planes[a][:, j * N : (j + 1) * N],
+                rhs_scale=planes[a][:, j * N : (j + 1) * N],
                 start=(a == 0),
                 stop=(a == PASSES1 - 1),
             )
 
-        picked = [keep.tile([P, 2 * M], F32, name="picked%d" % s) for s in range(2)]
-        reduced = [keep.tile([P, 2 * M], F32, name="reduced%d" % s) for s in range(2)]
         banks = {}
-        for a in range(PASSES1):
+        for t in range(OPEN_TILES):
             for j in range(HALVES):
-                for t in range(OPEN_TILES):
-                    if a == 0:
-                        banks[t, j] = psum.tile([P, N], F32, name="bank%d" % (2 * t + j))
-                    first_product(banks[t, j], 0, t, j, a)
-        for step in range(W2_PARTS):
-            weave_w2(step)
-        load_w2(1, 1, "slot_g")
+                banks[t, j] = psum.tile([P, N], F32, name="bank%d" % (2 * t + j))
+                first_product(banks[t, j], 0, t, j, 0)
+        h_tiles = {}
         for i in range(TILES):
             b, t = divmod(i, PACK)
-            h_tiles[b, t] = keep.tile([P, S], F32, name="h%d%d" % (b, t))
+            h_tiles[i] = keep.tile([P, 2 * S], F32, name="h%d" % i)
             for j in range(HALVES):
                 if i >= OPEN_TILES:
-                    banks[t, j] = psum.tile([P, N], F32, name="bank%d" % (2 * (i % OPEN_TILES) + j))
-                    for a in range(PASSES1):
-                        first_product(banks[t, j], b, t, j, a)
-                nc.scalar.copy(out=h_tiles[b, t][:, j * N : (j + 1) * N], in_=banks[t, j][:])
-        gain_sb = keep.tile([P, PASSES2, PACK], F32, name="gain_sb", tag="v_codes01", align_bytes=64)
-        nc.sync.dma_start(out=gain_sb[:], in_=gain.rearrange("(b p t) -> p b t", p=P, t=PACK))
-        gain2 = keep.tile([P, PASSES2, PACK], F32, name="gain2")
-        nc.scalar.mul(gain2[:], gain_sb[:], -2.0)
-        for b in range(PASSES2):
-            sines = ring.tile([P, PACK, M], F32, name="sines")
-            for t in range(PACK):
-                healthy = picked[t // 2]
-                nc.vector.tensor_copy(
-                    out=healthy[:, M * (t % 2) : M * (t % 2 + 1)], in_=h_tiles[b, t][:].indirect(pos1_sb[:])
+                    banks[i, j] = psum.tile([P, N], F32, name="bank%d" % (2 * (i % OPEN_TILES) + j))
+                for a in range(1 if i < OPEN_TILES else 0, PASSES1):
+                    first_product(banks[i, j], b, t, j, a)
+                nc.scalar.copy(out=h_tiles[i][:, j * N : (j + 1) * N], in_=banks[i, j][:])
+
+        w2_codes = {}
+        w2_planes = {}
+
+        def weave_w2(b, pair):
+            woven = ring.tile([P, 2, PASSES2 * P, PACK], BF16, name="w2_woven", bufs=2, align_bytes=64)
+            for e in range(2):
+                nc.scalar.copy(
+                    out=woven[:, e].rearrange("p (j i) t -> p j t i", i=RUN),
+                    in_=w2_raw[b][:].rearrange("p t (j u i) -> p u j t i", u=PACK, i=RUN)[:, 2 * pair + e],
                 )
-                if t % 2 == 1:
-                    turns = ring.tile([P, 2 * M], I32, name="turns")
-                    nc.vector.tensor_scalar(turns[:], healthy[:], 1.0 / TWO_PI, None, ALU.mult)
-                    nc.vector.scalar_tensor_tensor(
-                        reduced[t // 2][:], turns[:], -TWO_PI, healthy[:], ALU.mult, ALU.add
-                    )
-                    nc.scalar.activation(
-                        sines[:, t - 1 : t + 1, :].rearrange("p t m -> p (t m)"), reduced[t // 2][:], ACT.Sin, scale=0.5
-                    )
-                    chunk = (PACK * b + t + 1) // 2
-                    if chunk < PASSES2 * PASSES2:
-                        for part in range(W2_PARTS):
-                            weave_w2(W2_PARTS * chunk + part)
+            w2_codes[b, pair] = keep.tile([P, 2 * PASSES2 * P], U32, name="w2_codes%d%d" % (b, pair), align_bytes=64)
+            w2_planes[b, pair] = keep.tile([P, 2 * PASSES2 * P], U8, name="w2_plane%d%d" % (b, pair), align_bytes=64)
+            nc.vector.quantize_mx(
+                out=w2_codes[b, pair][:].bitcast(FP8X4),
+                scales=w2_planes[b, pair][:],
+                in_=woven[:].rearrange("p e n t -> p (e n t)"),
+            )
+
+        x_codes = {}
+        x_planes = {}
+        for b in range(PASSES2):
+            phases = ring.tile([P, PACK, M], F32, name="phases")
+            for pair in range(2):
+                turns = ring.tile([P, 2, M], F32, name="turns", bufs=2)
+                for e in range(2):
+                    window = h_tiles[PACK * b + 2 * pair + e][:].indirect(pos1_sb[:])
+                    nc.vector.tensor_scalar(turns[:, e, :], window, 1.0 / TWO_PI, 0.25, ALU.mult, ALU.add)
+                whole = ring.tile([P, 2, M], I32, name="whole")
+                nc.vector.tensor_copy(whole[:], turns[:])
+                nc.vector.tensor_tensor(phases[:, 2 * pair : 2 * pair + 2, :], whole[:], turns[:], ALU.subtract)
+                weave_w2(b, pair)
             x_codes[b] = keep.tile([P, M], U32, name="x_codes%d" % b, align_bytes=64)
             x_planes[b] = keep.tile([P, M], U8, name="x_plane%d" % b, align_bytes=64)
             for j in range(X_PARTS):
                 cols = slice(j * X_COLS, (j + 1) * X_COLS)
-                squares = ring.tile([P, X_COLS, PACK], F32, name="squares")
-                last_squares = squares
+                cosines = ring.tile([P, X_COLS, PACK], F32, name="cosines")
                 nc.scalar.activation(
-                    squares[:].rearrange("p (c i) t -> p c t i", i=PACK),
-                    sines[:, :, cols].rearrange("p t (c i) -> p c t i", i=PACK),
-                    ACT.Square,
+                    cosines[:].rearrange("p (c i) t -> p c t i", i=PACK),
+                    phases[:, :, cols].rearrange("p t (c i) -> p c t i", i=PACK),
+                    ACT.Sin,
+                    scale=-TWO_PI,
                 )
                 x_woven = ring.tile([P, X_COLS, PACK], BF16, name="x_woven", align_bytes=64)
-                nc.vector.scalar_tensor_tensor(
+                nc.vector.tensor_tensor(
                     x_woven[:],
-                    squares[:],
-                    -0.5,
-                    gain2[:, b, :].unsqueeze(1).to_broadcast([P, X_COLS, PACK]),
-                    ALU.add,
+                    cosines[:],
+                    gain_sb[:, b, :, 0].unsqueeze(1).to_broadcast([P, X_COLS, PACK]),
                     ALU.mult,
                 )
                 nc.vector.quantize_mx(
@@ -256,51 +219,43 @@ def tile_list_escapement_wear_match_kernel(
                     in_=x_woven[:].rearrange("p m t -> p (m t)"),
                 )
 
-        nc.scalar.activation(warm[:, 1:2], last_squares[:, 0, 0:1], ACT.Exp)
-        nw_sb = keep.tile([P, PASSES2, PACK], F32, name="nw_sb", tag="v_codes00", align_bytes=64)
-        nc.sync.dma_start(out=nw_sb[:], in_=nw.rearrange("(b p t) -> p b t", p=P, t=PACK))
+        nw_sb = load_by_row(nw, "nw_sb", "slot_a")
         y_banks = {}
         for b in range(PASSES2):
-            for c in range(PASSES2):
-                for u in range(PACK):
-                    if b == 0:
-                        y_banks[c, u] = psum.tile([P, M], F32, name="bank%d" % (PACK * c + u))
-                    nc.tensor.matmul_mx(
-                        out=y_banks[c, u][:],
-                        lhsT=w2_codes[b, c][:, P * u : P * (u + 1)].bitcast(FP8X4),
-                        lhsT_scale=w2_planes[b, c][:, P * u : P * (u + 1)],
-                        rhs=x_codes[b][:].bitcast(FP8X4),
-                        rhs_scale=x_planes[b][:],
-                        start=(b == 0),
-                        stop=(b == PASSES2 - 1),
-                    )
-        out_rows = out.rearrange("(c p u) m -> c u p m", p=P, u=PACK)
-        spots = [
-            picked[1][:, 0:M],
-            picked[1][:, M : 2 * M],
-            reduced[1][:, 0:M],
-            last_squares[:].rearrange("p m t -> p (m t)")[:, M : 2 * M],
-        ]
-
-        def spot(i):
-            return spots[i] if i < len(spots) else spots[1 + (i - 1) % 3]
-
-        def pick_suspects(i):
-            nc.vector.tensor_copy(out=spot(i), in_=h_tiles[divmod(i, PACK)][:].indirect(pos2_sb[:]))
-
-        for i in range(len(spots)):
-            pick_suspects(i)
+            for i in range(TILES):
+                c, u = divmod(i, PACK)
+                first = P * (PASSES2 * (u % 2) + c)
+                if b == 0:
+                    y_banks[i] = psum.tile([P, M], F32, name="bank%d" % i)
+                nc.tensor.matmul_mx(
+                    out=y_banks[i][:],
+                    lhsT=w2_codes[b, u // 2][:, first : first + P].bitcast(FP8X4),
+                    lhsT_scale=w2_planes[b, u // 2][:, first : first + P],
+                    rhs=x_codes[b][:].bitcast(FP8X4),
+                    rhs_scale=x_planes[b][:],
+                    start=(b == 0),
+                    stop=(b == PASSES2 - 1),
+                )
+        out_rows = out.rearrange("(c j u i) m -> c u j i m", u=PACK, i=RUN, c=PASSES2)
+        FUSED = ()
         for i in range(TILES):
             c, u = divmod(i, PACK)
+            if i in FUSED:
+                expected = ring.tile([P, M], F32, name="expected")
+                nc.scalar.copy(out=expected[:], in_=y_banks[i][:])
+            else:
+                suspects = ring.tile([P, M], F32, name="suspects", bufs=EARLY_PICKS)
+                nc.vector.tensor_copy(out=suspects[:], in_=h_tiles[i][:, 0:S].indirect(pos2_sb[:]))
             width = M // 2 if i == TILES - 1 else M
             for first in range(0, M, width):
                 cols = slice(first, first + width)
                 diff = ring.tile([P, width], F32, name="diff", bufs=4)
-                nc.vector.tensor_tensor(diff[:], y_banks[c, u][:, cols], spot(i)[:, cols], ALU.subtract)
+                if i in FUSED:
+                    nc.vector.tensor_tensor(diff[:], h_tiles[i][:].indirect(pos2_sb[:]), expected[:], ALU.subtract)
+                else:
+                    nc.vector.tensor_tensor(diff[:], y_banks[i][:, cols], suspects[:, cols], ALU.subtract)
                 square = ring.tile([P, width], F32, name="square", bufs=3)
                 nc.scalar.activation(square[:], diff[:], ACT.Square)
                 score = ring.tile([P, width], F32, name="score", bufs=4)
-                nc.scalar.activation(score[:], square[:], ACT.Exp, scale=nw_sb[:, c, u : u + 1])
-                nc.sync.dma_start(out=out_rows[c, u][:, cols], in_=score[:])
-            if len(spots) <= i + 2 < TILES:
-                pick_suspects(i + 2)
+                nc.scalar.activation(score[:], square[:], ACT.Exp, scale=nw_sb[:, c, u, 0:1])
+                nc.sync.dma_start(out=out_rows[c, u][:, :, cols], in_=score[:])

@@ -19,7 +19,6 @@ ACT = mybir.ActivationFunctionType
 
 P = 128
 PACK = 4
-RUN = 8
 K_PASS = P * PACK
 PASSES1 = K // K_PASS
 PASSES2 = H // K_PASS
@@ -32,6 +31,8 @@ FIRST_ROW = P - PASSES1 * SCALE_ROWS
 TWO_PI = 2.0 * math.pi
 X_PARTS = 2
 X_COLS = M // X_PARTS
+W2_SLOTS = (("slot_a", "slot_b"), ("slot_r", "slot_w"))
+W2_PIECES = 2
 TILES = PASSES2 * PACK
 OPEN_TILES = 2
 EARLY_PICKS = 2
@@ -42,7 +43,6 @@ def tile_list_escapement_wear_match_kernel(
 ):
     nc = tc.nc
     with ExitStack() as ctx:
-        ctx.enter_context(nc.allow_non_contiguous_dma(reason="gain and nw land one value a row tile on each partition"))
         lists = ctx.enter_context(tc.tile_pool(name="lists", bufs=1))
         keep = ctx.enter_context(tc.tile_pool(name="keep", bufs=1))
         ring = ctx.enter_context(tc.tile_pool(name="ring", bufs=2))
@@ -56,7 +56,7 @@ def tile_list_escapement_wear_match_kernel(
         w1_scale_raw = keep.tile([P, H], U8, name="w1_scale_raw", align_bytes=64)
         planes = [keep.tile([P, S + H], U8, name="planes%d" % a, align_bytes=64) for a in range(PASSES1)]
         nc.vector.memset(tab_scale_window[0:FIRST_ROW, :].bitcast(I32), 0)
-        nc.gpsimd.memset(w1_scale_raw[P // 2 : FIRST_ROW, :].bitcast(I32), 0)
+        nc.gpsimd.memset(w1_scale_raw[0:FIRST_ROW, :].bitcast(I32), 0)
         nc.vector.memset(planes[0][:].bitcast(I32), 0)
         for a in range(1, PASSES1):
             nc.gpsimd.memset(planes[a][:].bitcast(I32), 0)
@@ -76,7 +76,7 @@ def tile_list_escapement_wear_match_kernel(
             tab_windows[a] = window
 
         load_table(0, "slot_a")
-        w1_raw = keep.tile([P, PASSES1, H // 2], I32, name="w1_raw", align_bytes=64)
+        w1_raw = keep.tile([P, PASSES1, H // 2], I32, name="w1_raw", tag="slot_w", align_bytes=64)
         nc.sync.dma_start(out=w1_raw[:], in_=w1_words.bitcast(I32).rearrange("a p w -> p a w"))
         nc.sync.dma_start(pos1_sb[:], pos1)
         nc.sync.dma_start(pos2_sb[:], pos2)
@@ -84,17 +84,16 @@ def tile_list_escapement_wear_match_kernel(
 
         v_packed = keep.tile([P, S], U8, name="v_packed", tag="slot_g", align_bytes=64)
         nc.vector.tensor_copy(out=v_packed[:], in_=tab_scale_window[:].indirect(offs_sb[:]))
-        scale_rows = keep.tile([P, (S + H) // 4], I32, name="scale_rows", align_bytes=64)
-        upper = slice(P // 2, P)
+        scale_rows = keep.tile([P, S + H], U8, name="scale_rows", tag="slot_r", align_bytes=64)
         nc.vector.tensor_copy(
-            out=scale_rows[upper, S // 4 :].rearrange("p (b t j w) -> p b t j w", b=PASSES2, t=PACK, w=RUN // 4),
-            in_=w1_scale_raw[upper].bitcast(I32).rearrange("p (b j t w) -> p b t j w", b=PASSES2, t=PACK, w=RUN // 4),
+            out=scale_rows[:, S:].rearrange("p (b t c) -> p b t c", b=PASSES2, t=PACK),
+            in_=w1_scale_raw[:].rearrange("p (b c t) -> p b t c", b=PASSES2, t=PACK),
         )
-        nc.vector.tensor_copy(out=scale_rows[upper, 0 : S // 4], in_=v_packed[upper].bitcast(I32))
+        nc.vector.tensor_copy(out=scale_rows[:, 0:S].bitcast(I32), in_=v_packed[:].bitcast(I32))
         for a in range(PASSES1):
             for q in range(4):
                 first = FIRST_ROW + SCALE_ROWS * a + 4 * q
-                nc.sync.dma_start(out=planes[a][QUAD * q : QUAD * q + 4, :].bitcast(I32), in_=scale_rows[first : first + 4, :])
+                nc.sync.dma_start(out=planes[a][QUAD * q : QUAD * q + 4, :].bitcast(I32), in_=scale_rows[first : first + 4, :].bitcast(I32))
                 if (a, q) == (1, 0):
                     load_table(2, "slot_g")
 
@@ -104,8 +103,8 @@ def tile_list_escapement_wear_match_kernel(
             words = slice(b * K_PASS // 2, (b + 1) * K_PASS // 2)
             w1_codes[b] = keep.tile([P, PASSES1, K_PASS // 2], I32, name="w1_codes%d" % b, align_bytes=64)
             nc.vector.tensor_copy(
-                out=w1_codes[b][:].rearrange("p a (t j w) -> p t a j w", t=PACK, w=RUN // 2),
-                in_=w1_raw[:, :, words].rearrange("p a (j t w) -> p t a j w", t=PACK, w=RUN // 2),
+                out=w1_codes[b][:].bitcast(U16).rearrange("p a (t c) -> p t a c", t=PACK),
+                in_=w1_raw[:, :, words].bitcast(U16).rearrange("p a (c t) -> p t a c", t=PACK),
             )
 
         v_codes = {}
@@ -121,18 +120,15 @@ def tile_list_escapement_wear_match_kernel(
         order_w1(1)
 
         w2_raw = {}
-        w2_rows = w2.rearrange("(b j t i) n -> b t j i n", t=PACK, i=RUN, b=PASSES2)
         for b in range(PASSES2):
-            w2_raw[b] = keep.tile([P, PACK, H], F32, name="w2_raw%d" % b, tag="slot_" + "ab"[b], align_bytes=64)
-            for t in range(PACK):
-                nc.sync.dma_start(out=w2_raw[b][:, t, :], in_=w2_rows[b, t])
+            for c in range(PASSES2):
+                w2_raw[b, c] = keep.tile([P, PACK, K_PASS], F32, name="w2_raw%d%d" % (b, c), tag=W2_SLOTS[b][c], align_bytes=64)
+                rows = w2[K_PASS * b : K_PASS * (b + 1), K_PASS * c : K_PASS * (c + 1)]
+                nc.sync.dma_start(out=w2_raw[b, c][:], in_=rows.rearrange("(p t) n -> p t n", t=PACK))
 
         def load_by_row(vec, name, tag):
-            tile = keep.tile([P, PASSES2, PACK, RUN], F32, name=name, tag=tag, align_bytes=64)
-            rows = vec.rearrange("(b j t i o) -> b t j i o", t=PACK, i=RUN, b=PASSES2, o=1)
-            for b in range(PASSES2):
-                for t in range(PACK):
-                    nc.sync.dma_start(out=tile[:, b, t, 0:1], in_=rows[b, t])
+            tile = keep.tile([P, PASSES2, PACK], F32, name=name, tag=tag, align_bytes=64)
+            nc.sync.dma_start(out=tile[:], in_=vec.rearrange("(b p t) -> p b t", p=P, t=PACK))
             return tile
 
         gain_sb = load_by_row(gain, "gain_sb", "slot_g")
@@ -167,19 +163,21 @@ def tile_list_escapement_wear_match_kernel(
         w2_codes = {}
         w2_planes = {}
 
-        def weave_w2(b, pair):
-            woven = ring.tile([P, 2, PASSES2 * P, PACK], BF16, name="w2_woven", bufs=2, align_bytes=64)
-            for e in range(2):
+        def weave_w2(b, c):
+            woven = ring.tile([P, PACK, P, PACK], BF16, name="w2_woven", bufs=2, align_bytes=64)
+            width = P // W2_PIECES
+            for piece in range(W2_PIECES):
+                cols = slice(piece * width, (piece + 1) * width)
                 nc.scalar.copy(
-                    out=woven[:, e].rearrange("p (j i) t -> p j t i", i=RUN),
-                    in_=w2_raw[b][:].rearrange("p t (j u i) -> p u j t i", u=PACK, i=RUN)[:, 2 * pair + e],
+                    out=woven[:, :, cols, :].rearrange("p u n t -> p n t u"),
+                    in_=w2_raw[b, c][:].rearrange("p t (n u) -> p n t u", u=PACK)[:, cols],
                 )
-            w2_codes[b, pair] = keep.tile([P, 2 * PASSES2 * P], U32, name="w2_codes%d%d" % (b, pair), align_bytes=64)
-            w2_planes[b, pair] = keep.tile([P, 2 * PASSES2 * P], U8, name="w2_plane%d%d" % (b, pair), align_bytes=64)
+            w2_codes[b, c] = keep.tile([P, K_PASS], U32, name="w2_codes%d%d" % (b, c), align_bytes=64)
+            w2_planes[b, c] = keep.tile([P, K_PASS], U8, name="w2_plane%d%d" % (b, c), align_bytes=64)
             nc.vector.quantize_mx(
-                out=w2_codes[b, pair][:].bitcast(FP8X4),
-                scales=w2_planes[b, pair][:],
-                in_=woven[:].rearrange("p e n t -> p (e n t)"),
+                out=w2_codes[b, c][:].bitcast(FP8X4),
+                scales=w2_planes[b, c][:],
+                in_=woven[:].rearrange("p u n t -> p (u n t)"),
             )
 
         x_codes = {}
@@ -210,7 +208,7 @@ def tile_list_escapement_wear_match_kernel(
                 nc.vector.tensor_tensor(
                     x_woven[:],
                     cosines[:],
-                    gain_sb[:, b, :, 0].unsqueeze(1).to_broadcast([P, X_COLS, PACK]),
+                    gain_sb[:, b, :].unsqueeze(1).to_broadcast([P, X_COLS, PACK]),
                     ALU.mult,
                 )
                 nc.vector.quantize_mx(
@@ -224,19 +222,18 @@ def tile_list_escapement_wear_match_kernel(
         for b in range(PASSES2):
             for i in range(TILES):
                 c, u = divmod(i, PACK)
-                first = P * (PASSES2 * (u % 2) + c)
                 if b == 0:
                     y_banks[i] = psum.tile([P, M], F32, name="bank%d" % i)
                 nc.tensor.matmul_mx(
                     out=y_banks[i][:],
-                    lhsT=w2_codes[b, u // 2][:, first : first + P].bitcast(FP8X4),
-                    lhsT_scale=w2_planes[b, u // 2][:, first : first + P],
+                    lhsT=w2_codes[b, c][:, P * u : P * (u + 1)].bitcast(FP8X4),
+                    lhsT_scale=w2_planes[b, c][:, P * u : P * (u + 1)],
                     rhs=x_codes[b][:].bitcast(FP8X4),
                     rhs_scale=x_planes[b][:],
                     start=(b == 0),
                     stop=(b == PASSES2 - 1),
                 )
-        out_rows = out.rearrange("(c j u i) m -> c u j i m", u=PACK, i=RUN, c=PASSES2)
+        out_rows = out.rearrange("(c p u) m -> c u p m", p=P, u=PACK)
         FUSED = ()
         for i in range(TILES):
             c, u = divmod(i, PACK)
@@ -257,5 +254,5 @@ def tile_list_escapement_wear_match_kernel(
                 square = ring.tile([P, width], F32, name="square", bufs=3)
                 nc.scalar.activation(square[:], diff[:], ACT.Square)
                 score = ring.tile([P, width], F32, name="score", bufs=4)
-                nc.scalar.activation(score[:], square[:], ACT.Exp, scale=nw_sb[:, c, u, 0:1])
-                nc.sync.dma_start(out=out_rows[c, u][:, :, cols], in_=score[:])
+                nc.scalar.activation(score[:], square[:], ACT.Exp, scale=nw_sb[:, c, u : u + 1])
+                nc.sync.dma_start(out=out_rows[c, u][:, cols], in_=score[:])

@@ -29,13 +29,13 @@ QUAD = 32
 SCALE_ROWS = 16
 FIRST_ROW = P - PASSES1 * SCALE_ROWS
 TWO_PI = 2.0 * math.pi
-X_PARTS = 2
+X_PARTS = 1
 X_COLS = M // X_PARTS
-W2_SLOTS = (("slot_a", "slot_b"), ("slot_r", "slot_w"))
+W2_SLOTS = (("slot_a", "slot_r"), ("slot_b", "slot_w"))
 W2_PIECES = 2
+GPSIMD_SQUARES = ()
 TILES = PASSES2 * PACK
 OPEN_TILES = 2
-EARLY_PICKS = 2
 
 
 def tile_list_escapement_wear_match_kernel(
@@ -152,7 +152,7 @@ def tile_list_escapement_wear_match_kernel(
         h_tiles = {}
         for i in range(TILES):
             b, t = divmod(i, PACK)
-            h_tiles[i] = keep.tile([P, 2 * S], F32, name="h%d" % i)
+            h_tiles[i] = keep.tile([P, 2 * S], F32, name="h%d" % i, align_bytes=64)
             for j in range(HALVES):
                 if i >= OPEN_TILES:
                     banks[i, j] = psum.tile([P, N], F32, name="bank%d" % (2 * (i % OPEN_TILES) + j))
@@ -163,8 +163,8 @@ def tile_list_escapement_wear_match_kernel(
         w2_codes = {}
         w2_planes = {}
 
-        def weave_w2(b, c):
-            woven = ring.tile([P, PACK, P, PACK], BF16, name="w2_woven", bufs=2, align_bytes=64)
+        def weave_w2(b, c, room):
+            woven = room.bitcast(BF16).rearrange("p (u n t) -> p u n t", u=PACK, t=PACK)
             width = P // W2_PIECES
             for piece in range(W2_PIECES):
                 cols = slice(piece * width, (piece + 1) * width)
@@ -177,53 +177,91 @@ def tile_list_escapement_wear_match_kernel(
             nc.vector.quantize_mx(
                 out=w2_codes[b, c][:].bitcast(FP8X4),
                 scales=w2_planes[b, c][:],
-                in_=woven[:].rearrange("p u n t -> p (u n t)"),
+                in_=room.bitcast(BF16),
+            )
+
+        def spare(i):
+            return h_tiles[i][:, S : 2 * S]
+
+        turns = {}
+        whole = {}
+        cosines = [keep.tile([P, 2, M, 2], F32, name="cosines%d" % b) for b in range(PASSES2)]
+
+        def pick_healthy(i):
+            pair, e = divmod(i, 2)
+            if e == 0:
+                turns[pair] = ring.tile([P, 2, M], F32, name="turns")
+            window = h_tiles[i][:].indirect(pos1_sb[:])
+            nc.vector.tensor_scalar(turns[pair][:, e, :], window, 1.0 / TWO_PI, 0.25, ALU.mult, ALU.add)
+            if e == 1:
+                whole[pair] = ring.tile([P, 2, M], I32, name="whole", align_bytes=64)
+                nc.gpsimd.tensor_scalar(whole[pair][:], turns[pair][:], 1.0, 0.0, ALU.mult, ALU.add)
+
+        def cosine(pair):
+            phases = spare((2 * pair + 2) % TILES).rearrange("p (e m) -> p e m", e=2)
+            nc.vector.tensor_tensor(phases, whole[pair][:], turns[pair][:], ALU.subtract)
+            nc.scalar.activation(
+                cosines[pair // 2][:, pair % 2].rearrange("p (c i) e -> p c e i", i=PACK),
+                phases.rearrange("p e (c i) -> p c e i", i=PACK),
+                ACT.Sin,
+                scale=-TWO_PI,
             )
 
         x_codes = {}
         x_planes = {}
-        for b in range(PASSES2):
-            phases = ring.tile([P, PACK, M], F32, name="phases")
-            for pair in range(2):
-                turns = ring.tile([P, 2, M], F32, name="turns", bufs=2)
-                for e in range(2):
-                    window = h_tiles[PACK * b + 2 * pair + e][:].indirect(pos1_sb[:])
-                    nc.vector.tensor_scalar(turns[:, e, :], window, 1.0 / TWO_PI, 0.25, ALU.mult, ALU.add)
-                whole = ring.tile([P, 2, M], I32, name="whole")
-                nc.vector.tensor_copy(whole[:], turns[:])
-                nc.vector.tensor_tensor(phases[:, 2 * pair : 2 * pair + 2, :], whole[:], turns[:], ALU.subtract)
-                weave_w2(b, pair)
+        x_woven = {}
+
+        def make_x(b):
             x_codes[b] = keep.tile([P, M], U32, name="x_codes%d" % b, align_bytes=64)
             x_planes[b] = keep.tile([P, M], U8, name="x_plane%d" % b, align_bytes=64)
+            x_woven[b] = keep.tile([P, M, PACK], BF16, name="x_woven%d" % b, align_bytes=64)
             for j in range(X_PARTS):
                 cols = slice(j * X_COLS, (j + 1) * X_COLS)
-                cosines = ring.tile([P, X_COLS, PACK], F32, name="cosines")
-                nc.scalar.activation(
-                    cosines[:].rearrange("p (c i) t -> p c t i", i=PACK),
-                    phases[:, :, cols].rearrange("p t (c i) -> p c t i", i=PACK),
-                    ACT.Sin,
-                    scale=-TWO_PI,
-                )
-                x_woven = ring.tile([P, X_COLS, PACK], BF16, name="x_woven", align_bytes=64)
                 nc.vector.tensor_tensor(
-                    x_woven[:],
-                    cosines[:],
-                    gain_sb[:, b, :].unsqueeze(1).to_broadcast([P, X_COLS, PACK]),
+                    x_woven[b][:, cols].rearrange("p m (h e) -> p m h e", e=2),
+                    cosines[b][:, :, cols].rearrange("p h m e -> p m h e"),
+                    gain_sb[:, b, :].rearrange("p (h e) -> p h e", e=2).unsqueeze(1).to_broadcast([P, X_COLS, 2, 2]),
                     ALU.mult,
                 )
+            for j in range(X_PARTS):
+                cols = slice(j * X_COLS, (j + 1) * X_COLS)
                 nc.vector.quantize_mx(
                     out=x_codes[b][:, cols].bitcast(FP8X4),
                     scales=x_planes[b][:, cols],
-                    in_=x_woven[:].rearrange("p m t -> p (m t)"),
+                    in_=x_woven[b][:, cols].rearrange("p m t -> p (m t)"),
                 )
 
+        suspects = {}
+
+        def pick_suspects(i, spot, columns):
+            suspects[i] = spot
+            nc.vector.tensor_copy(out=spot, in_=h_tiles[i][:, 0:columns].indirect(pos2_sb[:]))
+
+        pick_healthy(0)
+        pick_healthy(1)
+        for pair in range(PACK):
+            if pair < PACK - 1:
+                pick_healthy(2 * pair + 2)
+            else:
+                pick_suspects(0, spare(TILES - 1)[:, 0:M], 2 * S)
+            cosine(pair)
+            if pair < PACK - 1:
+                pick_healthy(2 * pair + 3)
+            if pair in (1, 2):
+                room = ring.tile([P, 2 * M], F32, name="w2_woven", align_bytes=64)
+                weave_w2(pair - 1, 0, room[:])
+        make_x(0)
+        pick_suspects(1, turns[PACK - 1][:, 0, :], S)
+        make_x(1)
+        pick_suspects(2, x_woven[1][:].rearrange("p m t -> p (m t)").bitcast(F32)[:, M : 2 * M], S)
+        weave_w2(0, 1, spare(0))
+        weave_w2(1, 1, whole[PACK - 1][:].rearrange("p e m -> p (e m)").bitcast(F32))
         nw_sb = load_by_row(nw, "nw_sb", "slot_a")
         y_banks = {}
-        for b in range(PASSES2):
-            for i in range(TILES):
-                c, u = divmod(i, PACK)
-                if b == 0:
-                    y_banks[i] = psum.tile([P, M], F32, name="bank%d" % i)
+        for i in range(TILES):
+            c, u = divmod(i, PACK)
+            y_banks[i] = psum.tile([P, M], F32, name="bank%d" % i)
+            for b in range(PASSES2):
                 nc.tensor.matmul_mx(
                     out=y_banks[i][:],
                     lhsT=w2_codes[b, c][:, P * u : P * (u + 1)].bitcast(FP8X4),
@@ -234,25 +272,22 @@ def tile_list_escapement_wear_match_kernel(
                     stop=(b == PASSES2 - 1),
                 )
         out_rows = out.rearrange("(c p u) m -> c u p m", p=P, u=PACK)
-        FUSED = ()
         for i in range(TILES):
             c, u = divmod(i, PACK)
-            if i in FUSED:
-                expected = ring.tile([P, M], F32, name="expected")
-                nc.scalar.copy(out=expected[:], in_=y_banks[i][:])
-            else:
-                suspects = ring.tile([P, M], F32, name="suspects", bufs=EARLY_PICKS)
-                nc.vector.tensor_copy(out=suspects[:], in_=h_tiles[i][:, 0:S].indirect(pos2_sb[:]))
             width = M // 2 if i == TILES - 1 else M
             for first in range(0, M, width):
                 cols = slice(first, first + width)
                 diff = ring.tile([P, width], F32, name="diff", bufs=4)
-                if i in FUSED:
-                    nc.vector.tensor_tensor(diff[:], h_tiles[i][:].indirect(pos2_sb[:]), expected[:], ALU.subtract)
-                else:
-                    nc.vector.tensor_tensor(diff[:], y_banks[i][:, cols], suspects[:, cols], ALU.subtract)
+                nc.vector.tensor_tensor(diff[:], y_banks[i][:, cols], suspects[i][:, cols], ALU.subtract)
                 square = ring.tile([P, width], F32, name="square", bufs=3)
-                nc.scalar.activation(square[:], diff[:], ACT.Square)
+                if i in GPSIMD_SQUARES:
+                    nc.gpsimd.tensor_tensor(square[:], diff[:], diff[:], ALU.mult)
+                elif i == TILES - 1 and True:
+                    nc.vector.tensor_tensor(square[:], diff[:], diff[:], ALU.mult)
+                else:
+                    nc.scalar.activation(square[:], diff[:], ACT.Square)
                 score = ring.tile([P, width], F32, name="score", bufs=4)
                 nc.scalar.activation(score[:], square[:], ACT.Exp, scale=nw_sb[:, c, u : u + 1])
                 nc.sync.dma_start(out=out_rows[c, u][:, cols], in_=score[:])
+            if 1 <= i < TILES - 2:
+                pick_suspects(i + 2, suspects[i], S)

@@ -29,9 +29,9 @@ QUAD = 32
 SCALE_ROWS = 16
 FIRST_ROW = P - PASSES1 * SCALE_ROWS
 TWO_PI = 2.0 * math.pi
-X_PARTS = 1
+X_PARTS = 2
 X_COLS = M // X_PARTS
-W2_SLOTS = (("slot_a", "slot_r"), ("slot_b", "slot_w"))
+W2_SLOTS = (("slot_b", "slot_w"), ("slot_r", "slot_a"))
 W2_PIECES = 2
 GPSIMD_SQUARES = ()
 TILES = PASSES2 * PACK
@@ -61,6 +61,10 @@ def tile_list_escapement_wear_match_kernel(
         for a in range(1, PASSES1):
             nc.gpsimd.memset(planes[a][:].bitcast(I32), 0)
 
+        warm = keep.tile([P, 2], F32, name="warm")
+        nc.gpsimd.memset(warm[:, 0:1], 0.0)
+        nc.scalar.activation(warm[:, 1:2], warm[:, 0:1], ACT.Sin)
+
         nc.sync.dma_start(offs_sb[:], offs)
         for tile, scales in ((tab_scale_window, tab_scales), (w1_scale_raw, w1_scales)):
             scale_rows = scales.rearrange("a q t -> (a q) t").bitcast(I32)
@@ -76,8 +80,14 @@ def tile_list_escapement_wear_match_kernel(
             tab_windows[a] = window
 
         load_table(0, "slot_a")
-        w1_raw = keep.tile([P, PASSES1, H // 2], I32, name="w1_raw", tag="slot_w", align_bytes=64)
-        nc.sync.dma_start(out=w1_raw[:], in_=w1_words.bitcast(I32).rearrange("a p w -> p a w"))
+        w1_raw = {}
+
+        def load_w1(b, tag):
+            w1_raw[b] = keep.tile([P, PASSES1, K_PASS // 2], I32, name="w1_raw%d" % b, tag=tag, align_bytes=64)
+            words = slice(b * K_PASS // 2, (b + 1) * K_PASS // 2)
+            nc.sync.dma_start(out=w1_raw[b][:], in_=w1_words.bitcast(I32).rearrange("a p w -> p a w")[:, :, words])
+
+        load_w1(0, "slot_w")
         nc.sync.dma_start(pos1_sb[:], pos1)
         nc.sync.dma_start(pos2_sb[:], pos2)
         load_table(1, "slot_b")
@@ -85,7 +95,7 @@ def tile_list_escapement_wear_match_kernel(
         v_packed = keep.tile([P, S], U8, name="v_packed", tag="slot_g", align_bytes=64)
         nc.vector.tensor_copy(out=v_packed[:], in_=tab_scale_window[:].indirect(offs_sb[:]))
         scale_rows = keep.tile([P, S + H], U8, name="scale_rows", tag="slot_r", align_bytes=64)
-        nc.vector.tensor_copy(
+        nc.gpsimd.tensor_copy(
             out=scale_rows[:, S:].rearrange("p (b t c) -> p b t c", b=PASSES2, t=PACK),
             in_=w1_scale_raw[:].rearrange("p (b c t) -> p b t c", b=PASSES2, t=PACK),
         )
@@ -99,12 +109,12 @@ def tile_list_escapement_wear_match_kernel(
 
         w1_codes = {}
 
-        def order_w1(b):
-            words = slice(b * K_PASS // 2, (b + 1) * K_PASS // 2)
-            w1_codes[b] = keep.tile([P, PASSES1, K_PASS // 2], I32, name="w1_codes%d" % b, align_bytes=64)
+        def order_w1(pair):
+            b, half = divmod(pair, 2)
+            w1_codes[pair] = keep.tile([P, PASSES1, P], I32, name="w1_codes%d" % pair, align_bytes=64)
             nc.vector.tensor_copy(
-                out=w1_codes[b][:].bitcast(U16).rearrange("p a (t c) -> p t a c", t=PACK),
-                in_=w1_raw[:, :, words].bitcast(U16).rearrange("p a (c t) -> p t a c", t=PACK),
+                out=w1_codes[pair][:].bitcast(U16).rearrange("p a (e c) -> p e a c", e=2),
+                in_=w1_raw[b][:].bitcast(U16).rearrange("p a (c t) -> p t a c", t=PACK)[:, 2 * half : 2 * half + 2],
             )
 
         v_codes = {}
@@ -117,7 +127,9 @@ def tile_list_escapement_wear_match_kernel(
                 )
             if a == 0:
                 order_w1(0)
-        order_w1(1)
+                load_w1(1, "slot_a")
+        for pair in range(1, PACK):
+            order_w1(pair)
 
         w2_raw = {}
         for b in range(PASSES2):
@@ -136,7 +148,7 @@ def tile_list_escapement_wear_match_kernel(
         def first_product(bank, b, t, j, a):
             nc.tensor.matmul_mx(
                 out=bank[:],
-                lhsT=w1_codes[b][:, a, t * P // 2 : (t + 1) * P // 2].bitcast(U8).bitcast(FP4X4),
+                lhsT=w1_codes[2 * b + t // 2][:, a, t % 2 * P // 2 : (t % 2 + 1) * P // 2].bitcast(U8).bitcast(FP4X4),
                 lhsT_scale=planes[a][:, S + K_PASS * b + P * t : S + K_PASS * b + P * (t + 1)],
                 rhs=v_codes[a, j][:].bitcast(FP8X4),
                 rhs_scale=planes[a][:, j * N : (j + 1) * N],
@@ -209,33 +221,36 @@ def tile_list_escapement_wear_match_kernel(
 
         x_codes = {}
         x_planes = {}
-        x_woven = {}
 
-        def make_x(b):
+        def weigh(engine, b, cols, woven):
+            width = cols.stop - cols.start
+            engine.tensor_tensor(
+                woven.rearrange("p (m h e) -> p m h e", h=2, e=2),
+                cosines[b][:, :, cols].rearrange("p h m e -> p m h e"),
+                gain_sb[:, b, :].rearrange("p (h e) -> p h e", e=2).unsqueeze(1).to_broadcast([P, width, 2, 2]),
+                ALU.mult,
+            )
+
+        def quantize_x(b, cols, woven):
+            nc.vector.quantize_mx(out=x_codes[b][:, cols].bitcast(FP8X4), scales=x_planes[b][:, cols], in_=woven)
+
+        for b in range(PASSES2):
             x_codes[b] = keep.tile([P, M], U32, name="x_codes%d" % b, align_bytes=64)
             x_planes[b] = keep.tile([P, M], U8, name="x_plane%d" % b, align_bytes=64)
-            x_woven[b] = keep.tile([P, M, PACK], BF16, name="x_woven%d" % b, align_bytes=64)
-            for j in range(X_PARTS):
-                cols = slice(j * X_COLS, (j + 1) * X_COLS)
-                nc.vector.tensor_tensor(
-                    x_woven[b][:, cols].rearrange("p m (h e) -> p m h e", e=2),
-                    cosines[b][:, :, cols].rearrange("p h m e -> p m h e"),
-                    gain_sb[:, b, :].rearrange("p (h e) -> p h e", e=2).unsqueeze(1).to_broadcast([P, X_COLS, 2, 2]),
-                    ALU.mult,
-                )
-            for j in range(X_PARTS):
-                cols = slice(j * X_COLS, (j + 1) * X_COLS)
-                nc.vector.quantize_mx(
-                    out=x_codes[b][:, cols].bitcast(FP8X4),
-                    scales=x_planes[b][:, cols],
-                    in_=x_woven[b][:, cols].rearrange("p m t -> p (m t)"),
-                )
 
         suspects = {}
 
         def pick_suspects(i, spot, columns):
             suspects[i] = spot
             nc.vector.tensor_copy(out=spot, in_=h_tiles[i][:, 0:columns].indirect(pos2_sb[:]))
+
+        def weigh_first_pass(half):
+            room = whole[2 + half][:, 0, :].bitcast(BF16)
+            for piece in range(2):
+                first = X_COLS * half + piece * X_COLS // 2
+                cols = slice(first, first + X_COLS // 2)
+                weigh(nc.gpsimd, 0, cols, room[:, piece * M : (piece + 1) * M])
+            return room
 
         pick_healthy(0)
         pick_healthy(1)
@@ -244,18 +259,27 @@ def tile_list_escapement_wear_match_kernel(
                 pick_healthy(2 * pair + 2)
             else:
                 pick_suspects(0, spare(TILES - 1)[:, 0:M], 2 * S)
+                pick_suspects(1, spare(TILES - 1)[:, M : 2 * M], S)
             cosine(pair)
             if pair < PACK - 1:
                 pick_healthy(2 * pair + 3)
             if pair in (1, 2):
                 room = ring.tile([P, 2 * M], F32, name="w2_woven", align_bytes=64)
                 weave_w2(pair - 1, 0, room[:])
-        make_x(0)
-        pick_suspects(1, turns[PACK - 1][:, 0, :], S)
-        make_x(1)
-        pick_suspects(2, x_woven[1][:].rearrange("p m t -> p (m t)").bitcast(F32)[:, M : 2 * M], S)
+        halves = [slice(X_COLS * half, X_COLS * (half + 1)) for half in range(X_PARTS)]
+        first_woven = [weigh_first_pass(half) for half in range(X_PARTS)]
+        for e in range(2):
+            pick_suspects(2 + e, turns[PACK - 1][:, e, :], S)
+        x_woven = keep.tile([P, X_PARTS, X_COLS * PACK], BF16, name="x_woven", align_bytes=64)
+        for half in range(X_PARTS):
+            weigh(nc.vector, 1, halves[half], x_woven[:, half, :])
+            quantize_x(0, halves[half], first_woven[half])
+        for half in range(X_PARTS):
+            quantize_x(1, halves[half], x_woven[:, half, :])
+        pick_suspects(4, x_woven[:, 1, :].bitcast(F32), S)
         weave_w2(0, 1, spare(0))
-        weave_w2(1, 1, whole[PACK - 1][:].rearrange("p e m -> p (e m)").bitcast(F32))
+        weave_w2(1, 1, spare(TILES - 2))
+        nc.scalar.activation(warm[:, 1:2], cosines[1][:, 1, 0, 0:1], ACT.Exp)
         nw_sb = load_by_row(nw, "nw_sb", "slot_a")
         y_banks = {}
         for i in range(TILES):
@@ -289,5 +313,5 @@ def tile_list_escapement_wear_match_kernel(
                 score = ring.tile([P, width], F32, name="score", bufs=4)
                 nc.scalar.activation(score[:], square[:], ACT.Exp, scale=nw_sb[:, c, u : u + 1])
                 nc.sync.dma_start(out=out_rows[c, u][:, cols], in_=score[:])
-            if 1 <= i < TILES - 2:
-                pick_suspects(i + 2, suspects[i], S)
+            if 2 <= i < TILES - 3:
+                pick_suspects(i + 3, suspects[i], S)

@@ -249,7 +249,7 @@ def tile_list_escapement_wear_match_kernel(
             for piece in range(2):
                 first = X_COLS * half + piece * X_COLS // 2
                 cols = slice(first, first + X_COLS // 2)
-                weigh(nc.gpsimd, 0, cols, room[:, piece * M : (piece + 1) * M])
+                weigh(nc.vector, 0, cols, room[:, piece * M : (piece + 1) * M])
             return room
 
         pick_healthy(0)

@@ -2,6 +2,7 @@ import math
 from contextlib import ExitStack
 
 import concourse.mybir as mybir
+from concourse.masks import make_identity
 
 K, H, T, S, M = 1536, 1024, 2048, 1024, 512
 FLOPS = 2 * K * H * S + 2 * H * H * M
@@ -31,11 +32,21 @@ FIRST_ROW = P - PASSES1 * SCALE_ROWS
 TWO_PI = 2.0 * math.pi
 X_PARTS = 2
 X_COLS = M // X_PARTS
-W2_SLOTS = (("slot_b", "slot_w"), ("slot_r", "slot_a"))
-W2_PIECES = 2
-GPSIMD_SQUARES = ()
-TILES = PASSES2 * PACK
+W2_SLOTS = (("slot_a", "slot_a"), ("slot_r", "slot_r"))
+W2_PIECES = 4
+TILES = H // P
+CHUNKS = M // P
 OPEN_TILES = 2
+LAG = 2
+VECTOR_SQUARES = (1, 3, 5, 7)
+HELD = (4, 5, 6)
+H_BANKS = 3
+PHASE_BANKS = (3, 7)
+BACK_BANKS = (7, 4, 5, 6)
+Y_BANKS = (0, 1, 2, 3) + BACK_BANKS
+TURN_OFFSET = 98304.0
+TURN_BITS = 1203765248.0
+TURN_STEP = 128.0
 
 
 def tile_list_escapement_wear_match_kernel(
@@ -53,10 +64,9 @@ def tile_list_escapement_wear_match_kernel(
         pos2_sb = lists.tile([P, M // LIST_ROWS], U16, name="pos2_sb")
 
         tab_scale_window = keep.tile([P, T], U8, name="tab_scale_window", tag="slot_s", align_bytes=64)
-        w1_scale_raw = keep.tile([P, H], U8, name="w1_scale_raw", align_bytes=64)
+        scale_rows = keep.tile([P, S + H], U8, name="scale_rows", tag="slot_r", align_bytes=64)
         planes = [keep.tile([P, S + H], U8, name="planes%d" % a, align_bytes=64) for a in range(PASSES1)]
         nc.vector.memset(tab_scale_window[0:FIRST_ROW, :].bitcast(I32), 0)
-        nc.gpsimd.memset(w1_scale_raw[0:FIRST_ROW, :].bitcast(I32), 0)
         nc.vector.memset(planes[0][:].bitcast(I32), 0)
         for a in range(1, PASSES1):
             nc.gpsimd.memset(planes[a][:].bitcast(I32), 0)
@@ -64,13 +74,17 @@ def tile_list_escapement_wear_match_kernel(
         warm = keep.tile([P, 2], F32, name="warm")
         nc.gpsimd.memset(warm[:, 0:1], 0.0)
         nc.scalar.activation(warm[:, 1:2], warm[:, 0:1], ACT.Sin)
+        identity = keep.tile([P, P], F32, name="identity", align_bytes=64)
+        make_identity(nc, identity[:])
+        less_offset = keep.tile([P, P], F32, name="less_offset", align_bytes=64)
+        nc.gpsimd.memset(less_offset[:], -TURN_OFFSET)
 
         nc.sync.dma_start(offs_sb[:], offs)
-        for tile, scales in ((tab_scale_window, tab_scales), (w1_scale_raw, w1_scales)):
-            scale_rows = scales.rearrange("a q t -> (a q) t").bitcast(I32)
+        for room, scales in ((tab_scale_window[:], tab_scales), (scale_rows[:, S:], w1_scales)):
+            rows_in_hbm = scales.rearrange("a q t -> (a q) t").bitcast(I32)
             for rows in (slice(0, 2 * SCALE_ROWS), slice(2 * SCALE_ROWS, 3 * SCALE_ROWS)):
                 nc.sync.dma_start(
-                    out=tile[FIRST_ROW + rows.start : FIRST_ROW + rows.stop, :].bitcast(I32), in_=scale_rows[rows]
+                    out=room[FIRST_ROW + rows.start : FIRST_ROW + rows.stop, :].bitcast(I32), in_=rows_in_hbm[rows]
                 )
         tab_windows = {}
 
@@ -80,76 +94,61 @@ def tile_list_escapement_wear_match_kernel(
             tab_windows[a] = window
 
         load_table(0, "slot_a")
-        w1_raw = {}
+        w1_codes = {}
 
         def load_w1(b, tag):
-            w1_raw[b] = keep.tile([P, PASSES1, K_PASS // 2], I32, name="w1_raw%d" % b, tag=tag, align_bytes=64)
+            w1_codes[b] = keep.tile([P, PASSES1, K_PASS // 2], I32, name="w1_codes%d" % b, tag=tag, align_bytes=64)
             words = slice(b * K_PASS // 2, (b + 1) * K_PASS // 2)
-            nc.sync.dma_start(out=w1_raw[b][:], in_=w1_words.bitcast(I32).rearrange("a p w -> p a w")[:, :, words])
+            nc.sync.dma_start(out=w1_codes[b][:], in_=w1_words.bitcast(I32).rearrange("a p w -> p a w")[:, :, words])
 
-        load_w1(0, "slot_w")
         nc.sync.dma_start(pos1_sb[:], pos1)
         nc.sync.dma_start(pos2_sb[:], pos2)
         load_table(1, "slot_b")
+        load_w1(0, "slot_w")
 
         v_packed = keep.tile([P, S], U8, name="v_packed", tag="slot_g", align_bytes=64)
         nc.vector.tensor_copy(out=v_packed[:], in_=tab_scale_window[:].indirect(offs_sb[:]))
-        scale_rows = keep.tile([P, S + H], U8, name="scale_rows", tag="slot_r", align_bytes=64)
-        nc.gpsimd.tensor_copy(
-            out=scale_rows[:, S:].rearrange("p (b t c) -> p b t c", b=PASSES2, t=PACK),
-            in_=w1_scale_raw[:].rearrange("p (b c t) -> p b t c", b=PASSES2, t=PACK),
-        )
         nc.vector.tensor_copy(out=scale_rows[:, 0:S].bitcast(I32), in_=v_packed[:].bitcast(I32))
         for a in range(PASSES1):
-            for q in range(4):
-                first = FIRST_ROW + SCALE_ROWS * a + 4 * q
-                nc.sync.dma_start(out=planes[a][QUAD * q : QUAD * q + 4, :].bitcast(I32), in_=scale_rows[first : first + 4, :].bitcast(I32))
-                if (a, q) == (1, 0):
+            for r in range(4):
+                first = FIRST_ROW + SCALE_ROWS * a
+                nc.sync.dma_start(
+                    out=planes[a][r:P:QUAD, :].bitcast(I32),
+                    in_=scale_rows[first + r : first + SCALE_ROWS : 4, :].bitcast(I32),
+                )
+                if (a, r) == (1, 0):
                     load_table(2, "slot_g")
-
-        w1_codes = {}
-
-        def order_w1(pair):
-            b, half = divmod(pair, 2)
-            w1_codes[pair] = keep.tile([P, PASSES1, P], I32, name="w1_codes%d" % pair, align_bytes=64)
-            nc.vector.tensor_copy(
-                out=w1_codes[pair][:].bitcast(U16).rearrange("p a (e c) -> p e a c", e=2),
-                in_=w1_raw[b][:].bitcast(U16).rearrange("p a (c t) -> p t a c", t=PACK)[:, 2 * half : 2 * half + 2],
-            )
 
         v_codes = {}
         for a in range(PASSES1):
             for j in range(HALVES):
-                v_codes[a, j] = keep.tile([P, N], U32, name="v_codes%d%d" % (a, j), tag="v_codes%d%d" % (a, j), align_bytes=64)
+                v_codes[a, j] = keep.tile([P, N], U32, name="v_codes%d%d" % (a, j), align_bytes=64)
                 cols = slice(j * N // LIST_ROWS, (j + 1) * N // LIST_ROWS)
                 nc.vector.tensor_copy(
                     out=v_codes[a, j][:], in_=tab_windows[a][:].bitcast(U32).indirect(offs_sb[:, cols])
                 )
-            if a == 0:
-                order_w1(0)
-                load_w1(1, "slot_a")
-        for pair in range(1, PACK):
-            order_w1(pair)
 
         w2_raw = {}
-        for b in range(PASSES2):
-            for c in range(PASSES2):
-                w2_raw[b, c] = keep.tile([P, PACK, K_PASS], F32, name="w2_raw%d%d" % (b, c), tag=W2_SLOTS[b][c], align_bytes=64)
-                rows = w2[K_PASS * b : K_PASS * (b + 1), K_PASS * c : K_PASS * (c + 1)]
-                nc.sync.dma_start(out=w2_raw[b, c][:], in_=rows.rearrange("(p t) n -> p t n", t=PACK))
 
-        def load_by_row(vec, name, tag):
-            tile = keep.tile([P, PASSES2, PACK], F32, name=name, tag=tag, align_bytes=64)
-            nc.sync.dma_start(out=tile[:], in_=vec.rearrange("(b p t) -> p b t", p=P, t=PACK))
-            return tile
+        def load_w2(b, c):
+            w2_raw[b, c] = keep.tile([P, PACK, K_PASS], F32, name="w2_raw%d%d" % (b, c), tag=W2_SLOTS[b][c], align_bytes=64)
+            rows = w2[K_PASS * b : K_PASS * (b + 1), K_PASS * c : K_PASS * (c + 1)]
+            nc.sync.dma_start(out=w2_raw[b, c][:], in_=rows.rearrange("(p t) n -> p t n", t=PACK))
 
-        gain_sb = load_by_row(gain, "gain_sb", "slot_g")
+        load_w2(0, 0)
+        load_w2(1, 0)
+        w1_late = keep.tile([P, PASSES1, K_PASS // 2], I32, name="w1_late", tag="slot_b", align_bytes=64)
+        nc.sync.dma_start(out=w1_late[:], in_=w1_words.bitcast(I32).rearrange("a p w -> p a w")[:, :, K_PASS // 2 :])
+        w1_codes[1] = w1_late
+        gain_sb = keep.tile([P, PASSES2, PACK], F32, name="gain_sb", tag="slot_g", align_bytes=64)
+        nc.sync.dma_start(out=gain_sb[:], in_=gain.rearrange("(b p t) -> p b t", p=P, t=PACK))
 
-        def first_product(bank, b, t, j, a):
+        def first_product(bank, i, j, a):
+            b, t = divmod(i, PACK)
             nc.tensor.matmul_mx(
                 out=bank[:],
-                lhsT=w1_codes[2 * b + t // 2][:, a, t % 2 * P // 2 : (t % 2 + 1) * P // 2].bitcast(U8).bitcast(FP4X4),
-                lhsT_scale=planes[a][:, S + K_PASS * b + P * t : S + K_PASS * b + P * (t + 1)],
+                lhsT=w1_codes[b][:, a, t * P // 2 : (t + 1) * P // 2].bitcast(U8).bitcast(FP4X4),
+                lhsT_scale=planes[a][:, S + P * i : S + P * (i + 1)],
                 rhs=v_codes[a, j][:].bitcast(FP8X4),
                 rhs_scale=planes[a][:, j * N : (j + 1) * N],
                 start=(a == 0),
@@ -157,32 +156,38 @@ def tile_list_escapement_wear_match_kernel(
             )
 
         banks = {}
-        for t in range(OPEN_TILES):
+        for i in range(OPEN_TILES):
             for j in range(HALVES):
-                banks[t, j] = psum.tile([P, N], F32, name="bank%d" % (2 * t + j))
-                first_product(banks[t, j], 0, t, j, 0)
+                banks[i, j] = psum.tile([P, N], F32, name="bank%d" % (2 * i + j))
+        for a in range(PASSES1 - 1):
+            for i in range(OPEN_TILES):
+                for j in range(HALVES):
+                    first_product(banks[i, j], i, j, a)
         h_tiles = {}
-        for i in range(TILES):
-            b, t = divmod(i, PACK)
+
+        def make_h(i):
             h_tiles[i] = keep.tile([P, 2 * S], F32, name="h%d" % i, align_bytes=64)
             for j in range(HALVES):
                 if i >= OPEN_TILES:
-                    banks[i, j] = psum.tile([P, N], F32, name="bank%d" % (2 * (i % OPEN_TILES) + j))
-                for a in range(1 if i < OPEN_TILES else 0, PASSES1):
-                    first_product(banks[i, j], b, t, j, a)
+                    banks[i, j] = psum.tile([P, N], F32, name="bank%d" % ((2 * i + j - 2 * OPEN_TILES) % H_BANKS))
+                for a in range(PASSES1 - 1 if i < OPEN_TILES else 0, PASSES1):
+                    first_product(banks[i, j], i, j, a)
                 nc.scalar.copy(out=h_tiles[i][:, j * N : (j + 1) * N], in_=banks[i, j][:])
+
+        def spare(i):
+            return h_tiles[i][:, S : 2 * S]
 
         w2_codes = {}
         w2_planes = {}
 
         def weave_w2(b, c, room):
-            woven = room.bitcast(BF16).rearrange("p (u n t) -> p u n t", u=PACK, t=PACK)
+            woven = room.bitcast(BF16).rearrange("p (n i t) -> p n t i", i=PACK, t=PACK)
             width = P // W2_PIECES
             for piece in range(W2_PIECES):
                 cols = slice(piece * width, (piece + 1) * width)
                 nc.scalar.copy(
-                    out=woven[:, :, cols, :].rearrange("p u n t -> p n t u"),
-                    in_=w2_raw[b, c][:].rearrange("p t (n u) -> p n t u", u=PACK)[:, cols],
+                    out=woven[:, cols],
+                    in_=w2_raw[b, c][:].rearrange("p t (n i) -> p n t i", i=PACK)[:, cols],
                 )
             w2_codes[b, c] = keep.tile([P, K_PASS], U32, name="w2_codes%d%d" % (b, c), align_bytes=64)
             w2_planes[b, c] = keep.tile([P, K_PASS], U8, name="w2_plane%d%d" % (b, c), align_bytes=64)
@@ -192,126 +197,137 @@ def tile_list_escapement_wear_match_kernel(
                 in_=room.bitcast(BF16),
             )
 
-        def spare(i):
-            return h_tiles[i][:, S : 2 * S]
-
         turns = {}
         whole = {}
-        cosines = [keep.tile([P, 2, M, 2], F32, name="cosines%d" % b) for b in range(PASSES2)]
+        cosines = [keep.tile([P, CHUNKS, PACK, P], F32, name="cosines%d" % b, align_bytes=64) for b in range(PASSES2)]
 
         def pick_healthy(i):
-            pair, e = divmod(i, 2)
-            if e == 0:
-                turns[pair] = ring.tile([P, 2, M], F32, name="turns")
-            window = h_tiles[i][:].indirect(pos1_sb[:])
-            nc.vector.tensor_scalar(turns[pair][:, e, :], window, 1.0 / TWO_PI, 0.25, ALU.mult, ALU.add)
-            if e == 1:
-                whole[pair] = ring.tile([P, 2, M], I32, name="whole", align_bytes=64)
-                nc.gpsimd.tensor_scalar(whole[pair][:], turns[pair][:], 1.0, 0.0, ALU.mult, ALU.add)
+            turns[i] = ring.tile([P, M], F32, name="turns", bufs=4, align_bytes=64)
+            nc.vector.tensor_scalar(turns[i][:], h_tiles[i][:].indirect(pos1_sb[:]), 1.0 / TWO_PI, 0.25, ALU.mult, ALU.add)
+            whole[i] = ring.tile([P, M], I32, name="whole", bufs=4, align_bytes=64)
+            nc.gpsimd.tensor_scalar(whole[i][:], turns[i][:], -TURN_STEP, TURN_BITS, ALU.mult, ALU.add)
 
-        def cosine(pair):
-            phases = spare((2 * pair + 2) % TILES).rearrange("p (e m) -> p e m", e=2)
-            nc.vector.tensor_tensor(phases, whole[pair][:], turns[pair][:], ALU.subtract)
+        def cosine(i):
+            b, t = divmod(i, PACK)
+            phases = psum.tile([P, CHUNKS, P], F32, name="bank%d" % PHASE_BANKS[i % 2])
+            for q in range(CHUNKS):
+                cols = slice(P * q, P * (q + 1))
+                terms = (whole[i][:, cols].bitcast(F32), less_offset[:], turns[i][:, cols])
+                for n, term in enumerate(terms):
+                    nc.tensor.matmul(
+                        out=phases[:, q, :], lhsT=term, rhs=identity[:], is_transpose=True,
+                        start=(n == 0), stop=(n == len(terms) - 1),
+                    )
             nc.scalar.activation(
-                cosines[pair // 2][:, pair % 2].rearrange("p (c i) e -> p c e i", i=PACK),
-                phases.rearrange("p e (c i) -> p c e i", i=PACK),
+                cosines[b][:, :, :, QUAD * t : QUAD * (t + 1)],
+                phases[:].rearrange("p q (s t) -> p q t s", t=PACK),
                 ACT.Sin,
-                scale=-TWO_PI,
+                scale=TWO_PI,
             )
 
         x_codes = {}
         x_planes = {}
+        x_woven = {}
 
-        def weigh(engine, b, cols, woven):
-            width = cols.stop - cols.start
-            engine.tensor_tensor(
-                woven.rearrange("p (m h e) -> p m h e", h=2, e=2),
-                cosines[b][:, :, cols].rearrange("p h m e -> p m h e"),
-                gain_sb[:, b, :].rearrange("p (h e) -> p h e", e=2).unsqueeze(1).to_broadcast([P, width, 2, 2]),
-                ALU.mult,
-            )
-
-        def quantize_x(b, cols, woven):
-            nc.vector.quantize_mx(out=x_codes[b][:, cols].bitcast(FP8X4), scales=x_planes[b][:, cols], in_=woven)
-
-        for b in range(PASSES2):
+        def make_x(b, bank_names):
             x_codes[b] = keep.tile([P, M], U32, name="x_codes%d" % b, align_bytes=64)
             x_planes[b] = keep.tile([P, M], U8, name="x_plane%d" % b, align_bytes=64)
+            x_woven[b] = keep.tile([P, M, PACK], BF16, name="x_woven%d" % b, align_bytes=64)
+            for q in range(CHUNKS):
+                back = psum.tile([P, PACK, P], F32, name="bank%d" % bank_names[q])
+                for t in range(PACK):
+                    nc.tensor.transpose(back[:, t, :], cosines[b][:, q, t, :], identity[:])
+                nc.vector.tensor_tensor(
+                    x_woven[b][:, P * q : P * (q + 1), :],
+                    back[:].rearrange("p t m -> p m t"),
+                    gain_sb[:, b, :].unsqueeze(1).to_broadcast([P, P, PACK]),
+                    ALU.mult,
+                )
+            for half in range(X_PARTS):
+                cols = slice(X_COLS * half, X_COLS * (half + 1))
+                nc.vector.quantize_mx(
+                    out=x_codes[b][:, cols].bitcast(FP8X4),
+                    scales=x_planes[b][:, cols],
+                    in_=x_woven[b][:, cols, :].rearrange("p m t -> p (m t)"),
+                )
 
         suspects = {}
 
-        def pick_suspects(i, spot, columns):
+        def pick_suspects(i, spot):
             suspects[i] = spot
-            nc.vector.tensor_copy(out=spot, in_=h_tiles[i][:, 0:columns].indirect(pos2_sb[:]))
+            nc.vector.tensor_copy(out=spot, in_=h_tiles[i][:, 0:S].indirect(pos2_sb[:]))
 
-        def weigh_first_pass(half):
-            room = whole[2 + half][:, 0, :].bitcast(BF16)
-            for piece in range(2):
-                first = X_COLS * half + piece * X_COLS // 2
-                cols = slice(first, first + X_COLS // 2)
-                weigh(nc.vector, 0, cols, room[:, piece * M : (piece + 1) * M])
-            return room
-
-        pick_healthy(0)
-        pick_healthy(1)
-        for pair in range(PACK):
-            if pair < PACK - 1:
-                pick_healthy(2 * pair + 2)
-            else:
-                pick_suspects(0, spare(TILES - 1)[:, 0:M], 2 * S)
-                pick_suspects(1, spare(TILES - 1)[:, M : 2 * M], S)
-            cosine(pair)
-            if pair < PACK - 1:
-                pick_healthy(2 * pair + 3)
-            if pair in (1, 2):
-                room = ring.tile([P, 2 * M], F32, name="w2_woven", align_bytes=64)
-                weave_w2(pair - 1, 0, room[:])
-        halves = [slice(X_COLS * half, X_COLS * (half + 1)) for half in range(X_PARTS)]
-        first_woven = [weigh_first_pass(half) for half in range(X_PARTS)]
-        for e in range(2):
-            pick_suspects(2 + e, turns[PACK - 1][:, e, :], S)
-        x_woven = keep.tile([P, X_PARTS, X_COLS * PACK], BF16, name="x_woven", align_bytes=64)
-        for half in range(X_PARTS):
-            weigh(nc.vector, 1, halves[half], x_woven[:, half, :])
-            quantize_x(0, halves[half], first_woven[half])
-        for half in range(X_PARTS):
-            quantize_x(1, halves[half], x_woven[:, half, :])
-        pick_suspects(4, x_woven[:, 1, :].bitcast(F32), S)
-        weave_w2(0, 1, spare(0))
-        weave_w2(1, 1, spare(TILES - 2))
-        nc.scalar.activation(warm[:, 1:2], cosines[1][:, 1, 0, 0:1], ACT.Exp)
-        nw_sb = load_by_row(nw, "nw_sb", "slot_a")
         y_banks = {}
-        for i in range(TILES):
+
+        def second_product(i, b):
             c, u = divmod(i, PACK)
-            y_banks[i] = psum.tile([P, M], F32, name="bank%d" % i)
-            for b in range(PASSES2):
-                nc.tensor.matmul_mx(
-                    out=y_banks[i][:],
-                    lhsT=w2_codes[b, c][:, P * u : P * (u + 1)].bitcast(FP8X4),
-                    lhsT_scale=w2_planes[b, c][:, P * u : P * (u + 1)],
-                    rhs=x_codes[b][:].bitcast(FP8X4),
-                    rhs_scale=x_planes[b][:],
-                    start=(b == 0),
-                    stop=(b == PASSES2 - 1),
-                )
-        out_rows = out.rearrange("(c p u) m -> c u p m", p=P, u=PACK)
+            if b == 0:
+                y_banks[i] = psum.tile([P, M], F32, name="bank%d" % Y_BANKS[i])
+            nc.tensor.matmul_mx(
+                out=y_banks[i][:],
+                lhsT=w2_codes[b, c][:, P * u : P * (u + 1)].bitcast(FP8X4),
+                lhsT_scale=w2_planes[b, c][:, P * u : P * (u + 1)],
+                rhs=x_codes[b][:].bitcast(FP8X4),
+                rhs_scale=x_planes[b][:],
+                start=(b == 0),
+                stop=(b == PASSES2 - 1),
+            )
+
+        picked = keep.tile([P, TILES - len(HELD), M], F32, name="picked", align_bytes=64)
+        free_picks = [i for i in range(TILES) if i not in HELD]
+        for step in range(TILES + 1):
+            if step < TILES:
+                make_h(step)
+            if step >= 1:
+                pick_healthy(step - 1)
+                if step == TILES:
+                    for e, i in enumerate(HELD[1:]):
+                        pick_suspects(i, spare(TILES - 1)[:, e * M : (e + 1) * M])
+                if step - 1 in free_picks:
+                    pick_suspects(step - 1, picked[:, free_picks.index(step - 1), :])
+            if step == PACK + LAG:
+                make_x(0, BACK_BANKS)
+            if step in (LAG + 1, LAG + 2):
+                cosine(step - LAG - 1)
+            if LAG + 2 <= step < PACK + LAG:
+                cosine(step - LAG)
+            if step == TILES - 1:
+                cosine(PACK)
+                cosine(PACK + 1)
+            if step == TILES - 1:
+                for b in range(PASSES2):
+                    room = ring.tile([P, 2 * M], F32, name="w2_woven", align_bytes=64)
+                    weave_w2(b, 0, room[:])
+                    load_w2(b, 1)
+        pick_suspects(HELD[0], turns[PACK + 1][:])
+        second_product(0, 0)
+        second_product(1, 0)
+        cosine(TILES - 2)
+        second_product(2, 0)
+        cosine(TILES - 1)
+        second_product(3, 0)
+        make_x(1, BACK_BANKS)
+        for b in range(PASSES2):
+            room = ring.tile([P, 2 * M], F32, name="w2_woven", align_bytes=64)
+            weave_w2(b, 1, room[:])
+        nc.scalar.activation(warm[:, 1:2], cosines[1][:, 0, 0, P - 1 : P], ACT.Exp)
+        nw_sb = keep.tile([P, TILES], F32, name="nw_sb", tag="slot_w", align_bytes=64)
+        with nc.allow_non_contiguous_dma(reason="one value of nw to a partition and row tile"):
+            nc.sync.dma_start(out=nw_sb[:], in_=nw.rearrange("(i p) -> p i", p=P))
         for i in range(TILES):
-            c, u = divmod(i, PACK)
+            for b in range(1 if i < PACK else 0, PASSES2):
+                second_product(i, b)
+        for i in range(TILES):
             width = M // 2 if i == TILES - 1 else M
             for first in range(0, M, width):
                 cols = slice(first, first + width)
                 diff = ring.tile([P, width], F32, name="diff", bufs=4)
                 nc.vector.tensor_tensor(diff[:], y_banks[i][:, cols], suspects[i][:, cols], ALU.subtract)
                 square = ring.tile([P, width], F32, name="square", bufs=3)
-                if i in GPSIMD_SQUARES:
-                    nc.gpsimd.tensor_tensor(square[:], diff[:], diff[:], ALU.mult)
-                elif i == TILES - 1 and True:
+                if i in VECTOR_SQUARES:
                     nc.vector.tensor_tensor(square[:], diff[:], diff[:], ALU.mult)
                 else:
                     nc.scalar.activation(square[:], diff[:], ACT.Square)
                 score = ring.tile([P, width], F32, name="score", bufs=4)
-                nc.scalar.activation(score[:], square[:], ACT.Exp, scale=nw_sb[:, c, u : u + 1])
-                nc.sync.dma_start(out=out_rows[c, u][:, cols], in_=score[:])
-            if 2 <= i < TILES - 3:
-                pick_suspects(i + 3, suspects[i], S)
+                nc.scalar.activation(score[:], square[:], ACT.Exp, scale=nw_sb[:, i : i + 1])
+                nc.sync.dma_start(out=out[P * i : P * (i + 1), cols], in_=score[:])

@@ -219,8 +219,8 @@ def tile_list_escapement_wear_match_kernel(
                         start=(n == 0), stop=(n == len(terms) - 1),
                     )
             nc.scalar.activation(
-                cosines[b][:, :, :, QUAD * t : QUAD * (t + 1)],
-                phases[:].rearrange("p q (s t) -> p q t s", t=PACK),
+                cosines[b][:, :, :, QUAD * t : QUAD * (t + 1)].rearrange("p q t s -> p q s t"),
+                phases[:].rearrange("p q (s t) -> p q s t", t=PACK),
                 ACT.Sin,
                 scale=TWO_PI,
             )
@@ -238,9 +238,9 @@ def tile_list_escapement_wear_match_kernel(
                 for t in range(PACK):
                     nc.tensor.transpose(back[:, t, :], cosines[b][:, q, t, :], identity[:])
                 nc.vector.tensor_tensor(
-                    x_woven[b][:, P * q : P * (q + 1), :],
-                    back[:].rearrange("p t m -> p m t"),
-                    gain_sb[:, b, :].unsqueeze(1).to_broadcast([P, P, PACK]),
+                    x_woven[b][:, P * q : P * (q + 1), :].rearrange("p (m e) t -> p m t e", e=2),
+                    back[:].rearrange("p t (m e) -> p m t e", e=2),
+                    gain_sb[:, b, :].unsqueeze(1).unsqueeze(3).to_broadcast([P, P // 2, PACK, 2]),
                     ALU.mult,
                 )
             for half in range(X_PARTS):

@@ -32,14 +32,12 @@ FIRST_ROW = P - PASSES1 * SCALE_ROWS
 TWO_PI = 2.0 * math.pi
 X_PARTS = 2
 X_COLS = M // X_PARTS
-W2_SLOTS = (("slot_a", "slot_a"), ("slot_r", "slot_r"))
+W2_SLOTS = (("slot_b", "slot_b"), ("slot_r", "slot_r"))
 W2_PIECES = 4
 TILES = H // P
 CHUNKS = M // P
 OPEN_TILES = 2
-LAG = 2
-VECTOR_SQUARES = (1, 3, 5, 7)
-HELD = (4, 5, 6)
+VECTOR_SQUARES = (7,)
 H_BANKS = 3
 PHASE_BANKS = (3, 7)
 BACK_BANKS = (7, 4, 5, 6)
@@ -67,6 +65,8 @@ def tile_list_escapement_wear_match_kernel(
         scale_rows = keep.tile([P, S + H], U8, name="scale_rows", tag="slot_r", align_bytes=64)
         planes = [keep.tile([P, S + H], U8, name="planes%d" % a, align_bytes=64) for a in range(PASSES1)]
         nc.vector.memset(tab_scale_window[0:FIRST_ROW, :].bitcast(I32), 0)
+        late_scale_raw = keep.tile([P, K_PASS], U8, name="late_scale_raw", align_bytes=64)
+        nc.gpsimd.memset(late_scale_raw[0:FIRST_ROW, :].bitcast(I32), 0)
         nc.vector.memset(planes[0][:].bitcast(I32), 0)
         for a in range(1, PASSES1):
             nc.gpsimd.memset(planes[a][:].bitcast(I32), 0)
@@ -80,7 +80,12 @@ def tile_list_escapement_wear_match_kernel(
         nc.gpsimd.memset(less_offset[:], -TURN_OFFSET)
 
         nc.sync.dma_start(offs_sb[:], offs)
-        for room, scales in ((tab_scale_window[:], tab_scales), (scale_rows[:, S:], w1_scales)):
+        scale_loads = (
+            (tab_scale_window[:], tab_scales),
+            (late_scale_raw[:], w1_scales[:, :, K_PASS:]),
+            (scale_rows[:, S : S + K_PASS], w1_scales[:, :, 0:K_PASS]),
+        )
+        for room, scales in scale_loads:
             rows_in_hbm = scales.rearrange("a q t -> (a q) t").bitcast(I32)
             for rows in (slice(0, 2 * SCALE_ROWS), slice(2 * SCALE_ROWS, 3 * SCALE_ROWS)):
                 nc.sync.dma_start(
@@ -108,15 +113,19 @@ def tile_list_escapement_wear_match_kernel(
 
         v_packed = keep.tile([P, S], U8, name="v_packed", tag="slot_g", align_bytes=64)
         nc.vector.tensor_copy(out=v_packed[:], in_=tab_scale_window[:].indirect(offs_sb[:]))
+        nc.gpsimd.tensor_copy(
+            out=scale_rows[:, S + K_PASS :].rearrange("p (t c) -> p t c", t=PACK),
+            in_=late_scale_raw[:].rearrange("p (c t) -> p t c", t=PACK),
+        )
         nc.vector.tensor_copy(out=scale_rows[:, 0:S].bitcast(I32), in_=v_packed[:].bitcast(I32))
         for a in range(PASSES1):
-            for r in range(4):
-                first = FIRST_ROW + SCALE_ROWS * a
+            for q in range(4):
+                first = FIRST_ROW + SCALE_ROWS * a + 4 * q
                 nc.sync.dma_start(
-                    out=planes[a][r:P:QUAD, :].bitcast(I32),
-                    in_=scale_rows[first + r : first + SCALE_ROWS : 4, :].bitcast(I32),
+                    out=planes[a][QUAD * q : QUAD * q + 4, :].bitcast(I32),
+                    in_=scale_rows[first : first + 4, :].bitcast(I32),
                 )
-                if (a, r) == (1, 0):
+                if (a, q) == (1, 0):
                     load_table(2, "slot_g")
 
         v_codes = {}
@@ -135,11 +144,16 @@ def tile_list_escapement_wear_match_kernel(
             rows = w2[K_PASS * b : K_PASS * (b + 1), K_PASS * c : K_PASS * (c + 1)]
             nc.sync.dma_start(out=w2_raw[b, c][:], in_=rows.rearrange("(p t) n -> p t n", t=PACK))
 
+        w1_late = keep.tile([P, PASSES1, K_PASS // 2], I32, name="w1_late", tag="slot_a", align_bytes=64)
+        nc.sync.dma_start(out=w1_late[:], in_=w1_words.bitcast(I32).rearrange("a p w -> p a w")[:, :, K_PASS // 2 :])
+        w1_codes[1] = keep.tile([P, PASSES1, K_PASS // 2], I32, name="w1_codes1", align_bytes=64)
+        for half in range(2):
+            nc.vector.tensor_copy(
+                out=w1_codes[1][:].bitcast(U16).rearrange("p a (t c) -> p t a c", t=PACK)[:, 2 * half : 2 * half + 2],
+                in_=w1_late[:].bitcast(U16).rearrange("p a (c t) -> p t a c", t=PACK)[:, 2 * half : 2 * half + 2],
+            )
         load_w2(0, 0)
         load_w2(1, 0)
-        w1_late = keep.tile([P, PASSES1, K_PASS // 2], I32, name="w1_late", tag="slot_b", align_bytes=64)
-        nc.sync.dma_start(out=w1_late[:], in_=w1_words.bitcast(I32).rearrange("a p w -> p a w")[:, :, K_PASS // 2 :])
-        w1_codes[1] = w1_late
         gain_sb = keep.tile([P, PASSES2, PACK], F32, name="gain_sb", tag="slot_g", align_bytes=64)
         nc.sync.dma_start(out=gain_sb[:], in_=gain.rearrange("(b p t) -> p b t", p=P, t=PACK))
 
@@ -181,7 +195,8 @@ def tile_list_escapement_wear_match_kernel(
         w2_planes = {}
 
         def weave_w2(b, c, room):
-            woven = room.bitcast(BF16).rearrange("p (n i t) -> p n t i", i=PACK, t=PACK)
+            order = "p (n i t) -> p n t i" if c == 0 else "p (i n t) -> p n t i"
+            woven = room.bitcast(BF16).rearrange(order, i=PACK, t=PACK)
             width = P // W2_PIECES
             for piece in range(W2_PIECES):
                 cols = slice(piece * width, (piece + 1) * width)
@@ -199,16 +214,41 @@ def tile_list_escapement_wear_match_kernel(
 
         turns = {}
         whole = {}
-        cosines = [keep.tile([P, CHUNKS, PACK, P], F32, name="cosines%d" % b, align_bytes=64) for b in range(PASSES2)]
+        cosines = keep.tile([P, CHUNKS, PACK, P], F32, name="cosines", align_bytes=64)
+        late_cosines = keep.tile([P, 2, M, 2], F32, name="late_cosines", align_bytes=64)
 
-        def pick_healthy(i):
-            turns[i] = ring.tile([P, M], F32, name="turns", bufs=4, align_bytes=64)
-            nc.vector.tensor_scalar(turns[i][:], h_tiles[i][:].indirect(pos1_sb[:]), 1.0 / TWO_PI, 0.25, ALU.mult, ALU.add)
-            whole[i] = ring.tile([P, M], I32, name="whole", bufs=4, align_bytes=64)
+        def pick_healthy(i, spot):
+            nc.vector.tensor_scalar(spot, h_tiles[i][:].indirect(pos1_sb[:]), 1.0 / TWO_PI, 0.25, ALU.mult, ALU.add)
+
+        def pick_early(i):
+            turns[i] = keep.tile([P, M], F32, name="turns%d" % i, align_bytes=64)
+            pick_healthy(i, turns[i][:])
+            whole[i] = ring.tile([P, M], I32, name="whole", bufs=3, align_bytes=64)
             nc.gpsimd.tensor_scalar(whole[i][:], turns[i][:], -TURN_STEP, TURN_BITS, ALU.mult, ALU.add)
 
+        late_turns = {}
+        late_whole = {}
+
+        def pick_late(i):
+            pair, e = divmod(i - PACK, 2)
+            if e == 0:
+                late_turns[pair] = keep.tile([P, 2, M], F32, name="late_turns%d" % pair, align_bytes=64)
+            pick_healthy(i, late_turns[pair][:, e, :])
+            if e == 1:
+                late_whole[pair] = keep.tile([P, 2, M], I32, name="late_whole%d" % pair, align_bytes=64)
+                nc.gpsimd.tensor_scalar(late_whole[pair][:], late_turns[pair][:], 1.0, 0.0, ALU.mult, ALU.add)
+
+        def late_cosine(pair, room):
+            phases = room.rearrange("p (e m) -> p e m", e=2)
+            nc.vector.tensor_tensor(phases, late_whole[pair][:], late_turns[pair][:], ALU.subtract)
+            nc.scalar.activation(
+                late_cosines[:, pair].rearrange("p (c i) e -> p c e i", i=PACK),
+                phases.rearrange("p e (c i) -> p c e i", i=PACK),
+                ACT.Sin,
+                scale=-TWO_PI,
+            )
+
         def cosine(i):
-            b, t = divmod(i, PACK)
             phases = psum.tile([P, CHUNKS, P], F32, name="bank%d" % PHASE_BANKS[i % 2])
             for q in range(CHUNKS):
                 cols = slice(P * q, P * (q + 1))
@@ -219,43 +259,46 @@ def tile_list_escapement_wear_match_kernel(
                         start=(n == 0), stop=(n == len(terms) - 1),
                     )
             nc.scalar.activation(
-                cosines[b][:, :, :, QUAD * t : QUAD * (t + 1)].rearrange("p q t s -> p q s t"),
+                cosines[:, :, :, QUAD * i : QUAD * (i + 1)].rearrange("p q t s -> p q s t"),
                 phases[:].rearrange("p q (s t) -> p q s t", t=PACK),
                 ACT.Sin,
                 scale=TWO_PI,
             )
 
-        x_codes = {}
-        x_planes = {}
-        x_woven = {}
+        x_codes = [keep.tile([P, M], U32, name="x_codes%d" % b, align_bytes=64) for b in range(PASSES2)]
+        x_planes = [keep.tile([P, M], U8, name="x_plane%d" % b, align_bytes=64) for b in range(PASSES2)]
+        halves = [slice(X_COLS * half, X_COLS * (half + 1)) for half in range(X_PARTS)]
+        back = {}
 
-        def make_x(b, bank_names):
-            x_codes[b] = keep.tile([P, M], U32, name="x_codes%d" % b, align_bytes=64)
-            x_planes[b] = keep.tile([P, M], U8, name="x_plane%d" % b, align_bytes=64)
-            x_woven[b] = keep.tile([P, M, PACK], BF16, name="x_woven%d" % b, align_bytes=64)
-            for q in range(CHUNKS):
-                back = psum.tile([P, PACK, P], F32, name="bank%d" % bank_names[q])
-                for t in range(PACK):
-                    nc.tensor.transpose(back[:, t, :], cosines[b][:, q, t, :], identity[:])
-                nc.vector.tensor_tensor(
-                    x_woven[b][:, P * q : P * (q + 1), :].rearrange("p (m e) t -> p m t e", e=2),
-                    back[:].rearrange("p t (m e) -> p m t e", e=2),
-                    gain_sb[:, b, :].unsqueeze(1).unsqueeze(3).to_broadcast([P, P // 2, PACK, 2]),
-                    ALU.mult,
-                )
-            for half in range(X_PARTS):
-                cols = slice(X_COLS * half, X_COLS * (half + 1))
-                nc.vector.quantize_mx(
-                    out=x_codes[b][:, cols].bitcast(FP8X4),
-                    scales=x_planes[b][:, cols],
-                    in_=x_woven[b][:, cols, :].rearrange("p m t -> p (m t)"),
-                )
+        def turn_back(q):
+            back[q] = psum.tile([P, PACK, P], F32, name="bank%d" % BACK_BANKS[q])
+            for t in range(PACK):
+                nc.tensor.transpose(back[q][:, t, :], cosines[:, q, t, :], identity[:])
+
+        def weigh_early(q, woven):
+            nc.vector.tensor_tensor(
+                woven.rearrange("p (m e t) -> p m t e", e=2, t=PACK),
+                back[q][:].rearrange("p t (m e) -> p m t e", e=2),
+                gain_sb[:, 0, :].unsqueeze(1).unsqueeze(3).to_broadcast([P, P // 2, PACK, 2]),
+                ALU.mult,
+            )
+
+        def weigh_late(cols, woven):
+            nc.vector.tensor_tensor(
+                woven.rearrange("p (m h e) -> p m h e", h=2, e=2),
+                late_cosines[:, :, cols].rearrange("p h m e -> p m h e"),
+                gain_sb[:, 1, :].rearrange("p (h e) -> p h e", e=2).unsqueeze(1).to_broadcast([P, X_COLS, 2, 2]),
+                ALU.mult,
+            )
+
+        def quantize_x(b, cols, woven):
+            nc.vector.quantize_mx(out=x_codes[b][:, cols].bitcast(FP8X4), scales=x_planes[b][:, cols], in_=woven)
 
         suspects = {}
 
-        def pick_suspects(i, spot):
+        def pick_suspects(i, spot, columns):
             suspects[i] = spot
-            nc.vector.tensor_copy(out=spot, in_=h_tiles[i][:, 0:S].indirect(pos2_sb[:]))
+            nc.vector.tensor_copy(out=spot, in_=h_tiles[i][:, 0:columns].indirect(pos2_sb[:]))
 
         y_banks = {}
 
@@ -273,52 +316,52 @@ def tile_list_escapement_wear_match_kernel(
                 stop=(b == PASSES2 - 1),
             )
 
-        picked = keep.tile([P, TILES - len(HELD), M], F32, name="picked", align_bytes=64)
-        free_picks = [i for i in range(TILES) if i not in HELD]
-        for step in range(TILES + 1):
-            if step < TILES:
-                make_h(step)
-            if step >= 1:
-                pick_healthy(step - 1)
-                if step == TILES:
-                    for e, i in enumerate(HELD[1:]):
-                        pick_suspects(i, spare(TILES - 1)[:, e * M : (e + 1) * M])
-                if step - 1 in free_picks:
-                    pick_suspects(step - 1, picked[:, free_picks.index(step - 1), :])
-            if step == PACK + LAG:
-                make_x(0, BACK_BANKS)
-            if step in (LAG + 1, LAG + 2):
-                cosine(step - LAG - 1)
-            if LAG + 2 <= step < PACK + LAG:
-                cosine(step - LAG)
-            if step == TILES - 1:
-                cosine(PACK)
-                cosine(PACK + 1)
-            if step == TILES - 1:
-                for b in range(PASSES2):
-                    room = ring.tile([P, 2 * M], F32, name="w2_woven", align_bytes=64)
-                    weave_w2(b, 0, room[:])
-                    load_w2(b, 1)
-        pick_suspects(HELD[0], turns[PACK + 1][:])
-        second_product(0, 0)
-        second_product(1, 0)
-        cosine(TILES - 2)
-        second_product(2, 0)
-        cosine(TILES - 1)
-        second_product(3, 0)
-        make_x(1, BACK_BANKS)
+        picked = keep.tile([P, PACK, M], F32, name="picked", align_bytes=64)
+        for i in range(TILES):
+            make_h(i)
+            if i < PACK:
+                pick_early(i)
+                pick_suspects(i, picked[:, i, :], S)
+            else:
+                pick_late(i)
+            if PACK - 1 <= i < TILES - 2:
+                cosine(i - PACK + 1)
+        cosine(PACK - 1)
+        for q in range(CHUNKS):
+            turn_back(q)
+        late_cosine(0, spare(6))
+        pick_suspects(4, spare(7)[:, 0:M], 2 * S)
+        late_cosine(1, spare(4))
         for b in range(PASSES2):
             room = ring.tile([P, 2 * M], F32, name="w2_woven", align_bytes=64)
-            weave_w2(b, 1, room[:])
-        nc.scalar.activation(warm[:, 1:2], cosines[1][:, 0, 0, P - 1 : P], ACT.Exp)
-        nw_sb = keep.tile([P, TILES], F32, name="nw_sb", tag="slot_w", align_bytes=64)
+            weave_w2(b, 0, room[:])
+            load_w2(b, 1)
+        early_woven = late_whole[1][:].rearrange("p e m -> p (e m)").bitcast(BF16)
+        for q in range(CHUNKS):
+            weigh_early(q, early_woven[:, M * q : M * (q + 1)])
+        x_woven = keep.tile([P, X_PARTS, X_COLS * PACK], BF16, name="x_woven", align_bytes=64)
+        for half in range(X_PARTS):
+            weigh_late(halves[half], x_woven[:, half, :])
+            quantize_x(0, halves[half], early_woven[:, 2 * M * half : 2 * M * (half + 1)])
+        for half in range(X_PARTS):
+            quantize_x(1, halves[half], x_woven[:, half, :])
+        pick_suspects(5, x_woven[:, 1, :].bitcast(F32), S)
+        weave_w2(0, 1, spare(4))
+        weave_w2(1, 1, spare(6))
+        nc.scalar.activation(warm[:, 1:2], late_cosines[:, 1, 0, 0:1], ACT.Exp)
+        nw_sb = keep.tile([P, PACK], F32, name="nw_sb", tag="slot_w", align_bytes=64)
         with nc.allow_non_contiguous_dma(reason="one value of nw to a partition and row tile"):
-            nc.sync.dma_start(out=nw_sb[:], in_=nw.rearrange("(i p) -> p i", p=P))
+            nc.sync.dma_start(out=nw_sb[:, 0:PACK], in_=nw[0:K_PASS].rearrange("(i p) -> p i", p=P))
+        late_nw = keep.tile([P, PACK], F32, name="late_nw", tag="slot_a", align_bytes=64)
+        nc.sync.dma_start(out=late_nw[:], in_=nw[K_PASS:].rearrange("(p t) -> p t", t=PACK))
         for i in range(TILES):
-            for b in range(1 if i < PACK else 0, PASSES2):
+            for b in range(PASSES2):
                 second_product(i, b)
+        late_rows = out[K_PASS:].rearrange("(p u) m -> u p m", u=PACK)
         for i in range(TILES):
             width = M // 2 if i == TILES - 1 else M
+            rows = out[P * i : P * (i + 1)] if i < PACK else late_rows[i - PACK]
+            sharpness = nw_sb[:, i : i + 1] if i < PACK else late_nw[:, i - PACK : i - PACK + 1]
             for first in range(0, M, width):
                 cols = slice(first, first + width)
                 diff = ring.tile([P, width], F32, name="diff", bufs=4)
@@ -328,6 +371,8 @@ def tile_list_escapement_wear_match_kernel(
                     nc.vector.tensor_tensor(square[:], diff[:], diff[:], ALU.mult)
                 else:
                     nc.scalar.activation(square[:], diff[:], ACT.Square)
-                score = ring.tile([P, width], F32, name="score", bufs=4)
-                nc.scalar.activation(score[:], square[:], ACT.Exp, scale=nw_sb[:, i : i + 1])
-                nc.sync.dma_start(out=out[P * i : P * (i + 1), cols], in_=score[:])
+                score = ring.tile([P, width], F32, name="score", bufs=6)
+                nc.scalar.activation(score[:], square[:], ACT.Exp, scale=sharpness)
+                nc.sync.dma_start(out=rows[:, cols], in_=score[:])
+            if 2 <= i < 4:
+                pick_suspects(i + PACK, suspects[i], S)

@@ -32,12 +32,14 @@ FIRST_ROW = P - PASSES1 * SCALE_ROWS
 TWO_PI = 2.0 * math.pi
 X_PARTS = 2
 X_COLS = M // X_PARTS
-W2_SLOTS = (("slot_b", "slot_b"), ("slot_r", "slot_r"))
-W2_PIECES = 4
+W2_SLOTS = (("slot_b", "slot_r"), ("slot_g", "slot_a"))
+EARLY_PIECE = 256
+LATE_PIECE = 32
 TILES = H // P
 CHUNKS = M // P
-OPEN_TILES = 2
+OPEN_TILES = 3
 VECTOR_SQUARES = (7,)
+COSINE_BEHIND = ((4, 1), (5, 1), (6, 0), (6, 1))
 H_BANKS = 3
 PHASE_BANKS = (3, 7)
 BACK_BANKS = (7, 4, 5, 6)
@@ -146,16 +148,15 @@ def tile_list_escapement_wear_match_kernel(
 
         w1_late = keep.tile([P, PASSES1, K_PASS // 2], I32, name="w1_late", tag="slot_a", align_bytes=64)
         nc.sync.dma_start(out=w1_late[:], in_=w1_words.bitcast(I32).rearrange("a p w -> p a w")[:, :, K_PASS // 2 :])
-        w1_codes[1] = keep.tile([P, PASSES1, K_PASS // 2], I32, name="w1_codes1", align_bytes=64)
+        w1_codes[1] = keep.tile([P, PASSES1, K_PASS // 2], I32, name="w1_codes1", tag="w1_codes1", align_bytes=64)
         for half in range(2):
             nc.vector.tensor_copy(
                 out=w1_codes[1][:].bitcast(U16).rearrange("p a (t c) -> p t a c", t=PACK)[:, 2 * half : 2 * half + 2],
                 in_=w1_late[:].bitcast(U16).rearrange("p a (c t) -> p t a c", t=PACK)[:, 2 * half : 2 * half + 2],
             )
-        load_w2(0, 0)
-        load_w2(1, 0)
-        gain_sb = keep.tile([P, PASSES2, PACK], F32, name="gain_sb", tag="slot_g", align_bytes=64)
-        nc.sync.dma_start(out=gain_sb[:], in_=gain.rearrange("(b p t) -> p b t", p=P, t=PACK))
+        for c in range(PASSES2):
+            for b in range(PASSES2):
+                load_w2(b, c)
 
         def first_product(bank, i, j, a):
             b, t = divmod(i, PACK)
@@ -187,6 +188,8 @@ def tile_list_escapement_wear_match_kernel(
                 for a in range(PASSES1 - 1 if i < OPEN_TILES else 0, PASSES1):
                     first_product(banks[i, j], i, j, a)
                 nc.scalar.copy(out=h_tiles[i][:, j * N : (j + 1) * N], in_=banks[i, j][:])
+                if (i, j) in COSINE_BEHIND:
+                    cosine(COSINE_BEHIND.index((i, j)))
 
         def spare(i):
             return h_tiles[i][:, S : 2 * S]
@@ -194,17 +197,25 @@ def tile_list_escapement_wear_match_kernel(
         w2_codes = {}
         w2_planes = {}
 
-        def weave_w2(b, c, room):
-            order = "p (n i t) -> p n t i" if c == 0 else "p (i n t) -> p n t i"
-            woven = room.bitcast(BF16).rearrange(order, i=PACK, t=PACK)
-            width = P // W2_PIECES
-            for piece in range(W2_PIECES):
-                cols = slice(piece * width, (piece + 1) * width)
-                nc.scalar.copy(
-                    out=woven[:, cols],
-                    in_=w2_raw[b, c][:].rearrange("p t (n i) -> p n t i", i=PACK)[:, cols],
-                )
-            w2_codes[b, c] = keep.tile([P, K_PASS], U32, name="w2_codes%d%d" % (b, c), align_bytes=64)
+        early_rooms = [keep.tile([P, 2 * M], F32, name="w2_woven%d" % b, align_bytes=64) for b in range(PASSES2)]
+
+        def weave_early(piece):
+            b, half = divmod(piece, 2)
+            cols = slice(half * EARLY_PIECE, (half + 1) * EARLY_PIECE)
+            woven = early_rooms[b][:].bitcast(BF16).rearrange("p (n t) -> p n t", t=PACK)
+            rows = w2_raw[b, 0][:].rearrange("p t n -> p n t")
+            nc.gpsimd.tensor_scalar(woven[:, cols], rows[:, cols], 1.0, 0.0, ALU.mult, ALU.add)
+            return w2_raw[b, 0][:, 0:2, cols]
+
+        def weave_late(b, room):
+            woven = room.bitcast(BF16).rearrange("p (i n t) -> p n t i", i=PACK, t=PACK)
+            for first in range(0, P, LATE_PIECE):
+                cols = slice(first, first + LATE_PIECE)
+                rows = w2_raw[b, 1][:].rearrange("p t (n i) -> p n t i", i=PACK)
+                nc.scalar.copy(out=woven[:, cols], in_=rows[:, cols])
+
+        def quantize_w2(b, c, room, tag):
+            w2_codes[b, c] = keep.tile([P, K_PASS], U32, name="w2_codes%d%d" % (b, c), tag=tag, align_bytes=64)
             w2_planes[b, c] = keep.tile([P, K_PASS], U8, name="w2_plane%d%d" % (b, c), align_bytes=64)
             nc.vector.quantize_mx(
                 out=w2_codes[b, c][:].bitcast(FP8X4),
@@ -213,9 +224,9 @@ def tile_list_escapement_wear_match_kernel(
             )
 
         turns = {}
-        whole = {}
+        first_whole = keep.tile([P, 2, EARLY_PIECE], F32, name="first_whole", align_bytes=64)
+        whole = {0: first_whole[:]}
         cosines = keep.tile([P, CHUNKS, PACK, P], F32, name="cosines", align_bytes=64)
-        late_cosines = keep.tile([P, 2, M, 2], F32, name="late_cosines", align_bytes=64)
 
         def pick_healthy(i, spot):
             nc.vector.tensor_scalar(spot, h_tiles[i][:].indirect(pos1_sb[:]), 1.0 / TWO_PI, 0.25, ALU.mult, ALU.add)
@@ -223,8 +234,9 @@ def tile_list_escapement_wear_match_kernel(
         def pick_early(i):
             turns[i] = keep.tile([P, M], F32, name="turns%d" % i, align_bytes=64)
             pick_healthy(i, turns[i][:])
-            whole[i] = ring.tile([P, M], I32, name="whole", bufs=3, align_bytes=64)
-            nc.gpsimd.tensor_scalar(whole[i][:], turns[i][:], -TURN_STEP, TURN_BITS, ALU.mult, ALU.add)
+            halved = turns[i][:].rearrange("p (e m) -> p e m", e=2)
+            nc.gpsimd.tensor_scalar(whole[i].bitcast(I32), halved, -TURN_STEP, TURN_BITS, ALU.mult, ALU.add)
+            whole[i + 1] = weave_early(i)
 
         late_turns = {}
         late_whole = {}
@@ -252,7 +264,7 @@ def tile_list_escapement_wear_match_kernel(
             phases = psum.tile([P, CHUNKS, P], F32, name="bank%d" % PHASE_BANKS[i % 2])
             for q in range(CHUNKS):
                 cols = slice(P * q, P * (q + 1))
-                terms = (whole[i][:, cols].bitcast(F32), less_offset[:], turns[i][:, cols])
+                terms = (whole[i][:, q // 2, P * (q % 2) : P * (q % 2 + 1)], less_offset[:], turns[i][:, cols])
                 for n, term in enumerate(terms):
                     nc.tensor.matmul(
                         out=phases[:, q, :], lhsT=term, rhs=identity[:], is_transpose=True,
@@ -268,20 +280,14 @@ def tile_list_escapement_wear_match_kernel(
         x_codes = [keep.tile([P, M], U32, name="x_codes%d" % b, align_bytes=64) for b in range(PASSES2)]
         x_planes = [keep.tile([P, M], U8, name="x_plane%d" % b, align_bytes=64) for b in range(PASSES2)]
         halves = [slice(X_COLS * half, X_COLS * (half + 1)) for half in range(X_PARTS)]
-        back = {}
 
-        def turn_back(q):
-            back[q] = psum.tile([P, PACK, P], F32, name="bank%d" % BACK_BANKS[q])
-            for t in range(PACK):
-                nc.tensor.transpose(back[q][:, t, :], cosines[:, q, t, :], identity[:])
+        early_pairs = keep.tile([P, 2, M, 2], BF16, name="early_pairs", align_bytes=64)
 
-        def weigh_early(q, woven):
-            nc.vector.tensor_tensor(
-                woven.rearrange("p (m e t) -> p m t e", e=2, t=PACK),
-                back[q][:].rearrange("p t (m e) -> p m t e", e=2),
-                gain_sb[:, 0, :].unsqueeze(1).unsqueeze(3).to_broadcast([P, P // 2, PACK, 2]),
-                ALU.mult,
-            )
+        def weigh_early(t):
+            back = psum.tile([P, M], F32, name="bank%d" % BACK_BANKS[t])
+            for q in range(CHUNKS):
+                nc.tensor.transpose(back[:, P * q : P * (q + 1)], cosines[:, q, t, :], identity[:])
+            nc.scalar.activation(early_pairs[:, t // 2, :, t % 2], back[:], ACT.Copy, scale=gain_sb[:, 0, t : t + 1])
 
         def weigh_late(cols, woven):
             nc.vector.tensor_tensor(
@@ -316,7 +322,7 @@ def tile_list_escapement_wear_match_kernel(
                 stop=(b == PASSES2 - 1),
             )
 
-        picked = keep.tile([P, PACK, M], F32, name="picked", align_bytes=64)
+        picked = keep.tile([P, PACK + 1, M], F32, name="picked", align_bytes=64)
         for i in range(TILES):
             make_h(i)
             if i < PACK:
@@ -324,35 +330,37 @@ def tile_list_escapement_wear_match_kernel(
                 pick_suspects(i, picked[:, i, :], S)
             else:
                 pick_late(i)
-            if PACK - 1 <= i < TILES - 2:
-                cosine(i - PACK + 1)
-        cosine(PACK - 1)
-        for q in range(CHUNKS):
-            turn_back(q)
+            if i == PACK + 1:
+                pick_suspects(i, picked[:, PACK, :], S)
+        gain_sb = keep.tile([P, PASSES2, PACK], F32, name="gain_sb", tag="turns0", align_bytes=64)
+        nc.sync.dma_start(out=gain_sb[:], in_=gain.rearrange("(b p t) -> p b t", p=P, t=PACK))
+        late_cosines = keep.tile([P, 2, M, 2], F32, name="late_cosines", tag="w1_codes1", align_bytes=64)
         late_cosine(0, spare(6))
+        for t in range(PACK):
+            weigh_early(t)
         pick_suspects(4, spare(7)[:, 0:M], 2 * S)
         late_cosine(1, spare(4))
         for b in range(PASSES2):
-            room = ring.tile([P, 2 * M], F32, name="w2_woven", align_bytes=64)
-            weave_w2(b, 0, room[:])
-            load_w2(b, 1)
-        early_woven = late_whole[1][:].rearrange("p e m -> p (e m)").bitcast(BF16)
-        for q in range(CHUNKS):
-            weigh_early(q, early_woven[:, M * q : M * (q + 1)])
+            weave_late(b, spare(b))
+            quantize_w2(b, 0, early_rooms[b][:], "late_turns%d" % b)
+        early_woven = late_whole[1][:].rearrange("p e m -> p (e m)").bitcast(U32)
+        nc.vector.tensor_copy(
+            out=early_woven.rearrange("p (m h) -> p m h", h=2),
+            in_=early_pairs[:].rearrange("p h m e -> p (h m e)").bitcast(U32).rearrange("p (h m) -> p m h", h=2),
+        )
+        quantize_x(0, slice(0, M), early_woven.bitcast(BF16))
+        quantize_w2(1, 1, spare(1), "early_pairs")
         x_woven = keep.tile([P, X_PARTS, X_COLS * PACK], BF16, name="x_woven", align_bytes=64)
         for half in range(X_PARTS):
             weigh_late(halves[half], x_woven[:, half, :])
-            quantize_x(0, halves[half], early_woven[:, 2 * M * half : 2 * M * (half + 1)])
         for half in range(X_PARTS):
             quantize_x(1, halves[half], x_woven[:, half, :])
-        pick_suspects(5, x_woven[:, 1, :].bitcast(F32), S)
-        weave_w2(0, 1, spare(4))
-        weave_w2(1, 1, spare(6))
+        quantize_w2(0, 1, spare(0), "w1_codes1")
         nc.scalar.activation(warm[:, 1:2], late_cosines[:, 1, 0, 0:1], ACT.Exp)
         nw_sb = keep.tile([P, PACK], F32, name="nw_sb", tag="slot_w", align_bytes=64)
         with nc.allow_non_contiguous_dma(reason="one value of nw to a partition and row tile"):
             nc.sync.dma_start(out=nw_sb[:, 0:PACK], in_=nw[0:K_PASS].rearrange("(i p) -> p i", p=P))
-        late_nw = keep.tile([P, PACK], F32, name="late_nw", tag="slot_a", align_bytes=64)
+        late_nw = keep.tile([P, PACK], F32, name="late_nw", tag="turns2", align_bytes=64)
         nc.sync.dma_start(out=late_nw[:], in_=nw[K_PASS:].rearrange("(p t) -> p t", t=PACK))
         for i in range(TILES):
             for b in range(PASSES2):

@@ -38,8 +38,8 @@ LATE_PIECE = 32
 TILES = H // P
 CHUNKS = M // P
 OPEN_TILES = 3
-VECTOR_SQUARES = (7,)
-COSINE_BEHIND = ((4, 1), (5, 1), (6, 0), (6, 1))
+VECTOR_SQUARES = (1, 3, 5, 7)
+COSINE_BEHIND = ((4, 1), (5, 1), (6, 1), (7, 0))
 H_BANKS = 3
 PHASE_BANKS = (3, 7)
 BACK_BANKS = (7, 4, 5, 6)
@@ -197,7 +197,7 @@ def tile_list_escapement_wear_match_kernel(
         w2_codes = {}
         w2_planes = {}
 
-        early_rooms = [keep.tile([P, 2 * M], F32, name="w2_woven%d" % b, align_bytes=64) for b in range(PASSES2)]
+        early_rooms = [keep.tile([P, 2 * M], F32, name="w2_woven%d" % b, tag="w2_woven%d" % b, align_bytes=64) for b in range(PASSES2)]
 
         def weave_early(piece):
             b, half = divmod(piece, 2)
@@ -232,33 +232,26 @@ def tile_list_escapement_wear_match_kernel(
             nc.vector.tensor_scalar(spot, h_tiles[i][:].indirect(pos1_sb[:]), 1.0 / TWO_PI, 0.25, ALU.mult, ALU.add)
 
         def pick_early(i):
-            turns[i] = keep.tile([P, M], F32, name="turns%d" % i, align_bytes=64)
+            turns[i] = keep.tile([P, M], F32, name="turns%d" % i, tag="turns%d" % i, align_bytes=64)
             pick_healthy(i, turns[i][:])
             halved = turns[i][:].rearrange("p (e m) -> p e m", e=2)
             nc.gpsimd.tensor_scalar(whole[i].bitcast(I32), halved, -TURN_STEP, TURN_BITS, ALU.mult, ALU.add)
             whole[i + 1] = weave_early(i)
 
-        late_turns = {}
-        late_whole = {}
-
         def pick_late(i):
-            pair, e = divmod(i - PACK, 2)
-            if e == 0:
-                late_turns[pair] = keep.tile([P, 2, M], F32, name="late_turns%d" % pair, align_bytes=64)
-            pick_healthy(i, late_turns[pair][:, e, :])
-            if e == 1:
-                late_whole[pair] = keep.tile([P, 2, M], I32, name="late_whole%d" % pair, align_bytes=64)
-                nc.gpsimd.tensor_scalar(late_whole[pair][:], late_turns[pair][:], 1.0, 0.0, ALU.mult, ALU.add)
+            turns[i] = keep.tile([P, M], F32, name="turns%d" % i, tag="turns%d" % i, align_bytes=64)
+            pick_healthy(i, turns[i][:])
 
-        def late_cosine(pair, room):
-            phases = room.rearrange("p (e m) -> p e m", e=2)
-            nc.vector.tensor_tensor(phases, late_whole[pair][:], late_turns[pair][:], ALU.subtract)
-            nc.scalar.activation(
-                late_cosines[:, pair].rearrange("p (c i) e -> p c e i", i=PACK),
-                phases.rearrange("p e (c i) -> p c e i", i=PACK),
-                ACT.Sin,
-                scale=-TWO_PI,
-            )
+        late_phases = {}
+
+        def late_phase(i, phases):
+            late_phases[i] = phases
+            late_whole = keep.tile([P, M], I32, name="late_whole%d" % i, tag="late_whole", align_bytes=64)
+            nc.gpsimd.tensor_scalar(late_whole[:], turns[i][:], 1.0, 0.0, ALU.mult, ALU.add)
+            nc.vector.tensor_tensor(phases, late_whole[:], turns[i][:], ALU.subtract)
+
+        def late_cosine(i):
+            nc.scalar.activation(late_cosines[:, i - PACK, :], late_phases[i], ACT.Sin, scale=-TWO_PI)
 
         def cosine(i):
             phases = psum.tile([P, CHUNKS, P], F32, name="bank%d" % PHASE_BANKS[i % 2])
@@ -281,7 +274,7 @@ def tile_list_escapement_wear_match_kernel(
         x_planes = [keep.tile([P, M], U8, name="x_plane%d" % b, align_bytes=64) for b in range(PASSES2)]
         halves = [slice(X_COLS * half, X_COLS * (half + 1)) for half in range(X_PARTS)]
 
-        early_pairs = keep.tile([P, 2, M, 2], BF16, name="early_pairs", align_bytes=64)
+        early_pairs = keep.tile([P, 2, M, 2], BF16, name="early_pairs", tag="early_pairs", align_bytes=64)
 
         def weigh_early(t):
             back = psum.tile([P, M], F32, name="bank%d" % BACK_BANKS[t])
@@ -289,13 +282,9 @@ def tile_list_escapement_wear_match_kernel(
                 nc.tensor.transpose(back[:, P * q : P * (q + 1)], cosines[:, q, t, :], identity[:])
             nc.scalar.activation(early_pairs[:, t // 2, :, t % 2], back[:], ACT.Copy, scale=gain_sb[:, 0, t : t + 1])
 
-        def weigh_late(cols, woven):
-            nc.vector.tensor_tensor(
-                woven.rearrange("p (m h e) -> p m h e", h=2, e=2),
-                late_cosines[:, :, cols].rearrange("p h m e -> p m h e"),
-                gain_sb[:, 1, :].rearrange("p (h e) -> p h e", e=2).unsqueeze(1).to_broadcast([P, X_COLS, 2, 2]),
-                ALU.mult,
-            )
+        def weave_pairs(pairs, cols, woven):
+            words = pairs[:].rearrange("p h m e -> p (h m e)").bitcast(U32).rearrange("p (h m) -> p m h", h=2)
+            nc.vector.tensor_copy(out=woven[:].rearrange("p (m h) -> p m h", h=2)[:, cols], in_=words[:, cols])
 
         def quantize_x(b, cols, woven):
             nc.vector.quantize_mx(out=x_codes[b][:, cols].bitcast(FP8X4), scales=x_planes[b][:, cols], in_=woven)
@@ -322,7 +311,7 @@ def tile_list_escapement_wear_match_kernel(
                 stop=(b == PASSES2 - 1),
             )
 
-        picked = keep.tile([P, PACK + 1, M], F32, name="picked", align_bytes=64)
+        picked = keep.tile([P, PACK + 2, M], F32, name="picked", align_bytes=64)
         for i in range(TILES):
             make_h(i)
             if i < PACK:
@@ -330,33 +319,40 @@ def tile_list_escapement_wear_match_kernel(
                 pick_suspects(i, picked[:, i, :], S)
             else:
                 pick_late(i)
-            if i == PACK + 1:
-                pick_suspects(i, picked[:, PACK, :], S)
+            if PACK < i < TILES - 1:
+                pick_suspects(i, picked[:, i - 1, :], S)
+        late_cosines = keep.tile([P, PACK, M], F32, name="late_cosines", tag="w1_codes1", align_bytes=64)
         gain_sb = keep.tile([P, PASSES2, PACK], F32, name="gain_sb", tag="turns0", align_bytes=64)
         nc.sync.dma_start(out=gain_sb[:], in_=gain.rearrange("(b p t) -> p b t", p=P, t=PACK))
-        late_cosines = keep.tile([P, 2, M, 2], F32, name="late_cosines", tag="w1_codes1", align_bytes=64)
-        late_cosine(0, spare(6))
+        for i in range(PACK, TILES - 1):
+            late_phase(i, spare(i + 1)[:, 0:M])
+        pick_suspects(PACK, spare(TILES - 1)[:, M:], 2 * S)
+        late_phase(TILES - 1, spare(PACK)[:, 0:M])
         for t in range(PACK):
             weigh_early(t)
-        pick_suspects(4, spare(7)[:, 0:M], 2 * S)
-        late_cosine(1, spare(4))
+        for i in range(PACK, TILES):
+            late_cosine(i)
         for b in range(PASSES2):
             weave_late(b, spare(b))
-            quantize_w2(b, 0, early_rooms[b][:], "late_turns%d" % b)
-        early_woven = late_whole[1][:].rearrange("p e m -> p (e m)").bitcast(U32)
-        nc.vector.tensor_copy(
-            out=early_woven.rearrange("p (m h) -> p m h", h=2),
-            in_=early_pairs[:].rearrange("p h m e -> p (h m e)").bitcast(U32).rearrange("p (h m) -> p m h", h=2),
-        )
-        quantize_x(0, slice(0, M), early_woven.bitcast(BF16))
-        quantize_w2(1, 1, spare(1), "early_pairs")
-        x_woven = keep.tile([P, X_PARTS, X_COLS * PACK], BF16, name="x_woven", align_bytes=64)
-        for half in range(X_PARTS):
-            weigh_late(halves[half], x_woven[:, half, :])
-        for half in range(X_PARTS):
-            quantize_x(1, halves[half], x_woven[:, half, :])
-        quantize_w2(0, 1, spare(0), "w1_codes1")
-        nc.scalar.activation(warm[:, 1:2], late_cosines[:, 1, 0, 0:1], ACT.Exp)
+        quantize_w2(0, 0, early_rooms[0][:], "turns7")
+        early_woven = keep.tile([P, 2 * M], U32, name="early_woven", tag="turns6", align_bytes=64)
+        weave_pairs(early_pairs, slice(0, M), early_woven)
+        quantize_w2(1, 0, early_rooms[1][:], "late_whole")
+        quantize_x(0, slice(0, M), early_woven[:].bitcast(BF16))
+        late_pairs = keep.tile([P, 2, M, 2], BF16, name="late_pairs", align_bytes=64)
+        for t in range(PACK):
+            nc.scalar.activation(
+                late_pairs[:, t // 2, :, t % 2], late_cosines[:, t, :], ACT.Copy, scale=gain_sb[:, 1, t : t + 1]
+            )
+        late_woven = keep.tile([P, 2 * M], U32, name="late_woven", align_bytes=64)
+        for cols in halves:
+            weave_pairs(late_pairs, cols, late_woven)
+        for cols in halves:
+            quantize_x(1, cols, late_woven[:, 2 * cols.start : 2 * cols.stop].bitcast(BF16))
+        quantize_w2(1, 1, spare(1), "w2_woven1")
+        quantize_w2(0, 1, spare(0), "early_pairs")
+        pick_suspects(TILES - 1, early_woven[:, 0:M].bitcast(F32), S)
+        nc.scalar.activation(warm[:, 1:2], late_pairs[:, 1, 0:1, 1], ACT.Exp, scale=0.0)
         nw_sb = keep.tile([P, PACK], F32, name="nw_sb", tag="slot_w", align_bytes=64)
         with nc.allow_non_contiguous_dma(reason="one value of nw to a partition and row tile"):
             nc.sync.dma_start(out=nw_sb[:, 0:PACK], in_=nw[0:K_PASS].rearrange("(i p) -> p i", p=P))
@@ -382,5 +378,3 @@ def tile_list_escapement_wear_match_kernel(
                 score = ring.tile([P, width], F32, name="score", bufs=6)
                 nc.scalar.activation(score[:], square[:], ACT.Exp, scale=sharpness)
                 nc.sync.dma_start(out=rows[:, cols], in_=score[:])
-            if 2 <= i < 4:
-                pick_suspects(i + PACK, suspects[i], S)

@@ -29,6 +29,7 @@ LIST_ROWS = 16
 QUAD = 32
 SCALE_ROWS = 16
 FIRST_ROW = P - PASSES1 * SCALE_ROWS
+OTHER_ROW = FIRST_ROW + SCALE_ROWS
 TWO_PI = 2.0 * math.pi
 X_PARTS = 2
 X_COLS = M // X_PARTS
@@ -37,8 +38,8 @@ EARLY_PIECE = 256
 LATE_PIECE = 32
 TILES = H // P
 CHUNKS = M // P
-OPEN_TILES = 3
-VECTOR_SQUARES = (1, 3, 5, 7)
+OPEN_TILES = 2
+VECTOR_SQUARES = (1, 3, 5, 6, 7)
 COSINE_BEHIND = ((4, 1), (5, 1), (6, 1), (7, 0))
 H_BANKS = 3
 PHASE_BANKS = (3, 7)
@@ -65,13 +66,14 @@ def tile_list_escapement_wear_match_kernel(
 
         tab_scale_window = keep.tile([P, T], U8, name="tab_scale_window", tag="slot_s", align_bytes=64)
         scale_rows = keep.tile([P, S + H], U8, name="scale_rows", tag="slot_r", align_bytes=64)
-        planes = [keep.tile([P, S + H], U8, name="planes%d" % a, align_bytes=64) for a in range(PASSES1)]
+        first_planes = keep.tile([P, S + H], U8, name="first_planes", align_bytes=64)
+        other_planes = keep.tile([P, PASSES1 - 1, S + H], U8, name="other_planes", align_bytes=64)
+        planes = [first_planes[:]] + [other_planes[:, a, :] for a in range(PASSES1 - 1)]
         nc.vector.memset(tab_scale_window[0:FIRST_ROW, :].bitcast(I32), 0)
         late_scale_raw = keep.tile([P, K_PASS], U8, name="late_scale_raw", align_bytes=64)
         nc.gpsimd.memset(late_scale_raw[0:FIRST_ROW, :].bitcast(I32), 0)
-        nc.vector.memset(planes[0][:].bitcast(I32), 0)
-        for a in range(1, PASSES1):
-            nc.gpsimd.memset(planes[a][:].bitcast(I32), 0)
+        nc.vector.memset(first_planes[:].bitcast(I32), 0)
+        nc.gpsimd.memset(other_planes[:].bitcast(I32), 0)
 
         warm = keep.tile([P, 2], F32, name="warm")
         nc.gpsimd.memset(warm[:, 0:1], 0.0)
@@ -88,11 +90,9 @@ def tile_list_escapement_wear_match_kernel(
             (scale_rows[:, S : S + K_PASS], w1_scales[:, :, 0:K_PASS]),
         )
         for room, scales in scale_loads:
-            rows_in_hbm = scales.rearrange("a q t -> (a q) t").bitcast(I32)
-            for rows in (slice(0, 2 * SCALE_ROWS), slice(2 * SCALE_ROWS, 3 * SCALE_ROWS)):
-                nc.sync.dma_start(
-                    out=room[FIRST_ROW + rows.start : FIRST_ROW + rows.stop, :].bitcast(I32), in_=rows_in_hbm[rows]
-                )
+            words = scales.bitcast(I32)
+            nc.sync.dma_start(out=room[OTHER_ROW:P, :].bitcast(I32), in_=words[1:].rearrange("a q t -> q a t"))
+            nc.sync.dma_start(out=room[FIRST_ROW:OTHER_ROW, :].bitcast(I32), in_=words[0])
         tab_windows = {}
 
         def load_table(a, tag):
@@ -101,17 +101,12 @@ def tile_list_escapement_wear_match_kernel(
             tab_windows[a] = window
 
         load_table(0, "slot_a")
-        w1_codes = {}
-
-        def load_w1(b, tag):
-            w1_codes[b] = keep.tile([P, PASSES1, K_PASS // 2], I32, name="w1_codes%d" % b, tag=tag, align_bytes=64)
-            words = slice(b * K_PASS // 2, (b + 1) * K_PASS // 2)
-            nc.sync.dma_start(out=w1_codes[b][:], in_=w1_words.bitcast(I32).rearrange("a p w -> p a w")[:, :, words])
-
+        w1_in_hbm = w1_words.bitcast(I32).rearrange("a p w -> p a w")
         nc.sync.dma_start(pos1_sb[:], pos1)
         nc.sync.dma_start(pos2_sb[:], pos2)
         load_table(1, "slot_b")
-        load_w1(0, "slot_w")
+        w1_early = keep.tile([P, PASSES1, K_PASS // 2], I32, name="w1_early", tag="slot_w", align_bytes=64)
+        nc.sync.dma_start(out=w1_early[:], in_=w1_in_hbm[:, :, 0 : K_PASS // 2])
 
         v_packed = keep.tile([P, S], U8, name="v_packed", tag="slot_g", align_bytes=64)
         nc.vector.tensor_copy(out=v_packed[:], in_=tab_scale_window[:].indirect(offs_sb[:]))
@@ -120,24 +115,23 @@ def tile_list_escapement_wear_match_kernel(
             in_=late_scale_raw[:].rearrange("p (c t) -> p t c", t=PACK),
         )
         nc.vector.tensor_copy(out=scale_rows[:, 0:S].bitcast(I32), in_=v_packed[:].bitcast(I32))
-        for a in range(PASSES1):
-            for q in range(4):
-                first = FIRST_ROW + SCALE_ROWS * a + 4 * q
-                nc.sync.dma_start(
-                    out=planes[a][QUAD * q : QUAD * q + 4, :].bitcast(I32),
-                    in_=scale_rows[first : first + 4, :].bitcast(I32),
-                )
-                if (a, q) == (1, 0):
-                    load_table(2, "slot_g")
+        for q in range(4):
+            rows = scale_rows[FIRST_ROW + 4 * q : FIRST_ROW + 4 * (q + 1), :]
+            nc.sync.dma_start(out=first_planes[QUAD * q : QUAD * q + 4, :].bitcast(I32), in_=rows.bitcast(I32))
+        load_table(2, "slot_g")
+        for q in range(4):
+            rows = scale_rows[OTHER_ROW + 8 * q : OTHER_ROW + 8 * (q + 1), :]
+            nc.sync.dma_start(out=other_planes[QUAD * q : QUAD * q + 4].bitcast(I32), in_=rows.bitcast(I32))
 
         v_codes = {}
         for a in range(PASSES1):
-            for j in range(HALVES):
-                v_codes[a, j] = keep.tile([P, N], U32, name="v_codes%d%d" % (a, j), align_bytes=64)
-                cols = slice(j * N // LIST_ROWS, (j + 1) * N // LIST_ROWS)
-                nc.vector.tensor_copy(
-                    out=v_codes[a, j][:], in_=tab_windows[a][:].bitcast(U32).indirect(offs_sb[:, cols])
-                )
+            width = N if a == PASSES1 - 1 else S
+            for first in range(0, S, width):
+                picked_words = keep.tile([P, width], U32, name="v_codes%d%d" % (a, first // N), align_bytes=64)
+                cols = slice(first // LIST_ROWS, (first + width) // LIST_ROWS)
+                nc.vector.tensor_copy(out=picked_words[:], in_=tab_windows[a][:].bitcast(U32).indirect(offs_sb[:, cols]))
+                for j in range(width // N):
+                    v_codes[a, first // N + j] = picked_words[:, j * N : (j + 1) * N]
 
         w2_raw = {}
 
@@ -147,11 +141,12 @@ def tile_list_escapement_wear_match_kernel(
             nc.sync.dma_start(out=w2_raw[b, c][:], in_=rows.rearrange("(p t) n -> p t n", t=PACK))
 
         w1_late = keep.tile([P, PASSES1, K_PASS // 2], I32, name="w1_late", tag="slot_a", align_bytes=64)
-        nc.sync.dma_start(out=w1_late[:], in_=w1_words.bitcast(I32).rearrange("a p w -> p a w")[:, :, K_PASS // 2 :])
-        w1_codes[1] = keep.tile([P, PASSES1, K_PASS // 2], I32, name="w1_codes1", tag="w1_codes1", align_bytes=64)
+        nc.sync.dma_start(out=w1_late[:], in_=w1_in_hbm[:, :, K_PASS // 2 :])
+        w1_ordered = keep.tile([P, PASSES1, K_PASS // 2], I32, name="w1_ordered", tag="w1_codes1", align_bytes=64)
+        w1_codes = [w1_early, w1_ordered]
         for half in range(2):
             nc.vector.tensor_copy(
-                out=w1_codes[1][:].bitcast(U16).rearrange("p a (t c) -> p t a c", t=PACK)[:, 2 * half : 2 * half + 2],
+                out=w1_ordered[:].bitcast(U16).rearrange("p a (t c) -> p t a c", t=PACK)[:, 2 * half : 2 * half + 2],
                 in_=w1_late[:].bitcast(U16).rearrange("p a (c t) -> p t a c", t=PACK)[:, 2 * half : 2 * half + 2],
             )
         for c in range(PASSES2):
@@ -164,7 +159,7 @@ def tile_list_escapement_wear_match_kernel(
                 out=bank[:],
                 lhsT=w1_codes[b][:, a, t * P // 2 : (t + 1) * P // 2].bitcast(U8).bitcast(FP4X4),
                 lhsT_scale=planes[a][:, S + P * i : S + P * (i + 1)],
-                rhs=v_codes[a, j][:].bitcast(FP8X4),
+                rhs=v_codes[a, j].bitcast(FP8X4),
                 rhs_scale=planes[a][:, j * N : (j + 1) * N],
                 start=(a == 0),
                 stop=(a == PASSES1 - 1),
@@ -297,19 +292,20 @@ def tile_list_escapement_wear_match_kernel(
 
         y_banks = {}
 
-        def second_product(i, b):
+        def second_product(i, cols, bank):
             c, u = divmod(i, PACK)
-            if b == 0:
-                y_banks[i] = psum.tile([P, M], F32, name="bank%d" % Y_BANKS[i])
-            nc.tensor.matmul_mx(
-                out=y_banks[i][:],
-                lhsT=w2_codes[b, c][:, P * u : P * (u + 1)].bitcast(FP8X4),
-                lhsT_scale=w2_planes[b, c][:, P * u : P * (u + 1)],
-                rhs=x_codes[b][:].bitcast(FP8X4),
-                rhs_scale=x_planes[b][:],
-                start=(b == 0),
-                stop=(b == PASSES2 - 1),
-            )
+            y_banks[i, cols.start] = psum.tile([P, cols.stop - cols.start], F32, name="bank%d" % bank)
+            for n in range(PASSES2):
+                b = (n + c) % PASSES2
+                nc.tensor.matmul_mx(
+                    out=y_banks[i, cols.start][:],
+                    lhsT=w2_codes[b, c][:, P * u : P * (u + 1)].bitcast(FP8X4),
+                    lhsT_scale=w2_planes[b, c][:, P * u : P * (u + 1)],
+                    rhs=x_codes[b][:, cols].bitcast(FP8X4),
+                    rhs_scale=x_planes[b][:, cols],
+                    start=(n == 0),
+                    stop=(n == PASSES2 - 1),
+                )
 
         picked = keep.tile([P, PACK + 2, M], F32, name="picked", align_bytes=64)
         for i in range(TILES):
@@ -339,7 +335,7 @@ def tile_list_escapement_wear_match_kernel(
         weave_pairs(early_pairs, slice(0, M), early_woven)
         quantize_w2(1, 0, early_rooms[1][:], "late_whole")
         quantize_x(0, slice(0, M), early_woven[:].bitcast(BF16))
-        late_pairs = keep.tile([P, 2, M, 2], BF16, name="late_pairs", align_bytes=64)
+        late_pairs = keep.tile([P, 2, M, 2], BF16, name="late_pairs", tag="late_pairs", align_bytes=64)
         for t in range(PACK):
             nc.scalar.activation(
                 late_pairs[:, t // 2, :, t % 2], late_cosines[:, t, :], ACT.Copy, scale=gain_sb[:, 1, t : t + 1]
@@ -349,8 +345,8 @@ def tile_list_escapement_wear_match_kernel(
             weave_pairs(late_pairs, cols, late_woven)
         for cols in halves:
             quantize_x(1, cols, late_woven[:, 2 * cols.start : 2 * cols.stop].bitcast(BF16))
-        quantize_w2(1, 1, spare(1), "w2_woven1")
-        quantize_w2(0, 1, spare(0), "early_pairs")
+        quantize_w2(0, 1, spare(0), "w2_woven1")
+        quantize_w2(1, 1, spare(1), "late_pairs")
         pick_suspects(TILES - 1, early_woven[:, 0:M].bitcast(F32), S)
         nc.scalar.activation(warm[:, 1:2], late_pairs[:, 1, 0:1, 1], ACT.Exp, scale=0.0)
         nw_sb = keep.tile([P, PACK], F32, name="nw_sb", tag="slot_w", align_bytes=64)
@@ -358,23 +354,27 @@ def tile_list_escapement_wear_match_kernel(
             nc.sync.dma_start(out=nw_sb[:, 0:PACK], in_=nw[0:K_PASS].rearrange("(i p) -> p i", p=P))
         late_nw = keep.tile([P, PACK], F32, name="late_nw", tag="turns2", align_bytes=64)
         nc.sync.dma_start(out=late_nw[:], in_=nw[K_PASS:].rearrange("(p t) -> p t", t=PACK))
-        for i in range(TILES):
-            for b in range(PASSES2):
-                second_product(i, b)
+        second_product(0, halves[0], Y_BANKS[0])
+        second_product(0, halves[1], Y_BANKS[-1])
+        for i in range(1, TILES - 1):
+            second_product(i, slice(0, M), Y_BANKS[i])
         late_rows = out[K_PASS:].rearrange("(p u) m -> u p m", u=PACK)
         for i in range(TILES):
-            width = M // 2 if i == TILES - 1 else M
+            cuts = {0: (0, M // 2, M), TILES - 1: (0, M // 2, 3 * M // 4, M)}.get(i, (0, M))
             rows = out[P * i : P * (i + 1)] if i < PACK else late_rows[i - PACK]
             sharpness = nw_sb[:, i : i + 1] if i < PACK else late_nw[:, i - PACK : i - PACK + 1]
-            for first in range(0, M, width):
-                cols = slice(first, first + width)
-                diff = ring.tile([P, width], F32, name="diff", bufs=4)
-                nc.vector.tensor_tensor(diff[:], y_banks[i][:, cols], suspects[i][:, cols], ALU.subtract)
-                square = ring.tile([P, width], F32, name="square", bufs=3)
+            for first, last in zip(cuts, cuts[1:]):
+                cols = slice(first, last)
+                width = last - first
+                diff = ring.tile([P, width], F32, name="diff", bufs=5)
+                nc.vector.tensor_tensor(diff[:], y_banks[i, first][:] if i == 0 else y_banks[i, 0][:, cols], suspects[i][:, cols], ALU.subtract)
+                square = ring.tile([P, width], F32, name="square", bufs=5)
                 if i in VECTOR_SQUARES:
                     nc.vector.tensor_tensor(square[:], diff[:], diff[:], ALU.mult)
                 else:
                     nc.scalar.activation(square[:], diff[:], ACT.Square)
-                score = ring.tile([P, width], F32, name="score", bufs=6)
+                score = ring.tile([P, width], F32, name="score", bufs=8)
                 nc.scalar.activation(score[:], square[:], ACT.Exp, scale=sharpness)
                 nc.sync.dma_start(out=rows[:, cols], in_=score[:])
+            if i == 0:
+                second_product(TILES - 1, slice(0, M), Y_BANKS[-1])

@@ -29,7 +29,6 @@ LIST_ROWS = 16
 QUAD = 32
 SCALE_ROWS = 16
 FIRST_ROW = P - PASSES1 * SCALE_ROWS
-OTHER_ROW = FIRST_ROW + SCALE_ROWS
 TWO_PI = 2.0 * math.pi
 X_PARTS = 2
 X_COLS = M // X_PARTS
@@ -38,7 +37,7 @@ EARLY_PIECE = 256
 LATE_PIECE = 32
 TILES = H // P
 CHUNKS = M // P
-OPEN_TILES = 2
+OPEN_TILES = 3
 VECTOR_SQUARES = (1, 3, 5, 6, 7)
 COSINE_BEHIND = ((4, 1), (5, 1), (6, 1), (7, 0))
 H_BANKS = 3
@@ -66,14 +65,13 @@ def tile_list_escapement_wear_match_kernel(
 
         tab_scale_window = keep.tile([P, T], U8, name="tab_scale_window", tag="slot_s", align_bytes=64)
         scale_rows = keep.tile([P, S + H], U8, name="scale_rows", tag="slot_r", align_bytes=64)
-        first_planes = keep.tile([P, S + H], U8, name="first_planes", align_bytes=64)
-        other_planes = keep.tile([P, PASSES1 - 1, S + H], U8, name="other_planes", align_bytes=64)
-        planes = [first_planes[:]] + [other_planes[:, a, :] for a in range(PASSES1 - 1)]
+        planes = [keep.tile([P, S + H], U8, name="planes%d" % a, align_bytes=64) for a in range(PASSES1)]
         nc.vector.memset(tab_scale_window[0:FIRST_ROW, :].bitcast(I32), 0)
         late_scale_raw = keep.tile([P, K_PASS], U8, name="late_scale_raw", align_bytes=64)
         nc.gpsimd.memset(late_scale_raw[0:FIRST_ROW, :].bitcast(I32), 0)
-        nc.vector.memset(first_planes[:].bitcast(I32), 0)
-        nc.gpsimd.memset(other_planes[:].bitcast(I32), 0)
+        nc.vector.memset(planes[0][:].bitcast(I32), 0)
+        for a in range(1, PASSES1):
+            nc.gpsimd.memset(planes[a][:].bitcast(I32), 0)
 
         warm = keep.tile([P, 2], F32, name="warm")
         nc.gpsimd.memset(warm[:, 0:1], 0.0)
@@ -90,9 +88,11 @@ def tile_list_escapement_wear_match_kernel(
             (scale_rows[:, S : S + K_PASS], w1_scales[:, :, 0:K_PASS]),
         )
         for room, scales in scale_loads:
-            words = scales.bitcast(I32)
-            nc.sync.dma_start(out=room[OTHER_ROW:P, :].bitcast(I32), in_=words[1:].rearrange("a q t -> q a t"))
-            nc.sync.dma_start(out=room[FIRST_ROW:OTHER_ROW, :].bitcast(I32), in_=words[0])
+            rows_in_hbm = scales.rearrange("a q t -> (a q) t").bitcast(I32)
+            for rows in (slice(0, 2 * SCALE_ROWS), slice(2 * SCALE_ROWS, 3 * SCALE_ROWS)):
+                nc.sync.dma_start(
+                    out=room[FIRST_ROW + rows.start : FIRST_ROW + rows.stop, :].bitcast(I32), in_=rows_in_hbm[rows]
+                )
         tab_windows = {}
 
         def load_table(a, tag):
@@ -101,12 +101,17 @@ def tile_list_escapement_wear_match_kernel(
             tab_windows[a] = window
 
         load_table(0, "slot_a")
-        w1_in_hbm = w1_words.bitcast(I32).rearrange("a p w -> p a w")
+        w1_codes = {}
+
+        def load_w1(b, tag):
+            w1_codes[b] = keep.tile([P, PASSES1, K_PASS // 2], I32, name="w1_codes%d" % b, tag=tag, align_bytes=64)
+            words = slice(b * K_PASS // 2, (b + 1) * K_PASS // 2)
+            nc.sync.dma_start(out=w1_codes[b][:], in_=w1_words.bitcast(I32).rearrange("a p w -> p a w")[:, :, words])
+
         nc.sync.dma_start(pos1_sb[:], pos1)
         nc.sync.dma_start(pos2_sb[:], pos2)
         load_table(1, "slot_b")
-        w1_early = keep.tile([P, PASSES1, K_PASS // 2], I32, name="w1_early", tag="slot_w", align_bytes=64)
-        nc.sync.dma_start(out=w1_early[:], in_=w1_in_hbm[:, :, 0 : K_PASS // 2])
+        load_w1(0, "slot_w")
 
         v_packed = keep.tile([P, S], U8, name="v_packed", tag="slot_g", align_bytes=64)
         nc.vector.tensor_copy(out=v_packed[:], in_=tab_scale_window[:].indirect(offs_sb[:]))
@@ -115,13 +120,15 @@ def tile_list_escapement_wear_match_kernel(
             in_=late_scale_raw[:].rearrange("p (c t) -> p t c", t=PACK),
         )
         nc.vector.tensor_copy(out=scale_rows[:, 0:S].bitcast(I32), in_=v_packed[:].bitcast(I32))
-        for q in range(4):
-            rows = scale_rows[FIRST_ROW + 4 * q : FIRST_ROW + 4 * (q + 1), :]
-            nc.sync.dma_start(out=first_planes[QUAD * q : QUAD * q + 4, :].bitcast(I32), in_=rows.bitcast(I32))
-        load_table(2, "slot_g")
-        for q in range(4):
-            rows = scale_rows[OTHER_ROW + 8 * q : OTHER_ROW + 8 * (q + 1), :]
-            nc.sync.dma_start(out=other_planes[QUAD * q : QUAD * q + 4].bitcast(I32), in_=rows.bitcast(I32))
+        for a in range(PASSES1):
+            for q in range(4):
+                first = FIRST_ROW + SCALE_ROWS * a + 4 * q
+                nc.sync.dma_start(
+                    out=planes[a][QUAD * q : QUAD * q + 4, :].bitcast(I32),
+                    in_=scale_rows[first : first + 4, :].bitcast(I32),
+                )
+                if (a, q) == (1, 0):
+                    load_table(2, "slot_g")
 
         v_codes = {}
         for a in range(PASSES1):
@@ -141,12 +148,11 @@ def tile_list_escapement_wear_match_kernel(
             nc.sync.dma_start(out=w2_raw[b, c][:], in_=rows.rearrange("(p t) n -> p t n", t=PACK))
 
         w1_late = keep.tile([P, PASSES1, K_PASS // 2], I32, name="w1_late", tag="slot_a", align_bytes=64)
-        nc.sync.dma_start(out=w1_late[:], in_=w1_in_hbm[:, :, K_PASS // 2 :])
-        w1_ordered = keep.tile([P, PASSES1, K_PASS // 2], I32, name="w1_ordered", tag="w1_codes1", align_bytes=64)
-        w1_codes = [w1_early, w1_ordered]
+        nc.sync.dma_start(out=w1_late[:], in_=w1_words.bitcast(I32).rearrange("a p w -> p a w")[:, :, K_PASS // 2 :])
+        w1_codes[1] = keep.tile([P, PASSES1, K_PASS // 2], I32, name="w1_codes1", tag="w1_codes1", align_bytes=64)
         for half in range(2):
             nc.vector.tensor_copy(
-                out=w1_ordered[:].bitcast(U16).rearrange("p a (t c) -> p t a c", t=PACK)[:, 2 * half : 2 * half + 2],
+                out=w1_codes[1][:].bitcast(U16).rearrange("p a (t c) -> p t a c", t=PACK)[:, 2 * half : 2 * half + 2],
                 in_=w1_late[:].bitcast(U16).rearrange("p a (c t) -> p t a c", t=PACK)[:, 2 * half : 2 * half + 2],
             )
         for c in range(PASSES2):

@@ -227,7 +227,7 @@ def tile_list_escapement_wear_match_kernel(
         turns = {}
         first_whole = keep.tile([P, 2, EARLY_PIECE], F32, name="first_whole", align_bytes=64)
         whole = {0: first_whole[:]}
-        cosines = keep.tile([P, CHUNKS, PACK, P], F32, name="cosines", align_bytes=64)
+        cosines = keep.tile([P, CHUNKS, PACK, P], F32, name="cosines", tag="cosines", align_bytes=64)
 
         def pick_healthy(i, spot):
             nc.vector.tensor_scalar(spot, h_tiles[i][:].indirect(pos1_sb[:]), 1.0 / TWO_PI, 0.25, ALU.mult, ALU.add)
@@ -245,9 +245,9 @@ def tile_list_escapement_wear_match_kernel(
 
         late_phases = {}
 
-        def late_phase(i, phases):
+        def late_phase(i, phases, tag):
             late_phases[i] = phases
-            late_whole = keep.tile([P, M], I32, name="late_whole%d" % i, tag="late_whole", align_bytes=64)
+            late_whole = keep.tile([P, M], I32, name="late_whole%d" % i, tag=tag, align_bytes=64)
             nc.gpsimd.tensor_scalar(late_whole[:], turns[i][:], 1.0, 0.0, ALU.mult, ALU.add)
             nc.vector.tensor_tensor(phases, late_whole[:], turns[i][:], ALU.subtract)
 
@@ -313,7 +313,7 @@ def tile_list_escapement_wear_match_kernel(
                     stop=(n == PASSES2 - 1),
                 )
 
-        picked = keep.tile([P, PACK + 2, M], F32, name="picked", align_bytes=64)
+        picked = keep.tile([P, TILES - 1, M], F32, name="picked", align_bytes=64)
         for i in range(TILES):
             make_h(i)
             if i < PACK:
@@ -321,40 +321,41 @@ def tile_list_escapement_wear_match_kernel(
                 pick_suspects(i, picked[:, i, :], S)
             else:
                 pick_late(i)
-            if PACK < i < TILES - 1:
+            if i > PACK:
                 pick_suspects(i, picked[:, i - 1, :], S)
         late_cosines = keep.tile([P, PACK, M], F32, name="late_cosines", tag="w1_codes1", align_bytes=64)
         gain_sb = keep.tile([P, PASSES2, PACK], F32, name="gain_sb", tag="turns0", align_bytes=64)
         nc.sync.dma_start(out=gain_sb[:], in_=gain.rearrange("(b p t) -> p b t", p=P, t=PACK))
         for i in range(PACK, TILES - 1):
-            late_phase(i, spare(i + 1)[:, 0:M])
-        pick_suspects(PACK, spare(TILES - 1)[:, M:], 2 * S)
-        late_phase(TILES - 1, spare(PACK)[:, 0:M])
+            late_phase(i, spare(i + 1)[:, 0:M], "late_whole")
+        late_phase(TILES - 1, spare(TILES - 1)[:, M:], "turns4")
         for t in range(PACK):
             weigh_early(t)
         for i in range(PACK, TILES):
             late_cosine(i)
         for b in range(PASSES2):
             weave_late(b, spare(b))
-        quantize_w2(0, 0, early_rooms[0][:], "turns7")
-        early_woven = keep.tile([P, 2 * M], U32, name="early_woven", tag="turns6", align_bytes=64)
+        quantize_w2(0, 0, early_rooms[0][:], "cosines")
+        quantize_w2(1, 0, early_rooms[1][:], "turns6")
+        quantize_w2(0, 1, spare(0), "late_whole")
+        early_woven = keep.tile([P, 2 * M], U32, name="early_woven", align_bytes=64)
         weave_pairs(early_pairs, slice(0, M), early_woven)
-        quantize_w2(1, 0, early_rooms[1][:], "late_whole")
         quantize_x(0, slice(0, M), early_woven[:].bitcast(BF16))
-        late_pairs = keep.tile([P, 2, M, 2], BF16, name="late_pairs", tag="late_pairs", align_bytes=64)
+        pick_suspects(PACK, turns[TILES - 1][:], S)
+        late_planes = keep.tile([P, PACK, M], BF16, name="late_planes", tag="late_planes", align_bytes=64)
         for t in range(PACK):
-            nc.scalar.activation(
-                late_pairs[:, t // 2, :, t % 2], late_cosines[:, t, :], ACT.Copy, scale=gain_sb[:, 1, t : t + 1]
-            )
+            nc.scalar.activation(late_planes[:, t, :], late_cosines[:, t, :], ACT.Copy, scale=gain_sb[:, 1, t : t + 1])
         late_woven = keep.tile([P, 2 * M], U32, name="late_woven", align_bytes=64)
         for cols in halves:
-            weave_pairs(late_pairs, cols, late_woven)
+            woven = late_woven[:, 2 * cols.start : 2 * cols.stop].bitcast(BF16)
+            nc.vector.tensor_copy(
+                out=woven.rearrange("p (c i t) -> p c t i", i=PACK, t=PACK),
+                in_=late_planes[:, :, cols].rearrange("p t (c i) -> p c t i", i=PACK),
+            )
         for cols in halves:
             quantize_x(1, cols, late_woven[:, 2 * cols.start : 2 * cols.stop].bitcast(BF16))
-        quantize_w2(0, 1, spare(0), "w2_woven1")
-        quantize_w2(1, 1, spare(1), "late_pairs")
-        pick_suspects(TILES - 1, early_woven[:, 0:M].bitcast(F32), S)
-        nc.scalar.activation(warm[:, 1:2], late_pairs[:, 1, 0:1, 1], ACT.Exp, scale=0.0)
+        nc.scalar.activation(warm[:, 1:2], late_cosines[:, PACK - 1, 0:1], ACT.Exp)
+        quantize_w2(1, 1, spare(1), "late_planes")
         nw_sb = keep.tile([P, PACK], F32, name="nw_sb", tag="slot_w", align_bytes=64)
         with nc.allow_non_contiguous_dma(reason="one value of nw to a partition and row tile"):
             nc.sync.dma_start(out=nw_sb[:, 0:PACK], in_=nw[0:K_PASS].rearrange("(i p) -> p i", p=P))

@@ -37,9 +37,10 @@ EARLY_PIECE = 256
 LATE_PIECE = 32
 TILES = H // P
 CHUNKS = M // P
-OPEN_TILES = 3
+OPEN_TILES = 2
 VECTOR_SQUARES = (1, 3, 5, 6, 7)
 COSINE_BEHIND = ((4, 1), (5, 1), (6, 1), (7, 0))
+THREE_TERM_TILES = 3
 H_BANKS = 3
 PHASE_BANKS = (3, 7)
 BACK_BANKS = (7, 4, 5, 6)
@@ -225,6 +226,7 @@ def tile_list_escapement_wear_match_kernel(
             )
 
         turns = {}
+        less = {}
         first_whole = keep.tile([P, 2, EARLY_PIECE], F32, name="first_whole", align_bytes=64)
         whole = {0: first_whole[:]}
         cosines = keep.tile([P, CHUNKS, PACK, P], F32, name="cosines", tag="cosines", align_bytes=64)
@@ -237,6 +239,9 @@ def tile_list_escapement_wear_match_kernel(
             pick_healthy(i, turns[i][:])
             halved = turns[i][:].rearrange("p (e m) -> p e m", e=2)
             nc.gpsimd.tensor_scalar(whole[i].bitcast(I32), halved, -TURN_STEP, TURN_BITS, ALU.mult, ALU.add)
+            if i >= THREE_TERM_TILES:
+                less[i] = keep.tile([P, 2, EARLY_PIECE], F32, name="less%d" % i, tag="less", align_bytes=64)
+                nc.gpsimd.tensor_scalar(less[i][:], whole[i], 1.0, -TURN_OFFSET, ALU.mult, ALU.add)
             whole[i + 1] = weave_early(i)
 
         def pick_late(i):
@@ -258,7 +263,11 @@ def tile_list_escapement_wear_match_kernel(
             phases = psum.tile([P, CHUNKS, P], F32, name="bank%d" % PHASE_BANKS[i % 2])
             for q in range(CHUNKS):
                 cols = slice(P * q, P * (q + 1))
-                terms = (whole[i][:, q // 2, P * (q % 2) : P * (q % 2 + 1)], less_offset[:], turns[i][:, cols])
+                part = slice(P * (q % 2), P * (q % 2 + 1))
+                if i < THREE_TERM_TILES:
+                    terms = (whole[i][:, q // 2, part], less_offset[:], turns[i][:, cols])
+                else:
+                    terms = (less[i][:, q // 2, part], turns[i][:, cols])
                 for n, term in enumerate(terms):
                     nc.tensor.matmul(
                         out=phases[:, q, :], lhsT=term, rhs=identity[:], is_transpose=True,
@@ -373,7 +382,7 @@ def tile_list_escapement_wear_match_kernel(
             for first, last in zip(cuts, cuts[1:]):
                 cols = slice(first, last)
                 width = last - first
-                diff = ring.tile([P, width], F32, name="diff", bufs=5)
+                diff = ring.tile([P, width], F32, name="diff", bufs=4)
                 nc.vector.tensor_tensor(diff[:], y_banks[i, first][:] if i == 0 else y_banks[i, 0][:, cols], suspects[i][:, cols], ALU.subtract)
                 square = ring.tile([P, width], F32, name="square", bufs=5)
                 if i in VECTOR_SQUARES:

@@ -30,21 +30,14 @@ QUAD = 32
 SCALE_ROWS = 16
 FIRST_ROW = P - PASSES1 * SCALE_ROWS
 TWO_PI = 2.0 * math.pi
-X_PARTS = 2
-X_COLS = M // X_PARTS
-W2_SLOTS = (("slot_b", "slot_r"), ("slot_g", "slot_a"))
-EARLY_PIECE = 256
-LATE_PIECE = 32
 TILES = H // P
 CHUNKS = M // P
 OPEN_TILES = 2
-VECTOR_SQUARES = (1, 3, 5, 6, 7)
-COSINE_BEHIND = ((4, 1), (5, 1), (6, 1), (7, 0))
-THREE_TERM_TILES = 3
-H_BANKS = 3
-PHASE_BANKS = (3, 7)
-BACK_BANKS = (7, 4, 5, 6)
-Y_BANKS = (0, 1, 2, 3) + BACK_BANKS
+H_BANKS = {(7, 0): 4, (7, 1): 0}
+PHASE_BANKS = {2: 2, 3: 3, 5: 4, 6: 0}
+Y_BANKS = (4, 6, 7, 5, 1, 2, 3, 0)
+BACK_BANKS = {2: 5, 3: 6, 5: 7, 6: 5}
+LAST_TILE = 3
 TURN_OFFSET = 98304.0
 TURN_BITS = 1203765248.0
 TURN_STEP = 128.0
@@ -60,65 +53,61 @@ def tile_list_escapement_wear_match_kernel(
         ring = ctx.enter_context(tc.tile_pool(name="ring", bufs=2))
         psum = ctx.enter_context(tc.psum_pool(name="psum", bufs=1))
 
+        def room(shape, dtype, name, tag=None):
+            return keep.tile(shape, dtype, name=name, tag=tag or name, align_bytes=64)
+
         offs_sb = lists.tile([P, S // LIST_ROWS], U16, name="offs_sb")
         pos1_sb = lists.tile([P, M // LIST_ROWS], U16, name="pos1_sb")
         pos2_sb = lists.tile([P, M // LIST_ROWS], U16, name="pos2_sb")
 
-        tab_scale_window = keep.tile([P, T], U8, name="tab_scale_window", tag="slot_s", align_bytes=64)
-        scale_rows = keep.tile([P, S + H], U8, name="scale_rows", tag="slot_r", align_bytes=64)
-        planes = [keep.tile([P, S + H], U8, name="planes%d" % a, align_bytes=64) for a in range(PASSES1)]
+        tab_scale_window = room([P, T], U8, "tab_scale_window")
+        scale_rows = room([P, S + H], U8, "scale_rows")
+        planes = [room([P, S + H], U8, "planes%d" % a) for a in range(PASSES1)]
         nc.vector.memset(tab_scale_window[0:FIRST_ROW, :].bitcast(I32), 0)
-        late_scale_raw = keep.tile([P, K_PASS], U8, name="late_scale_raw", align_bytes=64)
-        nc.gpsimd.memset(late_scale_raw[0:FIRST_ROW, :].bitcast(I32), 0)
+        w1_scale_raw = room([P, H], U8, "w1_scale_raw")
+        nc.gpsimd.memset(w1_scale_raw[0:FIRST_ROW, :].bitcast(I32), 0)
         nc.vector.memset(planes[0][:].bitcast(I32), 0)
         for a in range(1, PASSES1):
             nc.gpsimd.memset(planes[a][:].bitcast(I32), 0)
 
-        warm = keep.tile([P, 2], F32, name="warm")
-        nc.gpsimd.memset(warm[:, 0:1], 0.0)
-        nc.scalar.activation(warm[:, 1:2], warm[:, 0:1], ACT.Sin)
-        identity = keep.tile([P, P], F32, name="identity", align_bytes=64)
-        make_identity(nc, identity[:])
-        less_offset = keep.tile([P, P], F32, name="less_offset", align_bytes=64)
-        nc.gpsimd.memset(less_offset[:], -TURN_OFFSET)
+        warm = room([P, PACK + 1], F32, "warm")
+        nc.gpsimd.memset(warm[:, 0:PACK], 0.0)
+        nc.scalar.activation(warm[:, PACK:], warm[:, 0:1], ACT.Sin)
 
         nc.sync.dma_start(offs_sb[:], offs)
-        scale_loads = (
-            (tab_scale_window[:], tab_scales),
-            (late_scale_raw[:], w1_scales[:, :, K_PASS:]),
-            (scale_rows[:, S : S + K_PASS], w1_scales[:, :, 0:K_PASS]),
-        )
-        for room, scales in scale_loads:
+        for spot, scales in ((tab_scale_window, tab_scales), (w1_scale_raw, w1_scales)):
             rows_in_hbm = scales.rearrange("a q t -> (a q) t").bitcast(I32)
             for rows in (slice(0, 2 * SCALE_ROWS), slice(2 * SCALE_ROWS, 3 * SCALE_ROWS)):
                 nc.sync.dma_start(
-                    out=room[FIRST_ROW + rows.start : FIRST_ROW + rows.stop, :].bitcast(I32), in_=rows_in_hbm[rows]
+                    out=spot[FIRST_ROW + rows.start : FIRST_ROW + rows.stop, :].bitcast(I32), in_=rows_in_hbm[rows]
                 )
         tab_windows = {}
 
         def load_table(a, tag):
-            window = keep.tile([P, T], I32, name="tab_window%d" % a, tag=tag, align_bytes=64)
-            nc.sync.dma_start(out=window[:], in_=tab_words[a].rearrange("p t i -> p (t i)").bitcast(I32))
-            tab_windows[a] = window
-
-        load_table(0, "slot_a")
-        w1_codes = {}
+            tab_windows[a] = room([P, T], I32, "tab_window%d" % a, tag)
+            nc.sync.dma_start(out=tab_windows[a][:], in_=tab_words[a].rearrange("p t i -> p (t i)").bitcast(I32))
 
         def load_w1(b, tag):
-            w1_codes[b] = keep.tile([P, PASSES1, K_PASS // 2], I32, name="w1_codes%d" % b, tag=tag, align_bytes=64)
-            words = slice(b * K_PASS // 2, (b + 1) * K_PASS // 2)
-            nc.sync.dma_start(out=w1_codes[b][:], in_=w1_words.bitcast(I32).rearrange("a p w -> p a w")[:, :, words])
+            words = room([P, PASSES1, K_PASS // 2], I32, "w1_words%d" % b, tag)
+            cols = slice(b * K_PASS // 2, (b + 1) * K_PASS // 2)
+            nc.sync.dma_start(out=words[:], in_=w1_words.bitcast(I32).rearrange("a p w -> p a w")[:, :, cols])
+            return words
 
+        load_table(0, "slot_a")
         nc.sync.dma_start(pos1_sb[:], pos1)
         nc.sync.dma_start(pos2_sb[:], pos2)
         load_table(1, "slot_b")
-        load_w1(0, "slot_w")
+        w1_early = load_w1(0, "slot_w")
 
-        v_packed = keep.tile([P, S], U8, name="v_packed", tag="slot_g", align_bytes=64)
+        v_packed = room([P, S], U8, "v_packed", "slot_g")
         nc.vector.tensor_copy(out=v_packed[:], in_=tab_scale_window[:].indirect(offs_sb[:]))
         nc.gpsimd.tensor_copy(
+            out=scale_rows[:, S : S + K_PASS].rearrange("p (t c) -> p t c", t=PACK),
+            in_=w1_scale_raw[:, 0:K_PASS].rearrange("p (c t) -> p t c", t=PACK),
+        )
+        nc.vector.tensor_copy(
             out=scale_rows[:, S + K_PASS :].rearrange("p (t c) -> p t c", t=PACK),
-            in_=late_scale_raw[:].rearrange("p (c t) -> p t c", t=PACK),
+            in_=w1_scale_raw[:, K_PASS:].rearrange("p (c t) -> p t c", t=PACK),
         )
         nc.vector.tensor_copy(out=scale_rows[:, 0:S].bitcast(I32), in_=v_packed[:].bitcast(I32))
         for a in range(PASSES1):
@@ -130,41 +119,60 @@ def tile_list_escapement_wear_match_kernel(
                 )
                 if (a, q) == (1, 0):
                     load_table(2, "slot_g")
+            if a == 1:
+                w1_late = load_w1(1, "slot_a")
+
+        less_offset = room([P, P], F32, "less_offset", "tab_scale_window")
+        nc.gpsimd.memset(less_offset[:], -TURN_OFFSET)
+        identity = room([P, P], F32, "identity", "w1_scale_raw")
+        make_identity(nc, identity[:])
+        w1_dealt = {}
+
+        def deal(words, b, a, pair, engine):
+            w1_dealt[2 * b + pair, a] = room([P, P], I32, "w1_dealt%d%d" % (2 * b + pair, a))
+            spot = w1_dealt[2 * b + pair, a][:].bitcast(U16).rearrange("p (t c) -> p c t", t=2)
+            engine(out=spot, in_=words[:, a, :].bitcast(U16).rearrange("p (c t) -> p c t", t=PACK)[:, :, 2 * pair : 2 * pair + 2])
+
+        for pair in range(2):
+            for a in range(PASSES1):
+                deal(w1_early, 0, a, pair, nc.scalar.copy)
+        for pair in range(2):
+            for a in range(PASSES1 - 1):
+                deal(w1_late, 1, a, pair, nc.scalar.copy)
 
         v_codes = {}
         for a in range(PASSES1):
             width = N if a == PASSES1 - 1 else S
             for first in range(0, S, width):
-                picked_words = keep.tile([P, width], U32, name="v_codes%d%d" % (a, first // N), align_bytes=64)
+                picked_words = room([P, width], U32, "v_codes%d%d" % (a, first // N))
                 cols = slice(first // LIST_ROWS, (first + width) // LIST_ROWS)
                 nc.vector.tensor_copy(out=picked_words[:], in_=tab_windows[a][:].bitcast(U32).indirect(offs_sb[:, cols]))
                 for j in range(width // N):
                     v_codes[a, first // N + j] = picked_words[:, j * N : (j + 1) * N]
 
+        for pair in range(2):
+            deal(w1_late, 1, PASSES1 - 1, pair, nc.vector.tensor_copy)
         w2_raw = {}
 
-        def load_w2(b, c):
-            w2_raw[b, c] = keep.tile([P, PACK, K_PASS], F32, name="w2_raw%d%d" % (b, c), tag=W2_SLOTS[b][c], align_bytes=64)
+        def load_w2(b, c, tag):
+            w2_raw[b, c] = room([P, PACK, K_PASS], F32, "w2_raw%d%d" % (b, c), tag)
             rows = w2[K_PASS * b : K_PASS * (b + 1), K_PASS * c : K_PASS * (c + 1)]
             nc.sync.dma_start(out=w2_raw[b, c][:], in_=rows.rearrange("(p t) n -> p t n", t=PACK))
 
-        w1_late = keep.tile([P, PASSES1, K_PASS // 2], I32, name="w1_late", tag="slot_a", align_bytes=64)
-        nc.sync.dma_start(out=w1_late[:], in_=w1_words.bitcast(I32).rearrange("a p w -> p a w")[:, :, K_PASS // 2 :])
-        w1_codes[1] = keep.tile([P, PASSES1, K_PASS // 2], I32, name="w1_codes1", tag="w1_codes1", align_bytes=64)
-        for half in range(2):
-            nc.vector.tensor_copy(
-                out=w1_codes[1][:].bitcast(U16).rearrange("p a (t c) -> p t a c", t=PACK)[:, 2 * half : 2 * half + 2],
-                in_=w1_late[:].bitcast(U16).rearrange("p a (c t) -> p t a c", t=PACK)[:, 2 * half : 2 * half + 2],
-            )
-        for c in range(PASSES2):
-            for b in range(PASSES2):
-                load_w2(b, c)
+        first_raw = []
+        for half, tag in enumerate(("slot_b", "slot_w")):
+            first_raw.append(room([P, PACK, K_PASS // 2], F32, "first_raw%d" % half, tag))
+            rows = w2[0:K_PASS, K_PASS + half * K_PASS // 2 : K_PASS + (half + 1) * K_PASS // 2]
+            nc.sync.dma_start(out=first_raw[half][:], in_=rows.rearrange("(p t) n -> p t n", t=PACK))
+        load_w2(1, 1, "slot_g")
+        gain_sb = room([P, PASSES2, PACK], F32, "gain_sb", "slot_a")
+        nw_sb = room([P, PASSES2, PACK], F32, "nw_sb", "w1_dealt11")
 
         def first_product(bank, i, j, a):
-            b, t = divmod(i, PACK)
+            pair, t = divmod(i, 2)
             nc.tensor.matmul_mx(
                 out=bank[:],
-                lhsT=w1_codes[b][:, a, t * P // 2 : (t + 1) * P // 2].bitcast(U8).bitcast(FP4X4),
+                lhsT=w1_dealt[pair, a][:, t * P // 2 : (t + 1) * P // 2].bitcast(U8).bitcast(FP4X4),
                 lhsT_scale=planes[a][:, S + P * i : S + P * (i + 1)],
                 rhs=v_codes[a, j].bitcast(FP8X4),
                 rhs_scale=planes[a][:, j * N : (j + 1) * N],
@@ -182,215 +190,281 @@ def tile_list_escapement_wear_match_kernel(
                     first_product(banks[i, j], i, j, a)
         h_tiles = {}
 
-        def make_h(i):
-            h_tiles[i] = keep.tile([P, 2 * S], F32, name="h%d" % i, align_bytes=64)
-            for j in range(HALVES):
-                if i >= OPEN_TILES:
-                    banks[i, j] = psum.tile([P, N], F32, name="bank%d" % ((2 * i + j - 2 * OPEN_TILES) % H_BANKS))
-                for a in range(PASSES1 - 1 if i < OPEN_TILES else 0, PASSES1):
+        def make_half(i, j, passes=range(PASSES1)):
+            if (i, j) not in banks:
+                banks[i, j] = psum.tile([P, N], F32, name="bank%d" % H_BANKS.get((i, j), 2 * (i % 2) + j))
+            for a in passes:
+                if i >= OPEN_TILES or a == PASSES1 - 1:
                     first_product(banks[i, j], i, j, a)
+            if PASSES1 - 1 in passes:
+                if j == 0:
+                    h_tiles[i] = room([P, 2 * S], F32, "h%d" % i)
                 nc.scalar.copy(out=h_tiles[i][:, j * N : (j + 1) * N], in_=banks[i, j][:])
-                if (i, j) in COSINE_BEHIND:
-                    cosine(COSINE_BEHIND.index((i, j)))
+
+        def make_h(i):
+            for j in range(HALVES):
+                make_half(i, j)
 
         def spare(i):
             return h_tiles[i][:, S : 2 * S]
 
+        woven = {}
+
         w2_codes = {}
         w2_planes = {}
 
-        early_rooms = [keep.tile([P, 2 * M], F32, name="w2_woven%d" % b, tag="w2_woven%d" % b, align_bytes=64) for b in range(PASSES2)]
+        def weave(b, c, first, last):
+            rows = w2_raw[b, c][:].rearrange("p t (n i) -> p n i t", i=PACK)
+            spot = woven[b, c].bitcast(BF16).rearrange("p (i n t) -> p n i t", i=PACK, t=PACK)
+            nc.gpsimd.tensor_scalar(spot[:, first:last], rows[:, first:last], 1.0, 0.0, ALU.mult, ALU.add)
 
-        def weave_early(piece):
-            b, half = divmod(piece, 2)
-            cols = slice(half * EARLY_PIECE, (half + 1) * EARLY_PIECE)
-            woven = early_rooms[b][:].bitcast(BF16).rearrange("p (n t) -> p n t", t=PACK)
-            rows = w2_raw[b, 0][:].rearrange("p t n -> p n t")
-            nc.gpsimd.tensor_scalar(woven[:, cols], rows[:, cols], 1.0, 0.0, ALU.mult, ALU.add)
-            return w2_raw[b, 0][:, 0:2, cols]
+        def weave_first(half):
+            rows = first_raw[half][:].rearrange("p t (n i) -> p n i t", i=PACK)
+            spot = woven[0, 1].bitcast(BF16).rearrange("p (i n t) -> p n i t", i=PACK, t=PACK)[:, half * P // 2 : (half + 1) * P // 2]
+            nc.gpsimd.tensor_scalar(spot, rows, 1.0, 0.0, ALU.mult, ALU.add)
 
-        def weave_late(b, room):
-            woven = room.bitcast(BF16).rearrange("p (i n t) -> p n t i", i=PACK, t=PACK)
-            for first in range(0, P, LATE_PIECE):
-                cols = slice(first, first + LATE_PIECE)
-                rows = w2_raw[b, 1][:].rearrange("p t (n i) -> p n t i", i=PACK)
-                nc.scalar.copy(out=woven[:, cols], in_=rows[:, cols])
-
-        def quantize_w2(b, c, room, tag):
-            w2_codes[b, c] = keep.tile([P, K_PASS], U32, name="w2_codes%d%d" % (b, c), tag=tag, align_bytes=64)
-            w2_planes[b, c] = keep.tile([P, K_PASS], U8, name="w2_plane%d%d" % (b, c), align_bytes=64)
+        def quantize_w2(b, c, tag):
+            w2_codes[b, c] = room([P, K_PASS], U32, "w2_codes%d%d" % (b, c), tag)
+            w2_planes[b, c] = room([P, K_PASS], U8, "w2_plane%d%d" % (b, c))
             nc.vector.quantize_mx(
-                out=w2_codes[b, c][:].bitcast(FP8X4),
-                scales=w2_planes[b, c][:],
-                in_=room.bitcast(BF16),
+                out=w2_codes[b, c][:].bitcast(FP8X4), scales=w2_planes[b, c][:], in_=woven[b, c].bitcast(BF16)
             )
 
         turns = {}
-        less = {}
-        first_whole = keep.tile([P, 2, EARLY_PIECE], F32, name="first_whole", align_bytes=64)
-        whole = {0: first_whole[:]}
-        cosines = keep.tile([P, CHUNKS, PACK, P], F32, name="cosines", tag="cosines", align_bytes=64)
+        whole = {}
 
         def pick_healthy(i, spot):
+            turns[i] = spot
             nc.vector.tensor_scalar(spot, h_tiles[i][:].indirect(pos1_sb[:]), 1.0 / TWO_PI, 0.25, ALU.mult, ALU.add)
-
-        def pick_early(i):
-            turns[i] = keep.tile([P, M], F32, name="turns%d" % i, tag="turns%d" % i, align_bytes=64)
-            pick_healthy(i, turns[i][:])
-            halved = turns[i][:].rearrange("p (e m) -> p e m", e=2)
-            nc.gpsimd.tensor_scalar(whole[i].bitcast(I32), halved, -TURN_STEP, TURN_BITS, ALU.mult, ALU.add)
-            if i >= THREE_TERM_TILES:
-                less[i] = keep.tile([P, 2, EARLY_PIECE], F32, name="less%d" % i, tag="less", align_bytes=64)
-                nc.gpsimd.tensor_scalar(less[i][:], whole[i], 1.0, -TURN_OFFSET, ALU.mult, ALU.add)
-            whole[i + 1] = weave_early(i)
-
-        def pick_late(i):
-            turns[i] = keep.tile([P, M], F32, name="turns%d" % i, tag="turns%d" % i, align_bytes=64)
-            pick_healthy(i, turns[i][:])
-
-        late_phases = {}
-
-        def late_phase(i, phases, tag):
-            late_phases[i] = phases
-            late_whole = keep.tile([P, M], I32, name="late_whole%d" % i, tag=tag, align_bytes=64)
-            nc.gpsimd.tensor_scalar(late_whole[:], turns[i][:], 1.0, 0.0, ALU.mult, ALU.add)
-            nc.vector.tensor_tensor(phases, late_whole[:], turns[i][:], ALU.subtract)
-
-        def late_cosine(i):
-            nc.scalar.activation(late_cosines[:, i - PACK, :], late_phases[i], ACT.Sin, scale=-TWO_PI)
-
-        def cosine(i):
-            phases = psum.tile([P, CHUNKS, P], F32, name="bank%d" % PHASE_BANKS[i % 2])
-            for q in range(CHUNKS):
-                cols = slice(P * q, P * (q + 1))
-                part = slice(P * (q % 2), P * (q % 2 + 1))
-                if i < THREE_TERM_TILES:
-                    terms = (whole[i][:, q // 2, part], less_offset[:], turns[i][:, cols])
-                else:
-                    terms = (less[i][:, q // 2, part], turns[i][:, cols])
-                for n, term in enumerate(terms):
-                    nc.tensor.matmul(
-                        out=phases[:, q, :], lhsT=term, rhs=identity[:], is_transpose=True,
-                        start=(n == 0), stop=(n == len(terms) - 1),
-                    )
-            nc.scalar.activation(
-                cosines[:, :, :, QUAD * i : QUAD * (i + 1)].rearrange("p q t s -> p q s t"),
-                phases[:].rearrange("p q (s t) -> p q s t", t=PACK),
-                ACT.Sin,
-                scale=TWO_PI,
-            )
-
-        x_codes = [keep.tile([P, M], U32, name="x_codes%d" % b, align_bytes=64) for b in range(PASSES2)]
-        x_planes = [keep.tile([P, M], U8, name="x_plane%d" % b, align_bytes=64) for b in range(PASSES2)]
-        halves = [slice(X_COLS * half, X_COLS * (half + 1)) for half in range(X_PARTS)]
-
-        early_pairs = keep.tile([P, 2, M, 2], BF16, name="early_pairs", tag="early_pairs", align_bytes=64)
-
-        def weigh_early(t):
-            back = psum.tile([P, M], F32, name="bank%d" % BACK_BANKS[t])
-            for q in range(CHUNKS):
-                nc.tensor.transpose(back[:, P * q : P * (q + 1)], cosines[:, q, t, :], identity[:])
-            nc.scalar.activation(early_pairs[:, t // 2, :, t % 2], back[:], ACT.Copy, scale=gain_sb[:, 0, t : t + 1])
-
-        def weave_pairs(pairs, cols, woven):
-            words = pairs[:].rearrange("p h m e -> p (h m e)").bitcast(U32).rearrange("p (h m) -> p m h", h=2)
-            nc.vector.tensor_copy(out=woven[:].rearrange("p (m h) -> p m h", h=2)[:, cols], in_=words[:, cols])
-
-        def quantize_x(b, cols, woven):
-            nc.vector.quantize_mx(out=x_codes[b][:, cols].bitcast(FP8X4), scales=x_planes[b][:, cols], in_=woven)
 
         suspects = {}
 
-        def pick_suspects(i, spot, columns):
+        def pick_suspects(i, tag):
+            pick_suspects_onto(i, room([P, M], F32, "suspects%d" % i, tag)[:])
+
+        def count_bits(i, spot):
+            whole[i] = spot
+            nc.gpsimd.tensor_scalar(spot.bitcast(I32), turns[i].rearrange("p (i n) -> p i n", i=PACK), -TURN_STEP, TURN_BITS, ALU.mult, ALU.add)
+
+        def count_turns(i, spot):
+            whole[i] = spot
+            nc.gpsimd.tensor_scalar(spot, turns[i].rearrange("p (i n) -> p i n", i=PACK), 1.0, 0.0, ALU.mult, ALU.add)
+
+        cosines = {}
+        turned = {}
+
+        def cosine_turned(i, spot):
+            phases = psum.tile([P, CHUNKS, P], F32, name="bank%d" % PHASE_BANKS[i])
+            for q in range(CHUNKS):
+                cols = slice(P * q, P * (q + 1))
+                terms = (whole[i][:, q, :], less_offset[:], turns[i][:, cols])
+                for m, term in enumerate(terms):
+                    nc.tensor.matmul(
+                        out=phases[:, q, :], lhsT=term, rhs=identity[:], is_transpose=True,
+                        start=(m == 0), stop=(m == len(terms) - 1),
+                    )
+            turned[i] = quarters(spot)
+            nc.scalar.activation(turned[i], phases[:], ACT.Sin, scale=TWO_PI)
+
+        def turn_back(i):
+            back = psum.tile([P, M], F32, name="bank%d" % BACK_BANKS[i])
+            for q in range(CHUNKS):
+                nc.tensor.transpose(back[:, P * q : P * (q + 1)], turned[i][:, q, :], identity[:])
+            cosines[i] = back[:]
+
+        pairs = [room([P, 2, M, 2], BF16, "pairs%d" % b) for b in range(PASSES2)]
+
+        def weigh(i):
+            b, t = divmod(i, PACK)
+            nc.scalar.activation(pairs[b][:, t // 2, :, t % 2], cosines[i], ACT.Copy, scale=gain_sb[:, b, t : t + 1])
+
+        def quarters(values):
+            return values.rearrange("p (i n) -> p i n", i=PACK)
+
+        def subtract(i, spot):
+            nc.vector.tensor_tensor(quarters(spot), whole[i], quarters(turns[i]), ALU.subtract)
+
+        def sine_plain(i, phases, tag):
+            result = room(list(phases.shape), F32, "cosines%d" % i, tag)
+            nc.scalar.activation(result[:], phases, ACT.Sin, scale=-TWO_PI)
+            return result
+
+        def own(name):
+            return room([P, M], F32, name)[:]
+
+        def pick_suspects_onto(i, spot):
             suspects[i] = spot
-            nc.vector.tensor_copy(out=spot, in_=h_tiles[i][:, 0:columns].indirect(pos2_sb[:]))
+            nc.vector.tensor_copy(out=spot, in_=h_tiles[i][:, 0:S].indirect(pos2_sb[:]))
+
+        woven[0, 1] = room([P, 2 * M], F32, "woven01")[:]
+        woven[1, 1] = room([P, 2 * M], F32, "woven11")[:]
+        woven[0, 0] = room([P, 2 * M], F32, "woven00")[:]
+        split_raw = {}
+
+        def load_split(half, tag):
+            split_raw[half] = room([P, PACK, K_PASS // 2], F32, "split_raw%d" % half, tag)
+            rows = w2[0:K_PASS, half * K_PASS // 2 : (half + 1) * K_PASS // 2]
+            nc.sync.dma_start(out=split_raw[half][:], in_=rows.rearrange("(p t) n -> p t n", t=PACK))
+
+        counted = woven[1, 1].bitcast(I32).rearrange("p (i e n) -> p e i n", e=2, i=PACK)
+        pair_turns = room([P, 2 * M], F32, "pair_turns")
+        weave_first(0)
+        load_split(0, "slot_b")
+        nc.sync.dma_start(out=gain_sb[:], in_=gain.rearrange("(b p t) -> p b t", p=P, t=PACK))
+        make_h(0)
+        make_h(1)
+        weave_first(1)
+        load_w2(1, 0, "slot_w")
+        pick_healthy(0, pair_turns[:, 0:M])
+        count_turns(0, counted[:, 0])
+        pick_healthy(1, pair_turns[:, M:])
+        pick_suspects_onto(1, spare(0)[:, 0:M])
+        count_turns(1, counted[:, 1])
+        nc.vector.tensor_tensor(
+            spare(1).rearrange("p (e i n) -> p e i n", e=2, i=PACK),
+            counted,
+            pair_turns[:].rearrange("p (e i n) -> p e i n", e=2, i=PACK),
+            ALU.subtract,
+        )
+        for i in range(2, 6):
+            make_h(i)
+            if i == PACK - 1:
+                nc.sync.dma_start(out=nw_sb[:], in_=nw.rearrange("(b p t) -> p b t", p=P, t=PACK))
+        make_half(6, 0)
+        pick_healthy(2, pair_turns[:, 0:M])
+        pick_healthy(3, pair_turns[:, M:])
+        pick_healthy(4, own("turns4"))
+        pick_suspects_onto(4, spare(0)[:, M:])
+        cos01 = sine_plain(0, spare(1), "w1_dealt20")
+        for first in range(0, P // 2, P // 4):
+            nc.scalar.copy(
+                out=woven[0, 0].bitcast(BF16).rearrange("p (i n t) -> p n t i", i=PACK, t=PACK)[:, first : first + P // 4],
+                in_=split_raw[0][:].rearrange("p t (n i) -> p n t i", i=PACK)[:, first : first + P // 4],
+            )
+        cosines[0], cosines[1] = cos01[:, 0:M], cos01[:, M:]
+        weave(1, 1, 0, P // 2)
+        count_bits(2, quarters(own("whole2")))
+        count_bits(3, quarters(own("whole3")))
+        count_turns(4, counted[:, 1])
+        phases4 = room([P, M], F32, "phases4")
+        subtract(4, phases4[:])
+        load_split(1, "turns4")
+        weave(1, 1, P // 2, P)
+        cosine_turned(2, own("turned2"))
+        make_half(6, 1)
+        cosine_turned(3, own("turned3"))
+        make_half(7, 0)
+        turn_back(2)
+        make_half(7, 1)
+        pick_healthy(5, h_tiles[4][:, 0:M])
+        pick_healthy(6, h_tiles[4][:, M : 2 * M])
+        pick_suspects_onto(6, spare(2)[:, 0:M])
+        pick_healthy(7, own("turns7"))
+        pick_suspects_onto(7, spare(2)[:, M:])
+        count_bits(5, quarters(own("whole5")))
+        nc.gpsimd.tensor_scalar(
+            woven[0, 0].bitcast(BF16).rearrange("p (i n t) -> p n i t", i=PACK, t=PACK)[:, P // 2 :],
+            split_raw[1][:].rearrange("p t (n i) -> p n i t", i=PACK),
+            1.0, 0.0, ALU.mult, ALU.add,
+        )
+        count_bits(6, quarters(own("whole6")))
+        count_turns(7, quarters(room([P, M], I32, "whole7", "last_room")[:]))
+        subtract(7, spare(7)[:, 0:M])
+        weigh(0)
+        weigh(1)
+        cosines[4] = sine_plain(4, phases4[:], "whole3")[:]
+        turn_back(3)
+        weigh(2)
+        cosine_turned(5, own("turned5"))
+        weigh(3)
+        weigh(4)
+        cosine_turned(6, own("turned6"))
+        cosines[7] = sine_plain(7, spare(7)[:, 0:M], "whole6")[:]
+        turn_back(5)
+        weigh(5)
+        turn_back(6)
+        weigh(6)
+        weigh(7)
+        nc.scalar.activation(gain_sb[:, 1, :], warm[:, 0:PACK], ACT.Exp)
+
+        x_codes = [room([P, M], U32, "x_codes%d" % b) for b in range(PASSES2)]
+        x_planes = [room([P, M], U8, "x_plane%d" % b) for b in range(PASSES2)]
+        halves = (slice(0, M // 2), slice(M // 2, M))
+
+        def weave_pairs(b, cols, spot):
+            words = pairs[b][:].rearrange("p h m e -> p (h m e)").bitcast(U32).rearrange("p (h m) -> p m h", h=2)
+            nc.vector.tensor_copy(out=spot.rearrange("p (m h) -> p m h", h=2), in_=words[:, cols])
+
+        def quantize_x(b, cols, spot):
+            nc.vector.quantize_mx(out=x_codes[b][:, cols].bitcast(FP8X4), scales=x_planes[b][:, cols], in_=spot.bitcast(BF16))
+
+        quantize_w2(0, 1, "turns7")
+        early_woven = room([P, 2 * M], U32, "early_woven", "last_room")[:]
+        weave_pairs(0, slice(0, M), early_woven)
+        quantize_w2(1, 1, "woven01")
+        quantize_x(0, slice(0, M), early_woven)
+        last_room = room([P, 4 * M - P], F32, "last_room")
+        woven[1, 0] = last_room[:, 0 : 2 * M]
+        weave(1, 0, 0, P // 2)
+        pick_suspects(5, "pairs0")
+        late_woven = last_room[:, 2 * M - P :].bitcast(U32)
+        for cols in halves:
+            weave_pairs(1, cols, late_woven[:, 2 * cols.start : 2 * cols.stop])
+        for cols in halves:
+            quantize_x(1, cols, late_woven[:, 2 * cols.start : 2 * cols.stop])
 
         y_banks = {}
 
-        def second_product(i, cols, bank):
+        def second_product(i):
             c, u = divmod(i, PACK)
-            y_banks[i, cols.start] = psum.tile([P, cols.stop - cols.start], F32, name="bank%d" % bank)
-            for n in range(PASSES2):
-                b = (n + c) % PASSES2
+            y_banks[i] = psum.tile([P, M], F32, name="bank%d" % Y_BANKS[i])
+            for b in range(PASSES2):
                 nc.tensor.matmul_mx(
-                    out=y_banks[i, cols.start][:],
+                    out=y_banks[i][:],
                     lhsT=w2_codes[b, c][:, P * u : P * (u + 1)].bitcast(FP8X4),
                     lhsT_scale=w2_planes[b, c][:, P * u : P * (u + 1)],
-                    rhs=x_codes[b][:, cols].bitcast(FP8X4),
-                    rhs_scale=x_planes[b][:, cols],
-                    start=(n == 0),
-                    stop=(n == PASSES2 - 1),
+                    rhs=x_codes[b][:].bitcast(FP8X4),
+                    rhs_scale=x_planes[b][:],
+                    start=(b == 0),
+                    stop=(b == PASSES2 - 1),
                 )
 
-        picked = keep.tile([P, TILES - 1, M], F32, name="picked", align_bytes=64)
-        for i in range(TILES):
-            make_h(i)
-            if i < PACK:
-                pick_early(i)
-                pick_suspects(i, picked[:, i, :], S)
-            else:
-                pick_late(i)
-            if i > PACK:
-                pick_suspects(i, picked[:, i - 1, :], S)
-        late_cosines = keep.tile([P, PACK, M], F32, name="late_cosines", tag="w1_codes1", align_bytes=64)
-        gain_sb = keep.tile([P, PASSES2, PACK], F32, name="gain_sb", tag="turns0", align_bytes=64)
-        nc.sync.dma_start(out=gain_sb[:], in_=gain.rearrange("(b p t) -> p b t", p=P, t=PACK))
-        for i in range(PACK, TILES - 1):
-            late_phase(i, spare(i + 1)[:, 0:M], "late_whole")
-        late_phase(TILES - 1, spare(TILES - 1)[:, M:], "turns4")
-        for t in range(PACK):
-            weigh_early(t)
-        for i in range(PACK, TILES):
-            late_cosine(i)
-        for b in range(PASSES2):
-            weave_late(b, spare(b))
-        quantize_w2(0, 0, early_rooms[0][:], "cosines")
-        quantize_w2(1, 0, early_rooms[1][:], "turns6")
-        quantize_w2(0, 1, spare(0), "late_whole")
-        early_woven = keep.tile([P, 2 * M], U32, name="early_woven", align_bytes=64)
-        weave_pairs(early_pairs, slice(0, M), early_woven)
-        quantize_x(0, slice(0, M), early_woven[:].bitcast(BF16))
-        pick_suspects(PACK, turns[TILES - 1][:], S)
-        late_planes = keep.tile([P, PACK, M], BF16, name="late_planes", tag="late_planes", align_bytes=64)
-        for t in range(PACK):
-            nc.scalar.activation(late_planes[:, t, :], late_cosines[:, t, :], ACT.Copy, scale=gain_sb[:, 1, t : t + 1])
-        late_woven = keep.tile([P, 2 * M], U32, name="late_woven", align_bytes=64)
-        for cols in halves:
-            woven = late_woven[:, 2 * cols.start : 2 * cols.stop].bitcast(BF16)
-            nc.vector.tensor_copy(
-                out=woven.rearrange("p (c i t) -> p c t i", i=PACK, t=PACK),
-                in_=late_planes[:, :, cols].rearrange("p t (c i) -> p c t i", i=PACK),
-            )
-        for cols in halves:
-            quantize_x(1, cols, late_woven[:, 2 * cols.start : 2 * cols.stop].bitcast(BF16))
-        nc.scalar.activation(warm[:, 1:2], late_cosines[:, PACK - 1, 0:1], ACT.Exp)
-        quantize_w2(1, 1, spare(1), "late_planes")
-        nw_sb = keep.tile([P, PACK], F32, name="nw_sb", tag="slot_w", align_bytes=64)
-        with nc.allow_non_contiguous_dma(reason="one value of nw to a partition and row tile"):
-            nc.sync.dma_start(out=nw_sb[:, 0:PACK], in_=nw[0:K_PASS].rearrange("(i p) -> p i", p=P))
-        late_nw = keep.tile([P, PACK], F32, name="late_nw", tag="turns2", align_bytes=64)
-        nc.sync.dma_start(out=late_nw[:], in_=nw[K_PASS:].rearrange("(p t) -> p t", t=PACK))
-        second_product(0, halves[0], Y_BANKS[0])
-        second_product(0, halves[1], Y_BANKS[-1])
-        for i in range(1, TILES - 1):
-            second_product(i, slice(0, M), Y_BANKS[i])
-        late_rows = out[K_PASS:].rearrange("(p u) m -> u p m", u=PACK)
-        for i in range(TILES):
-            cuts = {0: (0, M // 2, M), TILES - 1: (0, M // 2, 3 * M // 4, M)}.get(i, (0, M))
-            rows = out[P * i : P * (i + 1)] if i < PACK else late_rows[i - PACK]
-            sharpness = nw_sb[:, i : i + 1] if i < PACK else late_nw[:, i - PACK : i - PACK + 1]
+        out_rows = out.rearrange("(c p u) m -> c u p m", p=P, u=PACK)
+
+        def score(i, n):
+            c, u = divmod(i, PACK)
+            cuts = (0, M // 2, 3 * M // 4, M) if i == LAST_TILE else (0, M)
+            diff = spare(5 + n // 2)[:, M * (n % 2) : M * (n % 2 + 1)] if n < 4 else room([P, M], F32, "diff%d" % i)[:]
+            for first, last in zip(cuts, cuts[1:]):
+                cols = slice(first, last)
+                nc.vector.tensor_tensor(diff[:, cols], y_banks[i][:, cols], suspects[i][:, cols], ALU.subtract)
             for first, last in zip(cuts, cuts[1:]):
                 cols = slice(first, last)
                 width = last - first
-                diff = ring.tile([P, width], F32, name="diff", bufs=4)
-                nc.vector.tensor_tensor(diff[:], y_banks[i, first][:] if i == 0 else y_banks[i, 0][:, cols], suspects[i][:, cols], ALU.subtract)
-                square = ring.tile([P, width], F32, name="square", bufs=5)
-                if i in VECTOR_SQUARES:
-                    nc.vector.tensor_tensor(square[:], diff[:], diff[:], ALU.mult)
+                square = ring.tile([P, width], F32, name="square", bufs=4)
+                if i == LAST_TILE:
+                    nc.vector.tensor_tensor(square[:], diff[:, cols], diff[:, cols], ALU.mult)
                 else:
-                    nc.scalar.activation(square[:], diff[:], ACT.Square)
-                score = ring.tile([P, width], F32, name="score", bufs=8)
-                nc.scalar.activation(score[:], square[:], ACT.Exp, scale=sharpness)
-                nc.sync.dma_start(out=rows[:, cols], in_=score[:])
-            if i == 0:
-                second_product(TILES - 1, slice(0, M), Y_BANKS[-1])
+                    nc.scalar.activation(square[:], diff[:, cols], ACT.Square)
+                match = ring.tile([P, width], F32, name="match", bufs=6)
+                nc.scalar.activation(match[:], square[:], ACT.Exp, scale=nw_sb[:, c, u : u + 1])
+                nc.sync.dma_start(out=out_rows[c, u][:, cols], in_=match[:])
+
+        pick_suspects(0, "pairs1")
+        weave(1, 0, P // 2, P)
+        for i in range(PACK, TILES):
+            second_product(i)
+        score(4, 0)
+        score(5, 1)
+        quantize_w2(0, 0, "slot_w")
+        quantize_w2(1, 0, "w2_codes10")
+        score(6, 2)
+        score(7, 3)
+        for i in (1, 0, 2, 3):
+            second_product(i)
+        pick_suspects_onto(2, suspects[6])
+        score(1, 4)
+        score(0, 5)
+        pick_suspects_onto(3, suspects[1])
+        score(2, 6)
+        score(3, 7)

@@ -33,10 +33,10 @@ TWO_PI = 2.0 * math.pi
 TILES = H // P
 CHUNKS = M // P
 OPEN_TILES = 2
-H_BANKS = {(7, 0): 4, (7, 1): 0}
-PHASE_BANKS = {2: 2, 3: 3, 5: 4, 6: 0}
-Y_BANKS = (4, 6, 7, 5, 1, 2, 3, 0)
-BACK_BANKS = {2: 5, 3: 6, 5: 7, 6: 5}
+H_BANKS = {(7, 0): 0, (7, 1): 1}
+PHASE_BANKS = {2: 2, 3: 3, 5: 0, 6: 1}
+Y_BANKS = (2, 0, 3, 4, 1, 7, 1, 7)
+BACK_BANKS = {2: 4, 3: 5, 5: 6, 6: 7}
 LAST_TILE = 3
 TURN_OFFSET = 98304.0
 TURN_BITS = 1203765248.0
@@ -221,7 +221,10 @@ def tile_list_escapement_wear_match_kernel(
         def weave_first(half):
             rows = first_raw[half][:].rearrange("p t (n i) -> p n i t", i=PACK)
             spot = woven[0, 1].bitcast(BF16).rearrange("p (i n t) -> p n i t", i=PACK, t=PACK)[:, half * P // 2 : (half + 1) * P // 2]
-            nc.gpsimd.tensor_scalar(spot, rows, 1.0, 0.0, ALU.mult, ALU.add)
+            if half == 0:
+                nc.vector.tensor_copy(out=spot, in_=rows)
+            else:
+                nc.gpsimd.tensor_scalar(spot, rows, 1.0, 0.0, ALU.mult, ALU.add)
 
         def quantize_w2(b, c, tag):
             w2_codes[b, c] = room([P, K_PASS], U32, "w2_codes%d%d" % (b, c), tag)
@@ -326,11 +329,10 @@ def tile_list_escapement_wear_match_kernel(
             pair_turns[:].rearrange("p (e i n) -> p e i n", e=2, i=PACK),
             ALU.subtract,
         )
-        for i in range(2, 6):
+        for i in range(2, 7):
             make_h(i)
             if i == PACK - 1:
                 nc.sync.dma_start(out=nw_sb[:], in_=nw.rearrange("(b p t) -> p b t", p=P, t=PACK))
-        make_half(6, 0)
         pick_healthy(2, pair_turns[:, 0:M])
         pick_healthy(3, pair_turns[:, M:])
         pick_healthy(4, own("turns4"))
@@ -348,41 +350,40 @@ def tile_list_escapement_wear_match_kernel(
         count_turns(4, counted[:, 1])
         phases4 = room([P, M], F32, "phases4")
         subtract(4, phases4[:])
-        load_split(1, "turns4")
         weave(1, 1, P // 2, P)
         cosine_turned(2, own("turned2"))
-        make_half(6, 1)
-        cosine_turned(3, own("turned3"))
         make_half(7, 0)
-        turn_back(2)
+        cosine_turned(3, own("turned3"))
+        load_split(1, "whole3")
         make_half(7, 1)
+        turn_back(2)
         pick_healthy(5, h_tiles[4][:, 0:M])
         pick_healthy(6, h_tiles[4][:, M : 2 * M])
         pick_suspects_onto(6, spare(2)[:, 0:M])
         pick_healthy(7, own("turns7"))
         pick_suspects_onto(7, spare(2)[:, M:])
         count_bits(5, quarters(own("whole5")))
+        count_bits(6, quarters(own("whole6")))
         nc.gpsimd.tensor_scalar(
             woven[0, 0].bitcast(BF16).rearrange("p (i n t) -> p n i t", i=PACK, t=PACK)[:, P // 2 :],
             split_raw[1][:].rearrange("p t (n i) -> p n i t", i=PACK),
             1.0, 0.0, ALU.mult, ALU.add,
         )
-        count_bits(6, quarters(own("whole6")))
-        count_turns(7, quarters(room([P, M], I32, "whole7", "last_room")[:]))
+        count_turns(7, split_raw[1][:, :, 0:P].bitcast(I32))
         subtract(7, spare(7)[:, 0:M])
         weigh(0)
         weigh(1)
-        cosines[4] = sine_plain(4, phases4[:], "whole3")[:]
+        cosines[4] = sine_plain(4, phases4[:], "v_codes21")[:]
         turn_back(3)
         weigh(2)
         cosine_turned(5, own("turned5"))
         weigh(3)
         weigh(4)
         cosine_turned(6, own("turned6"))
-        cosines[7] = sine_plain(7, spare(7)[:, 0:M], "whole6")[:]
         turn_back(5)
         weigh(5)
         turn_back(6)
+        cosines[7] = sine_plain(7, spare(7)[:, 0:M], "turned6")[:]
         weigh(6)
         weigh(7)
         nc.scalar.activation(gain_sb[:, 1, :], warm[:, 0:PACK], ACT.Exp)
@@ -399,11 +400,11 @@ def tile_list_escapement_wear_match_kernel(
             nc.vector.quantize_mx(out=x_codes[b][:, cols].bitcast(FP8X4), scales=x_planes[b][:, cols], in_=spot.bitcast(BF16))
 
         quantize_w2(0, 1, "turns7")
-        early_woven = room([P, 2 * M], U32, "early_woven", "last_room")[:]
+        early_woven = room([P, 2 * M], U32, "early_woven", "whole3")[:]
         weave_pairs(0, slice(0, M), early_woven)
         quantize_w2(1, 1, "woven01")
         quantize_x(0, slice(0, M), early_woven)
-        last_room = room([P, 4 * M - P], F32, "last_room")
+        last_room = room([P, 4 * M - P], F32, "last_room", "whole3")
         woven[1, 0] = last_room[:, 0 : 2 * M]
         weave(1, 0, 0, P // 2)
         pick_suspects(5, "pairs0")
@@ -452,10 +453,12 @@ def tile_list_escapement_wear_match_kernel(
 
         pick_suspects(0, "pairs1")
         weave(1, 0, P // 2, P)
-        for i in range(PACK, TILES):
-            second_product(i)
+        second_product(4)
+        second_product(5)
         score(4, 0)
+        second_product(6)
         score(5, 1)
+        second_product(7)
         quantize_w2(0, 0, "slot_w")
         quantize_w2(1, 0, "w2_codes10")
         score(6, 2)

@@ -38,6 +38,7 @@ PHASE_BANKS = {2: 2, 3: 3, 5: 0, 6: 1}
 Y_BANKS = (2, 0, 3, 4, 1, 7, 1, 7)
 BACK_BANKS = {2: 4, 3: 5, 5: 6, 6: 7}
 LAST_TILE = 3
+LAST_CUT = 48
 TURN_OFFSET = 98304.0
 TURN_BITS = 1203765248.0
 TURN_STEP = 128.0
@@ -137,21 +138,24 @@ def tile_list_escapement_wear_match_kernel(
             for a in range(PASSES1):
                 deal(w1_early, 0, a, pair, nc.scalar.copy)
         for pair in range(2):
-            for a in range(PASSES1 - 1):
-                deal(w1_late, 1, a, pair, nc.scalar.copy)
+            deal(w1_late, 1, 0, pair, nc.scalar.copy)
 
         v_codes = {}
         for a in range(PASSES1):
             width = N if a == PASSES1 - 1 else S
             for first in range(0, S, width):
                 picked_words = room([P, width], U32, "v_codes%d%d" % (a, first // N))
-                cols = slice(first // LIST_ROWS, (first + width) // LIST_ROWS)
-                nc.vector.tensor_copy(out=picked_words[:], in_=tab_windows[a][:].bitcast(U32).indirect(offs_sb[:, cols]))
+                step = N // 2 if (a, first) == (PASSES1 - 1, N) else width
+                for part in range(0, width, step):
+                    cols = slice((first + part) // LIST_ROWS, (first + part + step) // LIST_ROWS)
+                    window = tab_windows[a][:].bitcast(U32)
+                    nc.vector.tensor_copy(out=picked_words[:, part : part + step], in_=window.indirect(offs_sb[:, cols]))
                 for j in range(width // N):
                     v_codes[a, first // N + j] = picked_words[:, j * N : (j + 1) * N]
 
         for pair in range(2):
-            deal(w1_late, 1, PASSES1 - 1, pair, nc.vector.tensor_copy)
+            for a in range(1, PASSES1):
+                deal(w1_late, 1, a, pair, nc.vector.tensor_copy)
         w2_raw = {}
 
         def load_w2(b, c, tag):
@@ -168,26 +172,33 @@ def tile_list_escapement_wear_match_kernel(
         gain_sb = room([P, PASSES2, PACK], F32, "gain_sb", "slot_a")
         nw_sb = room([P, PASSES2, PACK], F32, "nw_sb", "w1_dealt11")
 
-        def first_product(bank, i, j, a):
+        def first_product(bank, i, j, a, cols=slice(0, N)):
             pair, t = divmod(i, 2)
             nc.tensor.matmul_mx(
                 out=bank[:],
                 lhsT=w1_dealt[pair, a][:, t * P // 2 : (t + 1) * P // 2].bitcast(U8).bitcast(FP4X4),
                 lhsT_scale=planes[a][:, S + P * i : S + P * (i + 1)],
-                rhs=v_codes[a, j].bitcast(FP8X4),
-                rhs_scale=planes[a][:, j * N : (j + 1) * N],
+                rhs=v_codes[a, j][:, cols].bitcast(FP8X4),
+                rhs_scale=planes[a][:, j * N + cols.start : j * N + cols.stop],
                 start=(a == 0),
                 stop=(a == PASSES1 - 1),
             )
 
         banks = {}
+        quarter_cols = (slice(0, N // 2), slice(N // 2, N))
+        quarter_banks = [psum.tile([P, N // 2], F32, name="bank%d" % bank) for bank in (1, 4)]
         for i in range(OPEN_TILES):
             for j in range(HALVES):
-                banks[i, j] = psum.tile([P, N], F32, name="bank%d" % (2 * i + j))
+                if (i, j) != (0, 1):
+                    banks[i, j] = psum.tile([P, N], F32, name="bank%d" % (2 * i + j))
         for a in range(PASSES1 - 1):
             for i in range(OPEN_TILES):
                 for j in range(HALVES):
-                    first_product(banks[i, j], i, j, a)
+                    if (i, j) != (0, 1):
+                        first_product(banks[i, j], i, j, a)
+                    else:
+                        for bank, cols in zip(quarter_banks, quarter_cols):
+                            first_product(bank, i, j, a, cols)
         h_tiles = {}
 
         def make_half(i, j, passes=range(PASSES1)):
@@ -314,7 +325,10 @@ def tile_list_escapement_wear_match_kernel(
         weave_first(0)
         load_split(0, "slot_b")
         nc.sync.dma_start(out=gain_sb[:], in_=gain.rearrange("(b p t) -> p b t", p=P, t=PACK))
-        make_h(0)
+        make_half(0, 0)
+        for bank, cols in zip(quarter_banks, quarter_cols):
+            first_product(bank, 0, 1, PASSES1 - 1, cols)
+            nc.scalar.copy(out=h_tiles[0][:, N + cols.start : N + cols.stop], in_=bank[:])
         make_h(1)
         weave_first(1)
         load_w2(1, 0, "slot_w")
@@ -376,16 +390,16 @@ def tile_list_escapement_wear_match_kernel(
         cosines[4] = sine_plain(4, phases4[:], "v_codes21")[:]
         turn_back(3)
         weigh(2)
-        cosine_turned(5, own("turned5"))
         weigh(3)
+        cosine_turned(5, own("turned5"))
         weigh(4)
         cosine_turned(6, own("turned6"))
+        cosines[7] = sine_plain(7, spare(7)[:, 0:M], "whole6")[:]
         turn_back(5)
         weigh(5)
         turn_back(6)
-        cosines[7] = sine_plain(7, spare(7)[:, 0:M], "turned6")[:]
-        weigh(6)
         weigh(7)
+        weigh(6)
         nc.scalar.activation(gain_sb[:, 1, :], warm[:, 0:PACK], ACT.Exp)
 
         x_codes = [room([P, M], U32, "x_codes%d" % b) for b in range(PASSES2)]
@@ -404,11 +418,11 @@ def tile_list_escapement_wear_match_kernel(
         weave_pairs(0, slice(0, M), early_woven)
         quantize_w2(1, 1, "woven01")
         quantize_x(0, slice(0, M), early_woven)
-        last_room = room([P, 4 * M - P], F32, "last_room", "whole3")
+        last_room = room([P, 4 * M - 2 * (P - LAST_CUT)], F32, "last_room", "whole3")
         woven[1, 0] = last_room[:, 0 : 2 * M]
-        weave(1, 0, 0, P // 2)
+        weave(1, 0, 0, LAST_CUT)
         pick_suspects(5, "pairs0")
-        late_woven = last_room[:, 2 * M - P :].bitcast(U32)
+        late_woven = last_room[:, 2 * M - 2 * (P - LAST_CUT) :].bitcast(U32)
         for cols in halves:
             weave_pairs(1, cols, late_woven[:, 2 * cols.start : 2 * cols.stop])
         for cols in halves:
@@ -452,7 +466,7 @@ def tile_list_escapement_wear_match_kernel(
                 nc.sync.dma_start(out=out_rows[c, u][:, cols], in_=match[:])
 
         pick_suspects(0, "pairs1")
-        weave(1, 0, P // 2, P)
+        weave(1, 0, LAST_CUT, P)
         second_product(4)
         second_product(5)
         score(4, 0)

@@ -34,11 +34,12 @@ TILES = H // P
 CHUNKS = M // P
 OPEN_TILES = 2
 H_BANKS = {(7, 0): 0, (7, 1): 1}
-PHASE_BANKS = {2: 2, 3: 3, 5: 0, 6: 1}
-Y_BANKS = (2, 0, 3, 4, 1, 7, 1, 7)
-BACK_BANKS = {2: 4, 3: 5, 5: 6, 6: 7}
+PHASE_BANKS = {2: 2, 3: 3, 4: 2, 5: 0, 6: 1}
+Y_BANKS = (2, 0, 3, 5, 1, 4, 1, 4)
+BACK_BANKS = {2: 4, 3: 5, 4: 6, 5: 7, 6: 4}
 LAST_TILE = 3
-LAST_CUT = 48
+VECTOR_SQUARES = (2, 3)
+LAST_CUT = 32
 TURN_OFFSET = 98304.0
 TURN_BITS = 1203765248.0
 TURN_STEP = 128.0
@@ -313,17 +314,10 @@ def tile_list_escapement_wear_match_kernel(
         woven[0, 1] = room([P, 2 * M], F32, "woven01")[:]
         woven[1, 1] = room([P, 2 * M], F32, "woven11")[:]
         woven[0, 0] = room([P, 2 * M], F32, "woven00")[:]
-        split_raw = {}
-
-        def load_split(half, tag):
-            split_raw[half] = room([P, PACK, K_PASS // 2], F32, "split_raw%d" % half, tag)
-            rows = w2[0:K_PASS, half * K_PASS // 2 : (half + 1) * K_PASS // 2]
-            nc.sync.dma_start(out=split_raw[half][:], in_=rows.rearrange("(p t) n -> p t n", t=PACK))
-
         counted = woven[1, 1].bitcast(I32).rearrange("p (i e n) -> p e i n", e=2, i=PACK)
         pair_turns = room([P, 2 * M], F32, "pair_turns")
         weave_first(0)
-        load_split(0, "slot_b")
+        load_w2(0, 0, "slot_b")
         nc.sync.dma_start(out=gain_sb[:], in_=gain.rearrange("(b p t) -> p b t", p=P, t=PACK))
         make_half(0, 0)
         for bank, cols in zip(quarter_banks, quarter_cols):
@@ -352,46 +346,42 @@ def tile_list_escapement_wear_match_kernel(
         pick_healthy(4, own("turns4"))
         pick_suspects_onto(4, spare(0)[:, M:])
         cos01 = sine_plain(0, spare(1), "w1_dealt20")
-        for first in range(0, P // 2, P // 4):
-            nc.scalar.copy(
-                out=woven[0, 0].bitcast(BF16).rearrange("p (i n t) -> p n t i", i=PACK, t=PACK)[:, first : first + P // 4],
-                in_=split_raw[0][:].rearrange("p t (n i) -> p n t i", i=PACK)[:, first : first + P // 4],
-            )
         cosines[0], cosines[1] = cos01[:, 0:M], cos01[:, M:]
         weave(1, 1, 0, P // 2)
         count_bits(2, quarters(own("whole2")))
         count_bits(3, quarters(own("whole3")))
-        count_turns(4, counted[:, 1])
-        phases4 = room([P, M], F32, "phases4")
-        subtract(4, phases4[:])
         weave(1, 1, P // 2, P)
+        count_bits(4, quarters(own("whole4")))
+        weave(0, 0, 0, P // 2)
         cosine_turned(2, own("turned2"))
-        make_half(7, 0)
+        make_half(7, 0, (0, 1))
         cosine_turned(3, own("turned3"))
-        load_split(1, "whole3")
-        make_half(7, 1)
+        make_half(7, 0, (2,))
+        make_half(7, 1, (0,))
+        cosine_turned(4, own("turned4"))
+        make_half(7, 1, (1, 2))
         turn_back(2)
-        pick_healthy(5, h_tiles[4][:, 0:M])
+        pick_healthy(5, own("turns5"))
+        pick_suspects_onto(5, spare(3)[:, 0:M])
         pick_healthy(6, h_tiles[4][:, M : 2 * M])
         pick_suspects_onto(6, spare(2)[:, 0:M])
         pick_healthy(7, own("turns7"))
         pick_suspects_onto(7, spare(2)[:, M:])
         count_bits(5, quarters(own("whole5")))
+        weave(0, 0, P // 2, P)
         count_bits(6, quarters(own("whole6")))
-        nc.gpsimd.tensor_scalar(
-            woven[0, 0].bitcast(BF16).rearrange("p (i n t) -> p n i t", i=PACK, t=PACK)[:, P // 2 :],
-            split_raw[1][:].rearrange("p t (n i) -> p n i t", i=PACK),
-            1.0, 0.0, ALU.mult, ALU.add,
-        )
-        count_turns(7, split_raw[1][:, :, 0:P].bitcast(I32))
+        last_room = room([P, 4 * M - 2 * (P - LAST_CUT)], F32, "last_room")
+        woven[1, 0] = last_room[:, 0 : 2 * M]
+        weave(1, 0, 0, LAST_CUT)
+        count_turns(7, quarters(room([P, M], I32, "whole7")[:]))
         subtract(7, spare(7)[:, 0:M])
         weigh(0)
         weigh(1)
-        cosines[4] = sine_plain(4, phases4[:], "v_codes21")[:]
-        turn_back(3)
         weigh(2)
+        turn_back(3)
         weigh(3)
         cosine_turned(5, own("turned5"))
+        turn_back(4)
         weigh(4)
         cosine_turned(6, own("turned6"))
         cosines[7] = sine_plain(7, spare(7)[:, 0:M], "whole6")[:]
@@ -414,14 +404,11 @@ def tile_list_escapement_wear_match_kernel(
             nc.vector.quantize_mx(out=x_codes[b][:, cols].bitcast(FP8X4), scales=x_planes[b][:, cols], in_=spot.bitcast(BF16))
 
         quantize_w2(0, 1, "turns7")
-        early_woven = room([P, 2 * M], U32, "early_woven", "whole3")[:]
+        early_woven = room([P, 2 * M], U32, "early_woven", "whole7")[:]
         weave_pairs(0, slice(0, M), early_woven)
         quantize_w2(1, 1, "woven01")
         quantize_x(0, slice(0, M), early_woven)
-        last_room = room([P, 4 * M - 2 * (P - LAST_CUT)], F32, "last_room", "whole3")
-        woven[1, 0] = last_room[:, 0 : 2 * M]
-        weave(1, 0, 0, LAST_CUT)
-        pick_suspects(5, "pairs0")
+        pick_suspects(0, "pairs0")
         late_woven = last_room[:, 2 * M - 2 * (P - LAST_CUT) :].bitcast(U32)
         for cols in halves:
             weave_pairs(1, cols, late_woven[:, 2 * cols.start : 2 * cols.stop])
@@ -457,7 +444,7 @@ def tile_list_escapement_wear_match_kernel(
                 cols = slice(first, last)
                 width = last - first
                 square = ring.tile([P, width], F32, name="square", bufs=4)
-                if i == LAST_TILE:
+                if i in VECTOR_SQUARES:
                     nc.vector.tensor_tensor(square[:], diff[:, cols], diff[:, cols], ALU.mult)
                 else:
                     nc.scalar.activation(square[:], diff[:, cols], ACT.Square)
@@ -465,7 +452,7 @@ def tile_list_escapement_wear_match_kernel(
                 nc.scalar.activation(match[:], square[:], ACT.Exp, scale=nw_sb[:, c, u : u + 1])
                 nc.sync.dma_start(out=out_rows[c, u][:, cols], in_=match[:])
 
-        pick_suspects(0, "pairs1")
+        pick_suspects(2, "pairs1")
         weave(1, 0, LAST_CUT, P)
         second_product(4)
         second_product(5)
@@ -479,9 +466,8 @@ def tile_list_escapement_wear_match_kernel(
         score(7, 3)
         for i in (1, 0, 2, 3):
             second_product(i)
-        pick_suspects_onto(2, suspects[6])
+        pick_suspects_onto(3, suspects[6])
         score(1, 4)
         score(0, 5)
-        pick_suspects_onto(3, suspects[1])
         score(2, 6)
         score(3, 7)

@@ -346,13 +346,17 @@ def tile_list_escapement_wear_match_kernel(
         pick_healthy(4, own("turns4"))
         pick_suspects_onto(4, spare(0)[:, M:])
         cos01 = sine_plain(0, spare(1), "w1_dealt20")
+        for first in range(0, P // 2, P // 4):
+            nc.scalar.copy(
+                out=woven[0, 0].bitcast(BF16).rearrange("p (i n t) -> p n t i", i=PACK, t=PACK)[:, first : first + P // 4],
+                in_=w2_raw[0, 0][:].rearrange("p t (n i) -> p n t i", i=PACK)[:, first : first + P // 4],
+            )
         cosines[0], cosines[1] = cos01[:, 0:M], cos01[:, M:]
         weave(1, 1, 0, P // 2)
         count_bits(2, quarters(own("whole2")))
         count_bits(3, quarters(own("whole3")))
         weave(1, 1, P // 2, P)
         count_bits(4, quarters(own("whole4")))
-        weave(0, 0, 0, P // 2)
         cosine_turned(2, own("turned2"))
         make_half(7, 0, (0, 1))
         cosine_turned(3, own("turned3"))
@@ -460,9 +464,9 @@ def tile_list_escapement_wear_match_kernel(
         second_product(6)
         score(5, 1)
         second_product(7)
+        score(6, 2)
         quantize_w2(0, 0, "slot_w")
         quantize_w2(1, 0, "w2_codes10")
-        score(6, 2)
         score(7, 3)
         for i in (1, 0, 2, 3):
             second_product(i)

@@ -341,7 +341,7 @@ def tile_list_escapement_wear_match_kernel(
             make_h(i)
             if i == PACK - 1:
                 nc.sync.dma_start(out=nw_sb[:], in_=nw.rearrange("(b p t) -> p b t", p=P, t=PACK))
-        pick_healthy(2, pair_turns[:, 0:M])
+        pick_healthy(2, room([P, M], F32, "turns2", "w1_dealt10")[:])
         pick_healthy(3, pair_turns[:, M:])
         pick_healthy(4, own("turns4"))
         pick_suspects_onto(4, spare(0)[:, M:])
@@ -439,7 +439,7 @@ def tile_list_escapement_wear_match_kernel(
 
         def score(i, n):
             c, u = divmod(i, PACK)
-            cuts = (0, M // 2, 3 * M // 4, M) if i == LAST_TILE else (0, M)
+            cuts = {PACK: (0, M // 2, M), LAST_TILE: (0, M // 2, 3 * M // 4, M)}.get(i, (0, M))
             diff = spare(5 + n // 2)[:, M * (n % 2) : M * (n % 2 + 1)] if n < 4 else room([P, M], F32, "diff%d" % i)[:]
             for first, last in zip(cuts, cuts[1:]):
                 cols = slice(first, last)
@@ -447,12 +447,12 @@ def tile_list_escapement_wear_match_kernel(
             for first, last in zip(cuts, cuts[1:]):
                 cols = slice(first, last)
                 width = last - first
-                square = ring.tile([P, width], F32, name="square", bufs=4)
+                square = ring.tile([P, width], F32, name="square", bufs=5)
                 if i in VECTOR_SQUARES:
                     nc.vector.tensor_tensor(square[:], diff[:, cols], diff[:, cols], ALU.mult)
                 else:
                     nc.scalar.activation(square[:], diff[:, cols], ACT.Square)
-                match = ring.tile([P, width], F32, name="match", bufs=6)
+                match = ring.tile([P, width], F32, name="match", bufs=7)
                 nc.scalar.activation(match[:], square[:], ACT.Exp, scale=nw_sb[:, c, u : u + 1])
                 nc.sync.dma_start(out=out_rows[c, u][:, cols], in_=match[:])
 

@@ -40,6 +40,7 @@ BACK_BANKS = {2: 4, 3: 5, 4: 6, 5: 7, 6: 4}
 LAST_TILE = 3
 VECTOR_SQUARES = (2, 3)
 LAST_CUT = 32
+SCALAR_CUT = 40
 TURN_OFFSET = 98304.0
 TURN_BITS = 1203765248.0
 TURN_STEP = 128.0
@@ -121,8 +122,7 @@ def tile_list_escapement_wear_match_kernel(
                 )
                 if (a, q) == (1, 0):
                     load_table(2, "slot_g")
-            if a == 1:
-                w1_late = load_w1(1, "slot_a")
+        w1_late = load_w1(1, "slot_a")
 
         less_offset = room([P, P], F32, "less_offset", "tab_scale_window")
         nc.gpsimd.memset(less_offset[:], -TURN_OFFSET)
@@ -138,8 +138,6 @@ def tile_list_escapement_wear_match_kernel(
         for pair in range(2):
             for a in range(PASSES1):
                 deal(w1_early, 0, a, pair, nc.scalar.copy)
-        for pair in range(2):
-            deal(w1_late, 1, 0, pair, nc.scalar.copy)
 
         v_codes = {}
         for a in range(PASSES1):
@@ -155,7 +153,7 @@ def tile_list_escapement_wear_match_kernel(
                     v_codes[a, first // N + j] = picked_words[:, j * N : (j + 1) * N]
 
         for pair in range(2):
-            for a in range(1, PASSES1):
+            for a in range(PASSES1):
                 deal(w1_late, 1, a, pair, nc.vector.tensor_copy)
         w2_raw = {}
 
@@ -233,10 +231,7 @@ def tile_list_escapement_wear_match_kernel(
         def weave_first(half):
             rows = first_raw[half][:].rearrange("p t (n i) -> p n i t", i=PACK)
             spot = woven[0, 1].bitcast(BF16).rearrange("p (i n t) -> p n i t", i=PACK, t=PACK)[:, half * P // 2 : (half + 1) * P // 2]
-            if half == 0:
-                nc.vector.tensor_copy(out=spot, in_=rows)
-            else:
-                nc.gpsimd.tensor_scalar(spot, rows, 1.0, 0.0, ALU.mult, ALU.add)
+            nc.gpsimd.tensor_scalar(spot, rows, 1.0, 0.0, ALU.mult, ALU.add)
 
         def quantize_w2(b, c, tag):
             w2_codes[b, c] = room([P, K_PASS], U32, "w2_codes%d%d" % (b, c), tag)
@@ -346,10 +341,10 @@ def tile_list_escapement_wear_match_kernel(
         pick_healthy(4, own("turns4"))
         pick_suspects_onto(4, spare(0)[:, M:])
         cos01 = sine_plain(0, spare(1), "w1_dealt20")
-        for first in range(0, P // 2, P // 4):
+        for first in range(0, SCALAR_CUT, SCALAR_CUT // 2):
             nc.scalar.copy(
-                out=woven[0, 0].bitcast(BF16).rearrange("p (i n t) -> p n t i", i=PACK, t=PACK)[:, first : first + P // 4],
-                in_=w2_raw[0, 0][:].rearrange("p t (n i) -> p n t i", i=PACK)[:, first : first + P // 4],
+                out=woven[0, 0].bitcast(BF16).rearrange("p (i n t) -> p n t i", i=PACK, t=PACK)[:, first : first + SCALAR_CUT // 2],
+                in_=w2_raw[0, 0][:].rearrange("p t (n i) -> p n t i", i=PACK)[:, first : first + SCALAR_CUT // 2],
             )
         cosines[0], cosines[1] = cos01[:, 0:M], cos01[:, M:]
         weave(1, 1, 0, P // 2)
@@ -372,7 +367,7 @@ def tile_list_escapement_wear_match_kernel(
         pick_healthy(7, own("turns7"))
         pick_suspects_onto(7, spare(2)[:, M:])
         count_bits(5, quarters(own("whole5")))
-        weave(0, 0, P // 2, P)
+        weave(0, 0, SCALAR_CUT, P)
         count_bits(6, quarters(own("whole6")))
         last_room = room([P, 4 * M - 2 * (P - LAST_CUT)], F32, "last_room")
         woven[1, 0] = last_room[:, 0 : 2 * M]

import math
from contextlib import ExitStack

import concourse.mybir as mybir
from concourse.masks import make_identity

K, H, T, S, M = 1536, 1024, 2048, 1024, 512
FLOPS = 2 * K * H * S + 2 * H * H * M

F32 = mybir.dt.float32
BF16 = mybir.dt.bfloat16
I32 = mybir.dt.int32
U32 = mybir.dt.uint32
U16 = mybir.dt.uint16
U8 = mybir.dt.uint8
FP8X4 = mybir.dt.float8_e4m3fn_x4
FP4X4 = mybir.dt.float4_e2m1fn_x4
ALU = mybir.AluOpType
ACT = mybir.ActivationFunctionType

P = 128
PACK = 4
K_PASS = P * PACK
PASSES1 = K // K_PASS
PASSES2 = H // K_PASS
N = 512
HALVES = S // N
LIST_ROWS = 16
QUAD = 32
SCALE_ROWS = 16
FIRST_ROW = P - PASSES1 * SCALE_ROWS
TWO_PI = 2.0 * math.pi
TILES = H // P
CHUNKS = M // P
OPEN_TILES = 2
H_BANKS = {(7, 0): 0, (7, 1): 1}
PHASE_BANKS = {2: 2, 3: 3, 4: 2, 5: 0, 6: 1}
Y_BANKS = (2, 0, 3, 5, 1, 4, 1, 4)
BACK_BANKS = {2: 4, 3: 5, 4: 6, 5: 7, 6: 4}
LAST_TILE = 3
VECTOR_SQUARES = (2, 3)
LAST_CUT = 32
SCALAR_CUT = 40
TURN_OFFSET = 98304.0
TURN_BITS = 1203765248.0
TURN_STEP = 128.0


def tile_list_escapement_wear_match_kernel(
    tc, tab_words, tab_scales, offs, w1_words, w1_scales, pos1, pos2, gain, w2, nw, out
):
    nc = tc.nc
    with ExitStack() as ctx:
        lists = ctx.enter_context(tc.tile_pool(name="lists", bufs=1))
        keep = ctx.enter_context(tc.tile_pool(name="keep", bufs=1))
        ring = ctx.enter_context(tc.tile_pool(name="ring", bufs=2))
        psum = ctx.enter_context(tc.psum_pool(name="psum", bufs=1))

        def room(shape, dtype, name, tag=None):
            return keep.tile(shape, dtype, name=name, tag=tag or name, align_bytes=64)

        offs_sb = lists.tile([P, S // LIST_ROWS], U16, name="offs_sb")
        pos1_sb = lists.tile([P, M // LIST_ROWS], U16, name="pos1_sb")
        pos2_sb = lists.tile([P, M // LIST_ROWS], U16, name="pos2_sb")

        tab_scale_window = room([P, T], U8, "tab_scale_window")
        scale_rows = room([P, S + H], U8, "scale_rows")
        planes = [room([P, S + H], U8, "planes%d" % a) for a in range(PASSES1)]
        nc.vector.memset(tab_scale_window[0:FIRST_ROW, :].bitcast(I32), 0)
        w1_scale_raw = room([P, H], U8, "w1_scale_raw")
        nc.gpsimd.memset(w1_scale_raw[0:FIRST_ROW, :].bitcast(I32), 0)
        nc.vector.memset(planes[0][:].bitcast(I32), 0)
        for a in range(1, PASSES1):
            nc.gpsimd.memset(planes[a][:].bitcast(I32), 0)

        warm = room([P, PACK + 1], F32, "warm")
        nc.gpsimd.memset(warm[:, 0:PACK], 0.0)
        nc.scalar.activation(warm[:, PACK:], warm[:, 0:1], ACT.Sin)

        nc.sync.dma_start(offs_sb[:], offs)
        for spot, scales in ((tab_scale_window, tab_scales), (w1_scale_raw, w1_scales)):
            rows_in_hbm = scales.rearrange("a q t -> (a q) t").bitcast(I32)
            for rows in (slice(0, 2 * SCALE_ROWS), slice(2 * SCALE_ROWS, 3 * SCALE_ROWS)):
                nc.sync.dma_start(
                    out=spot[FIRST_ROW + rows.start : FIRST_ROW + rows.stop, :].bitcast(I32), in_=rows_in_hbm[rows]
                )
        tab_windows = {}

        def load_table(a, tag):
            tab_windows[a] = room([P, T], I32, "tab_window%d" % a, tag)
            nc.sync.dma_start(out=tab_windows[a][:], in_=tab_words[a].rearrange("p t i -> p (t i)").bitcast(I32))

        def load_w1(b, tag):
            words = room([P, PASSES1, K_PASS // 2], I32, "w1_words%d" % b, tag)
            cols = slice(b * K_PASS // 2, (b + 1) * K_PASS // 2)
            nc.sync.dma_start(out=words[:], in_=w1_words.bitcast(I32).rearrange("a p w -> p a w")[:, :, cols])
            return words

        load_table(0, "slot_a")
        nc.sync.dma_start(pos1_sb[:], pos1)
        nc.sync.dma_start(pos2_sb[:], pos2)
        load_table(1, "slot_b")
        w1_early = load_w1(0, "slot_w")

        v_packed = room([P, S], U8, "v_packed", "slot_g")
        nc.vector.tensor_copy(out=v_packed[:], in_=tab_scale_window[:].indirect(offs_sb[:]))
        nc.gpsimd.tensor_copy(
            out=scale_rows[:, S : S + K_PASS].rearrange("p (t c) -> p t c", t=PACK),
            in_=w1_scale_raw[:, 0:K_PASS].rearrange("p (c t) -> p t c", t=PACK),
        )
        nc.vector.tensor_copy(
            out=scale_rows[:, S + K_PASS :].rearrange("p (t c) -> p t c", t=PACK),
            in_=w1_scale_raw[:, K_PASS:].rearrange("p (c t) -> p t c", t=PACK),
        )
        nc.vector.tensor_copy(out=scale_rows[:, 0:S].bitcast(I32), in_=v_packed[:].bitcast(I32))
        for a in range(PASSES1):
            for q in range(4):
                first = FIRST_ROW + SCALE_ROWS * a + 4 * q
                nc.sync.dma_start(
                    out=planes[a][QUAD * q : QUAD * q + 4, :].bitcast(I32),
                    in_=scale_rows[first : first + 4, :].bitcast(I32),
                )
                if (a, q) == (1, 0):
                    load_table(2, "slot_g")
        w1_late = load_w1(1, "slot_a")

        less_offset = room([P, P], F32, "less_offset", "tab_scale_window")
        nc.gpsimd.memset(less_offset[:], -TURN_OFFSET)
        identity = room([P, P], F32, "identity", "w1_scale_raw")
        make_identity(nc, identity[:])
        w1_dealt = {}

        def deal(words, b, a, pair, engine):
            w1_dealt[2 * b + pair, a] = room([P, P], I32, "w1_dealt%d%d" % (2 * b + pair, a))
            spot = w1_dealt[2 * b + pair, a][:].bitcast(U16).rearrange("p (t c) -> p c t", t=2)
            engine(out=spot, in_=words[:, a, :].bitcast(U16).rearrange("p (c t) -> p c t", t=PACK)[:, :, 2 * pair : 2 * pair + 2])

        for pair in range(2):
            for a in range(PASSES1):
                deal(w1_early, 0, a, pair, nc.scalar.copy)

        v_codes = {}
        for a in range(PASSES1):
            width = N if a == PASSES1 - 1 else S
            for first in range(0, S, width):
                picked_words = room([P, width], U32, "v_codes%d%d" % (a, first // N))
                step = N // 2 if (a, first) == (PASSES1 - 1, N) else width
                for part in range(0, width, step):
                    cols = slice((first + part) // LIST_ROWS, (first + part + step) // LIST_ROWS)
                    window = tab_windows[a][:].bitcast(U32)
                    nc.vector.tensor_copy(out=picked_words[:, part : part + step], in_=window.indirect(offs_sb[:, cols]))
                for j in range(width // N):
                    v_codes[a, first // N + j] = picked_words[:, j * N : (j + 1) * N]

        for pair in range(2):
            for a in range(PASSES1):
                deal(w1_late, 1, a, pair, nc.vector.tensor_copy)
        w2_raw = {}

        def load_w2(b, c, tag):
            w2_raw[b, c] = room([P, PACK, K_PASS], F32, "w2_raw%d%d" % (b, c), tag)
            rows = w2[K_PASS * b : K_PASS * (b + 1), K_PASS * c : K_PASS * (c + 1)]
            nc.sync.dma_start(out=w2_raw[b, c][:], in_=rows.rearrange("(p t) n -> p t n", t=PACK))

        first_raw = []
        for half, tag in enumerate(("slot_b", "slot_w")):
            first_raw.append(room([P, PACK, K_PASS // 2], F32, "first_raw%d" % half, tag))
            rows = w2[0:K_PASS, K_PASS + half * K_PASS // 2 : K_PASS + (half + 1) * K_PASS // 2]
            nc.sync.dma_start(out=first_raw[half][:], in_=rows.rearrange("(p t) n -> p t n", t=PACK))
        load_w2(1, 1, "slot_g")
        gain_sb = room([P, PASSES2, PACK], F32, "gain_sb", "slot_a")
        nw_sb = room([P, PASSES2, PACK], F32, "nw_sb", "w1_dealt11")

        def first_product(bank, i, j, a, cols=slice(0, N)):
            pair, t = divmod(i, 2)
            nc.tensor.matmul_mx(
                out=bank[:],
                lhsT=w1_dealt[pair, a][:, t * P // 2 : (t + 1) * P // 2].bitcast(U8).bitcast(FP4X4),
                lhsT_scale=planes[a][:, S + P * i : S + P * (i + 1)],
                rhs=v_codes[a, j][:, cols].bitcast(FP8X4),
                rhs_scale=planes[a][:, j * N + cols.start : j * N + cols.stop],
                start=(a == 0),
                stop=(a == PASSES1 - 1),
            )

        banks = {}
        quarter_cols = (slice(0, N // 2), slice(N // 2, N))
        quarter_banks = [psum.tile([P, N // 2], F32, name="bank%d" % bank) for bank in (1, 4)]
        for i in range(OPEN_TILES):
            for j in range(HALVES):
                if (i, j) != (0, 1):
                    banks[i, j] = psum.tile([P, N], F32, name="bank%d" % (2 * i + j))
        for a in range(PASSES1 - 1):
            for i in range(OPEN_TILES):
                for j in range(HALVES):
                    if (i, j) != (0, 1):
                        first_product(banks[i, j], i, j, a)
                    else:
                        for bank, cols in zip(quarter_banks, quarter_cols):
                            first_product(bank, i, j, a, cols)
        h_tiles = {}

        def make_half(i, j, passes=range(PASSES1)):
            if (i, j) not in banks:
                banks[i, j] = psum.tile([P, N], F32, name="bank%d" % H_BANKS.get((i, j), 2 * (i % 2) + j))
            for a in passes:
                if i >= OPEN_TILES or a == PASSES1 - 1:
                    first_product(banks[i, j], i, j, a)
            if PASSES1 - 1 in passes:
                if j == 0:
                    h_tiles[i] = room([P, 2 * S], F32, "h%d" % i)
                nc.scalar.copy(out=h_tiles[i][:, j * N : (j + 1) * N], in_=banks[i, j][:])

        def make_h(i):
            for j in range(HALVES):
                make_half(i, j)

        def spare(i):
            return h_tiles[i][:, S : 2 * S]

        woven = {}

        w2_codes = {}
        w2_planes = {}

        def weave(b, c, first, last):
            rows = w2_raw[b, c][:].rearrange("p t (n i) -> p n i t", i=PACK)
            spot = woven[b, c].bitcast(BF16).rearrange("p (i n t) -> p n i t", i=PACK, t=PACK)
            nc.gpsimd.tensor_scalar(spot[:, first:last], rows[:, first:last], 1.0, 0.0, ALU.mult, ALU.add)

        def weave_first(half):
            rows = first_raw[half][:].rearrange("p t (n i) -> p n i t", i=PACK)
            spot = woven[0, 1].bitcast(BF16).rearrange("p (i n t) -> p n i t", i=PACK, t=PACK)[:, half * P // 2 : (half + 1) * P // 2]
            nc.gpsimd.tensor_scalar(spot, rows, 1.0, 0.0, ALU.mult, ALU.add)

        def quantize_w2(b, c, tag):
            w2_codes[b, c] = room([P, K_PASS], U32, "w2_codes%d%d" % (b, c), tag)
            w2_planes[b, c] = room([P, K_PASS], U8, "w2_plane%d%d" % (b, c))
            nc.vector.quantize_mx(
                out=w2_codes[b, c][:].bitcast(FP8X4), scales=w2_planes[b, c][:], in_=woven[b, c].bitcast(BF16)
            )

        turns = {}
        whole = {}

        def pick_healthy(i, spot):
            turns[i] = spot
            nc.vector.tensor_scalar(spot, h_tiles[i][:].indirect(pos1_sb[:]), 1.0 / TWO_PI, 0.25, ALU.mult, ALU.add)

        suspects = {}

        def pick_suspects(i, tag):
            pick_suspects_onto(i, room([P, M], F32, "suspects%d" % i, tag)[:])

        def count_bits(i, spot):
            whole[i] = spot
            nc.gpsimd.tensor_scalar(spot.bitcast(I32), turns[i].rearrange("p (i n) -> p i n", i=PACK), -TURN_STEP, TURN_BITS, ALU.mult, ALU.add)

        def count_turns(i, spot):
            whole[i] = spot
            nc.gpsimd.tensor_scalar(spot, turns[i].rearrange("p (i n) -> p i n", i=PACK), 1.0, 0.0, ALU.mult, ALU.add)

        cosines = {}
        turned = {}

        def cosine_turned(i, spot):
            phases = psum.tile([P, CHUNKS, P], F32, name="bank%d" % PHASE_BANKS[i])
            for q in range(CHUNKS):
                cols = slice(P * q, P * (q + 1))
                terms = (whole[i][:, q, :], less_offset[:], turns[i][:, cols])
                for m, term in enumerate(terms):
                    nc.tensor.matmul(
                        out=phases[:, q, :], lhsT=term, rhs=identity[:], is_transpose=True,
                        start=(m == 0), stop=(m == len(terms) - 1),
                    )
            turned[i] = quarters(spot)
            nc.scalar.activation(turned[i], phases[:], ACT.Sin, scale=TWO_PI)

        def turn_back(i):
            back = psum.tile([P, M], F32, name="bank%d" % BACK_BANKS[i])
            for q in range(CHUNKS):
                nc.tensor.transpose(back[:, P * q : P * (q + 1)], turned[i][:, q, :], identity[:])
            cosines[i] = back[:]

        pairs = [room([P, 2, M, 2], BF16, "pairs%d" % b) for b in range(PASSES2)]

        def weigh(i):
            b, t = divmod(i, PACK)
            nc.scalar.activation(pairs[b][:, t // 2, :, t % 2], cosines[i], ACT.Copy, scale=gain_sb[:, b, t : t + 1])

        def quarters(values):
            return values.rearrange("p (i n) -> p i n", i=PACK)

        def subtract(i, spot):
            nc.vector.tensor_tensor(quarters(spot), whole[i], quarters(turns[i]), ALU.subtract)

        def sine_plain(i, phases, tag):
            result = room(list(phases.shape), F32, "cosines%d" % i, tag)
            nc.scalar.activation(result[:], phases, ACT.Sin, scale=-TWO_PI)
            return result

        def own(name):
            return room([P, M], F32, name)[:]

        def pick_suspects_onto(i, spot):
            suspects[i] = spot
            nc.vector.tensor_copy(out=spot, in_=h_tiles[i][:, 0:S].indirect(pos2_sb[:]))

        woven[0, 1] = room([P, 2 * M], F32, "woven01")[:]
        woven[1, 1] = room([P, 2 * M], F32, "woven11")[:]
        woven[0, 0] = room([P, 2 * M], F32, "woven00")[:]
        counted = woven[1, 1].bitcast(I32).rearrange("p (i e n) -> p e i n", e=2, i=PACK)
        pair_turns = room([P, 2 * M], F32, "pair_turns")
        weave_first(0)
        load_w2(0, 0, "slot_b")
        nc.sync.dma_start(out=gain_sb[:], in_=gain.rearrange("(b p t) -> p b t", p=P, t=PACK))
        make_half(0, 0)
        for bank, cols in zip(quarter_banks, quarter_cols):
            first_product(bank, 0, 1, PASSES1 - 1, cols)
            nc.scalar.copy(out=h_tiles[0][:, N + cols.start : N + cols.stop], in_=bank[:])
        make_h(1)
        weave_first(1)
        load_w2(1, 0, "slot_w")
        pick_healthy(0, pair_turns[:, 0:M])
        count_turns(0, counted[:, 0])
        pick_healthy(1, pair_turns[:, M:])
        pick_suspects_onto(1, spare(0)[:, 0:M])
        count_turns(1, counted[:, 1])
        nc.vector.tensor_tensor(
            spare(1).rearrange("p (e i n) -> p e i n", e=2, i=PACK),
            counted,
            pair_turns[:].rearrange("p (e i n) -> p e i n", e=2, i=PACK),
            ALU.subtract,
        )
        for i in range(2, 7):
            make_h(i)
            if i == PACK - 1:
                nc.sync.dma_start(out=nw_sb[:], in_=nw.rearrange("(b p t) -> p b t", p=P, t=PACK))
        pick_healthy(2, room([P, M], F32, "turns2", "w1_dealt10")[:])
        pick_healthy(3, pair_turns[:, M:])
        pick_healthy(4, own("turns4"))
        pick_suspects_onto(4, spare(0)[:, M:])
        cos01 = sine_plain(0, spare(1), "w1_dealt20")
        for first in range(0, SCALAR_CUT, SCALAR_CUT // 2):
            nc.scalar.copy(
                out=woven[0, 0].bitcast(BF16).rearrange("p (i n t) -> p n t i", i=PACK, t=PACK)[:, first : first + SCALAR_CUT // 2],
                in_=w2_raw[0, 0][:].rearrange("p t (n i) -> p n t i", i=PACK)[:, first : first + SCALAR_CUT // 2],
            )
        cosines[0], cosines[1] = cos01[:, 0:M], cos01[:, M:]
        weave(1, 1, 0, P // 2)
        count_bits(2, quarters(own("whole2")))
        count_bits(3, quarters(own("whole3")))
        weave(1, 1, P // 2, P)
        count_bits(4, quarters(own("whole4")))
        cosine_turned(2, own("turned2"))
        make_half(7, 0, (0, 1))
        cosine_turned(3, own("turned3"))
        make_half(7, 0, (2,))
        make_half(7, 1, (0,))
        cosine_turned(4, own("turned4"))
        make_half(7, 1, (1, 2))
        turn_back(2)
        pick_healthy(5, own("turns5"))
        pick_suspects_onto(5, spare(3)[:, 0:M])
        pick_healthy(6, h_tiles[4][:, M : 2 * M])
        pick_suspects_onto(6, spare(2)[:, 0:M])
        pick_healthy(7, own("turns7"))
        pick_suspects_onto(7, spare(2)[:, M:])
        count_bits(5, quarters(own("whole5")))
        weave(0, 0, SCALAR_CUT, P)
        count_bits(6, quarters(own("whole6")))
        last_room = room([P, 4 * M - 2 * (P - LAST_CUT)], F32, "last_room")
        woven[1, 0] = last_room[:, 0 : 2 * M]
        weave(1, 0, 0, LAST_CUT)
        count_turns(7, quarters(room([P, M], I32, "whole7")[:]))
        subtract(7, spare(7)[:, 0:M])
        weigh(0)
        weigh(1)
        weigh(2)
        turn_back(3)
        weigh(3)
        cosine_turned(5, own("turned5"))
        turn_back(4)
        weigh(4)
        cosine_turned(6, own("turned6"))
        cosines[7] = sine_plain(7, spare(7)[:, 0:M], "whole6")[:]
        turn_back(5)
        weigh(5)
        turn_back(6)
        weigh(7)
        weigh(6)
        nc.scalar.activation(gain_sb[:, 1, :], warm[:, 0:PACK], ACT.Exp)

        x_codes = [room([P, M], U32, "x_codes%d" % b) for b in range(PASSES2)]
        x_planes = [room([P, M], U8, "x_plane%d" % b) for b in range(PASSES2)]
        halves = (slice(0, M // 2), slice(M // 2, M))

        def weave_pairs(b, cols, spot):
            words = pairs[b][:].rearrange("p h m e -> p (h m e)").bitcast(U32).rearrange("p (h m) -> p m h", h=2)
            nc.vector.tensor_copy(out=spot.rearrange("p (m h) -> p m h", h=2), in_=words[:, cols])

        def quantize_x(b, cols, spot):
            nc.vector.quantize_mx(out=x_codes[b][:, cols].bitcast(FP8X4), scales=x_planes[b][:, cols], in_=spot.bitcast(BF16))

        quantize_w2(0, 1, "turns7")
        early_woven = room([P, 2 * M], U32, "early_woven", "whole7")[:]
        weave_pairs(0, slice(0, M), early_woven)
        quantize_w2(1, 1, "woven01")
        quantize_x(0, slice(0, M), early_woven)
        pick_suspects(0, "pairs0")
        late_woven = last_room[:, 2 * M - 2 * (P - LAST_CUT) :].bitcast(U32)
        for cols in halves:
            weave_pairs(1, cols, late_woven[:, 2 * cols.start : 2 * cols.stop])
        for cols in halves:
            quantize_x(1, cols, late_woven[:, 2 * cols.start : 2 * cols.stop])

        y_banks = {}

        def second_product(i):
            c, u = divmod(i, PACK)
            y_banks[i] = psum.tile([P, M], F32, name="bank%d" % Y_BANKS[i])
            for b in range(PASSES2):
                nc.tensor.matmul_mx(
                    out=y_banks[i][:],
                    lhsT=w2_codes[b, c][:, P * u : P * (u + 1)].bitcast(FP8X4),
                    lhsT_scale=w2_planes[b, c][:, P * u : P * (u + 1)],
                    rhs=x_codes[b][:].bitcast(FP8X4),
                    rhs_scale=x_planes[b][:],
                    start=(b == 0),
                    stop=(b == PASSES2 - 1),
                )

        out_rows = out.rearrange("(c p u) m -> c u p m", p=P, u=PACK)

        def score(i, n):
            c, u = divmod(i, PACK)
            cuts = {PACK: (0, M // 2, M), LAST_TILE: (0, M // 2, 3 * M // 4, M)}.get(i, (0, M))
            diff = spare(5 + n // 2)[:, M * (n % 2) : M * (n % 2 + 1)] if n < 4 else room([P, M], F32, "diff%d" % i)[:]
            for first, last in zip(cuts, cuts[1:]):
                cols = slice(first, last)
                nc.vector.tensor_tensor(diff[:, cols], y_banks[i][:, cols], suspects[i][:, cols], ALU.subtract)
            for first, last in zip(cuts, cuts[1:]):
                cols = slice(first, last)
                width = last - first
                square = ring.tile([P, width], F32, name="square", bufs=5)
                if i in VECTOR_SQUARES:
                    nc.vector.tensor_tensor(square[:], diff[:, cols], diff[:, cols], ALU.mult)
                else:
                    nc.scalar.activation(square[:], diff[:, cols], ACT.Square)
                match = ring.tile([P, width], F32, name="match", bufs=7)
                nc.scalar.activation(match[:], square[:], ACT.Exp, scale=nw_sb[:, c, u : u + 1])
                nc.sync.dma_start(out=out_rows[c, u][:, cols], in_=match[:])

        pick_suspects(2, "pairs1")
        weave(1, 0, LAST_CUT, P)
        second_product(4)
        second_product(5)
        score(4, 0)
        second_product(6)
        score(5, 1)
        second_product(7)
        score(6, 2)
        quantize_w2(0, 0, "slot_w")
        quantize_w2(1, 0, "w2_codes10")
        score(7, 3)
        for i in (1, 0, 2, 3):
            second_product(i)
        pick_suspects_onto(3, suspects[6])
        score(1, 4)
        score(0, 5)
        score(2, 6)
        score(3, 7)
